import numpy as np
import ml_dtypes


def mxq(x, axis, fmt="e4m3"):
    dtype, down = {"e4m3": (ml_dtypes.float8_e4m3fn, 7), "e5m2": (ml_dtypes.float8_e5m2, 14)}[fmt]
    v = np.moveaxis(np.asarray(x, np.float32).astype(ml_dtypes.bfloat16).astype(np.float64), axis, -1)
    blocks = v.reshape(v.shape[:-1] + (-1, 32))
    amax = np.abs(blocks).max(-1, keepdims=True)
    byte = np.maximum(np.where(amax > 0, np.frexp(amax)[1] - 1 + 127, 0) - down, 1)
    scale = np.exp2(byte - 127.0)
    codes = (blocks / scale).astype(np.float32).astype(dtype).astype(np.float64)
    return np.moveaxis((codes * scale).reshape(v.shape), -1, axis)


WIDE = False


def mx_kscale(k):
    if not WIDE:
        return np.ones(k)
    levels = np.array([10, -10, 5, -5, 0])
    if k % 512:
        return np.exp2(np.random.permutation(np.resize(levels, k // 32))).repeat(32)
    a = np.empty((k // 512, 16))
    for p in range(k // 512):
        a[p, :8] = np.random.permutation(np.resize(levels, 8))
        for g in range(8):
            far = levels[np.abs(levels - a[p, g]) >= 10]
            a[p, g + 8] = far[np.random.randint(len(far))]
    return np.exp2(a.ravel()).repeat(32)


def f64(x):
    return np.asarray(x).astype(np.float64)


def striped(idx):
    return np.tile(idx.reshape(-1, 16).T, (8, 1)).astype(np.uint16)


def unstriped(offs):
    return offs[:16].T.reshape(-1).astype(np.int64)


E2M1 = np.array([0.0, 0.5, 1.0, 1.5, 2.0, 3.0, 4.0, 6.0, -0.0, -0.5, -1.0, -1.5, -2.0, -3.0, -4.0, -6.0])


def pack_weight(w, fmt):
    k, n = w.shape
    w = f64(np.asarray(w, np.float32).astype(ml_dtypes.bfloat16)).reshape(k // 32, 32, n)
    amax = np.abs(w).max(1)
    if fmt == "e4m3":
        byte = np.frexp(amax)[1] - 1 + 127 - 7
    else:
        mant, ex = np.frexp(amax / 6.0)
        byte = np.where(mant > 0.5, ex, ex - 1) + 127
    byte = np.clip(np.where(amax > 0, byte, 1), 1, 254)
    scaled = (w * np.exp2(127.0 - byte)[:, None, :]).reshape(k, n).astype(np.float32)
    by_word = np.ascontiguousarray(scaled.reshape(k // 512, 128, 4, n).transpose(0, 1, 3, 2))
    if fmt == "e4m3":
        words = by_word.astype(ml_dtypes.float8_e4m3fn).view(np.uint8)
    else:
        c = by_word.astype(ml_dtypes.float4_e2m1fn).view(np.uint8) & 0xF
        words = (c[..., 0::2] | (c[..., 1::2] << 4)).reshape(k // 512, 128, 2 * n)
    return np.ascontiguousarray(words), np.ascontiguousarray(byte.astype(np.uint8).reshape(k // 512, 16, n))


def unpack_weight(words, scales, fmt):
    g, _, n = scales.shape
    words = np.ascontiguousarray(words).reshape(g, 128, n, -1)
    if fmt == "e4m3":
        vals = words.view(ml_dtypes.float8_e4m3fn).astype(np.float64)
    else:
        nib = np.empty((g, 128, n, 4), np.uint8)
        nib[..., 0::2] = words & 0xF
        nib[..., 1::2] = words >> 4
        vals = E2M1[nib]
    vals = vals * np.repeat(np.exp2(scales.astype(np.float64) - 127.0), 8, axis=1)[..., None]
    return vals.transpose(0, 1, 3, 2).reshape(g * 512, n)


def planes(y):
    n, m = y.shape
    v = y.astype(np.float32).astype(ml_dtypes.bfloat16).astype(np.float64).reshape(n // 32, 32, m)
    top = np.abs(v).max(1)
    byte = np.clip(np.where(top > 0, np.frexp(top)[1] - 1 + 127 - 7, 1), 1, 254)
    codes = (v * np.exp2(127.0 - byte)[:, None, :]).reshape(n, m).astype(np.float32).astype(ml_dtypes.float8_e4m3fn).view(np.uint8)
    words = codes.reshape(n // 512, 128, 4, m).transpose(0, 1, 3, 2)
    return np.ascontiguousarray(words), np.ascontiguousarray(byte.astype(np.uint8).reshape(n // 512, 16, m))


def d_silu(v):
    s = 1.0 / (1.0 + np.exp(-np.maximum(v, -700.0)))
    return s * (1.0 + v * (1.0 - s))


K, T, E, C, H, N = 512, 768, 6, 128, 512, 1024


def by_expert(wq, xq):
    return np.concatenate([wq[e].T @ xq[:, e * C:(e + 1) * C] for e in range(E)], axis=1)


def setup_inputs():
    n = np.random.standard_normal
    v = mx_kscale(N)
    u = mx_kscale(H)
    slot_token = np.random.permutation(T)[:E * C]
    dy = pack_weight(n((N, T)) * v[:, None], "e4m3")
    w2t = [pack_weight(m, "e2m1") for m in n((E, N, H)) / np.sqrt(N) / v[None, :, None] * u]
    w1t = pack_weight(n((H, K)) / np.sqrt(H) / u[:, None], "e4m3")
    return {
        "dy_words": dy[0],
        "dy_scales": dy[1],
        "w2t_words": np.stack([m[0] for m in w2t]),
        "w2t_scales": np.stack([m[1] for m in w2t]),
        "w1t_words": w1t[0],
        "w1t_scales": w1t[1],
        "a": (n((H, T))).astype(np.float32),
        "gate": np.tile(np.random.uniform(0.2, 1.0, E * C), (128, 1)).astype(np.float32),
        "offs": striped(slot_token),
    }


def reference(dy_words, dy_scales, w2t_words, w2t_scales, w1t_words, w1t_scales, a, gate, offs):
    w2t = np.stack([unpack_weight(w2t_words[e], w2t_scales[e], "e2m1") for e in range(E)])
    w1t = unpack_weight(w1t_words, w1t_scales, "e4m3")
    idx = unstriped(offs)
    gq = unpack_weight(dy_words, dy_scales, "e4m3")[:, idx]
    y = by_expert(w2t, gq)
    dh = np.zeros((H, T))
    dh[:, idx] = f64(gate[:1]) * y
    out_0 = w1t.T @ mxq(dh * d_silu(f64(a)), 0, "e4m3")
    return (out_0,) + planes(out_0)

@@ -1,0 +1,217 @@
+from contextlib import ExitStack
+
+import concourse.mybir as mybir
+from concourse.masks import make_identity
+
+K, T, E, C, H, N = 512, 768, 6, 128, 512, 1024
+FLOPS = 2 * N * H * E * C + 2 * H * K * T
+
+F32 = mybir.dt.float32
+BF16 = mybir.dt.bfloat16
+I32 = mybir.dt.int32
+U32 = mybir.dt.uint32
+U16 = mybir.dt.uint16
+U8 = mybir.dt.uint8
+FP8X4 = mybir.dt.float8_e4m3fn_x4
+FP4X4 = mybir.dt.float4_e2m1fn_x4
+ACT = mybir.ActivationFunctionType
+ALU = mybir.AluOpType
+
+P = 128
+PACK = 4
+PASSES = N // (P * PACK)
+LIST_ROWS = 16
+GATHER_GROUPS = ((0, 2), (2, 6))
+SCATTER_GROUPS = ((0, 2), (2, 4), (4, 6))
+CHUNKS = ((0, 256, "vector"), (256, 512, "scalar"), (512, 640, "vector"), (640, 768, "vector"))
+
+
+def tile_moe_sub_silu_kernel(
+    tc, dy_words, dy_scales, w2t_words, w2t_scales, w1t_words, w1t_scales, a, gate, offs, out_0, out_1, out_2
+):
+    nc = tc.nc
+    with ExitStack() as ctx:
+        keep = ctx.enter_context(tc.tile_pool(name="keep", bufs=1))
+        ring = ctx.enter_context(tc.tile_pool(name="ring", bufs=2))
+        psum = ctx.enter_context(tc.psum_pool(name="psum", bufs=8))
+
+        def offsets_of(first, last):
+            return offsets[:, first * C // LIST_ROWS : last * C // LIST_ROWS]
+
+        def load_scale_rows(plane, rows):
+            for r in range(4):
+                nc.sync.dma_start(
+                    out=plane[r:P:32, :, :].bitcast(I32),
+                    in_=rows[:, r:16:4, :].rearrange("g q n -> q g n").bitcast(I32),
+                )
+
+        offsets = keep.tile([P, E * C // LIST_ROWS], U16, name="offsets")
+        nc.sync.dma_start(offsets[:], offs)
+
+        dy_plane = keep.tile([P, PASSES, T], U8, name="dy_plane", align_bytes=64)
+        nc.gpsimd.memset(dy_plane[:].rearrange("p s t -> p (s t)").bitcast(I32), 0)
+        dy_w = []
+        for s in range(PASSES):
+            w = keep.tile([P, T], I32, name=f"dy_w{s}", align_bytes=64)
+            nc.sync.dma_start(out=w[:], in_=dy_words[s].rearrange("p t d -> p (t d)").bitcast(I32))
+            dy_w.append(w)
+        load_scale_rows(dy_plane, dy_scales)
+
+        w2_plane = keep.tile([P, E * PASSES, H], U8, name="w2_plane", align_bytes=64)
+        nc.vector.memset(w2_plane[:].rearrange("p g i -> p (g i)").bitcast(I32), 0)
+        gate_rows = keep.tile([P, C], F32, name="gate_rows")
+        w2_w = []
+        for first, last in SCATTER_GROUPS:
+            w = keep.tile([P, (last - first) * PASSES, 2 * H], U8, name=f"w2_w{first}", align_bytes=64)
+            nc.sync.dma_start(
+                out=w[:].bitcast(I32),
+                in_=w2t_words[first:last].rearrange("e s p b -> p (e s) b").bitcast(I32),
+            )
+            for e in range(first, last):
+                w2_w.append([w[:, (e - first) * PASSES + s, :] for s in range(PASSES)])
+            if first == 0:
+                load_scale_rows(w2_plane, w2t_scales.rearrange("e s b i -> (e s) b i"))
+                nc.sync.dma_start(out=gate_rows[:], in_=gate.rearrange("p (e u) -> (p e) u", u=C)[0:P, :])
+        a_rows = []
+        for t in range(PACK):
+            rows = keep.tile([P, T], F32, name=f"a_rows{t}")
+            nc.sync.dma_start(out=rows[:], in_=a[t:H:PACK, :])
+            a_rows.append(rows)
+        w1_raw = keep.tile([P, K], I32, name="w1_raw")
+        nc.sync.dma_start(out=w1_raw[:], in_=w1t_words[0].rearrange("p k d -> p (k d)").bitcast(I32))
+        w1_plane_raw = keep.tile([P, 1, K], U8, name="w1_plane_raw", align_bytes=64)
+        nc.vector.memset(w1_plane_raw[:].rearrange("p g k -> p (g k)").bitcast(I32), 0)
+        load_scale_rows(w1_plane_raw, w1t_scales)
+
+        identity = keep.tile([P, P], F32, name="identity")
+        make_identity(nc, identity[:])
+        gate_ps = psum.tile([P, PACK, C], F32, name="gate_ps", tag="bank")
+        nc.tensor.transpose(gate_ps[:, 0, :], gate_rows[:], identity[:])
+        gate_col = keep.tile([P, E], F32, name="gate_col")
+        nc.scalar.copy(out=gate_col[:], in_=gate_ps[:, 0, 0:E])
+
+        slot_w, slot_plane = {}, {}
+        for first, last in GATHER_GROUPS:
+            width = (last - first) * C
+            for s in range(PASSES):
+                words = keep.tile([P, width], U32, name=f"slot_w{first}_{s}", align_bytes=64)
+                nc.vector.tensor_copy(out=words[:], in_=dy_w[s][:].bitcast(U32).indirect(offsets_of(first, last)))
+                for e in range(first, last):
+                    slot_w[e, s] = words[:, (e - first) * C : (e - first + 1) * C]
+            for s in range(PASSES):
+                plane = keep.tile([P, width], U8, name=f"slot_plane{first}_{s}", align_bytes=64)
+                nc.vector.tensor_copy(out=plane[:], in_=dy_plane[:, s, :].indirect(offsets_of(first, last)))
+                for e in range(first, last):
+                    slot_plane[e, s] = plane[:, (e - first) * C : (e - first + 1) * C]
+
+        dh = [keep.tile([P, T], F32, name=f"dh{t}") for t in range(PACK)]
+        for first, last in SCATTER_GROUPS:
+            y_rows = keep.tile([P, PACK, (last - first) * C], F32, name=f"y_rows{first}")
+            for e in range(first, last):
+                y_ps = psum.tile([P, H], F32, name="y_ps", tag="bank")
+                for s in range(PASSES):
+                    nc.tensor.matmul_mx(
+                        out=y_ps[:],
+                        lhsT=slot_w[e, s].bitcast(FP8X4),
+                        lhsT_scale=slot_plane[e, s],
+                        rhs=w2_w[e][s].bitcast(FP4X4),
+                        rhs_scale=w2_plane[:, e * PASSES + s, :],
+                        start=(s == 0),
+                        stop=(s == PASSES - 1),
+                    )
+                y_gated = ring.tile([P, PACK, P], F32, name="y_gated")
+                nc.scalar.activation(
+                    out=y_gated[:],
+                    in_=y_ps[:].rearrange("u (m t) -> u t m", t=PACK),
+                    func=ACT.Copy,
+                    scale=gate_col[:, e : e + 1],
+                )
+                turned = psum.tile([P, PACK, C], F32, name="turned", tag="bank")
+                for t in range(PACK):
+                    nc.tensor.transpose(turned[:, t, :], y_gated[:, t, :], identity[:])
+                nc.scalar.copy(out=y_rows[:, :, (e - first) * C : (e - first + 1) * C], in_=turned[:])
+            for t in range(PACK):
+                nc.vector.tensor_copy(out=dh[t][:].indirect(offsets_of(first, last)), in_=y_rows[:, t, :])
+
+        sig, neg_silu, neg_d = [], [], []
+        for t in range(PACK):
+            x = keep.tile([P, T], F32, name=f"sig{t}")
+            nc.scalar.activation(out=x[:], in_=a_rows[t][:], func=ACT.Sigmoid)
+            sig.append(x)
+        for t in range(PACK):
+            x = keep.tile([P, T], F32, name=f"neg_silu{t}")
+            nc.scalar.activation(out=x[:], in_=a_rows[t][:], func=ACT.Silu, scale=-1.0)
+            neg_silu.append(x)
+        for t in range(PACK):
+            x = keep.tile([P, T], F32, name=f"neg_d{t}")
+            nc.vector.scalar_tensor_tensor(
+                out=x[:], in0=neg_silu[t][:], scalar=1.0, in1=sig[t][:], op0=ALU.subtract, op1=ALU.mult
+            )
+            neg_d.append(x)
+
+        w1_w = keep.tile([P, PACK, P], I32, name="w1_w", align_bytes=64)
+        nc.vector.tensor_copy(out=w1_w[:], in_=w1_raw[:].rearrange("p (m d) -> p d m", d=PACK))
+        w1_plane = keep.tile([P, PACK, P], U8, name="w1_plane", align_bytes=64)
+        nc.vector.tensor_copy(out=w1_plane[:], in_=w1_plane_raw[:, 0, :].rearrange("p (m d) -> p d m", d=PACK))
+
+        da_rows = keep.tile([P, PACK, T], BF16, name="da_rows")
+
+        def make_da(t, cols):
+            nc.vector.scalar_tensor_tensor(
+                out=da_rows[:, t, cols], in0=dh[t][:, cols], scalar=-1.0, in1=neg_d[t][:, cols], op0=ALU.mult, op1=ALU.mult
+            )
+
+        for t in range(PACK - 1):
+            make_da(t, slice(0, T))
+        out_codes = keep.tile([P, T], U32, name="out_codes", align_bytes=64)
+        out_plane = keep.tile([P, T], U8, name="out_plane", align_bytes=64)
+        out_rows_hbm = out_0.rearrange("(p d) t -> p d t", d=PACK)
+        codes_hbm = out_1[0].rearrange("p t d -> p (t d)").bitcast(I32)
+        for lo, hi, who in CHUNKS:
+            make_da(PACK - 1, slice(lo, hi))
+        da_q = []
+        for lo, hi, who in CHUNKS:
+            width = hi - lo
+            grouped = keep.tile([P, width, PACK], BF16, name=f"da_grouped{lo}", align_bytes=64)
+            weave = nc.vector.tensor_copy if who == "vector" else nc.scalar.copy
+            weave(
+                out=grouped[:].rearrange("p (c i) t -> p c t i", i=4),
+                in_=da_rows[:, :, lo:hi].rearrange("p t (c i) -> p c t i", i=4),
+            )
+            codes = keep.tile([P, width], U32, name=f"da_codes{lo}", align_bytes=64)
+            plane = keep.tile([P, width], U8, name=f"da_plane{lo}", align_bytes=64)
+            nc.vector.quantize_mx(
+                out=codes[:].bitcast(FP8X4), scales=plane[:], in_=grouped[:].rearrange("p c t -> p (c t)")
+            )
+            da_q.append((codes, plane))
+        for (lo, hi, who), (codes, plane) in zip(CHUNKS, da_q):
+            width = hi - lo
+            per_bank = 512 // width
+            out_rows = keep.tile([P, PACK, width], F32, name=f"out_rows{lo}")
+            for d0 in range(0, PACK, per_bank):
+                acc = psum.tile([P, per_bank, width], F32, name="acc", tag="bank")
+                for j in range(per_bank):
+                    nc.tensor.matmul_mx(
+                        out=acc[:, j, :],
+                        lhsT=w1_w[:, d0 + j, :].bitcast(FP8X4),
+                        lhsT_scale=w1_plane[:, d0 + j, :],
+                        rhs=codes[:].bitcast(FP8X4),
+                        rhs_scale=plane[:],
+                        start=True,
+                        stop=True,
+                    )
+                nc.scalar.copy(out=out_rows[:, d0 : d0 + per_bank, :], in_=acc[:])
+            nc.sync.dma_start(out=out_rows_hbm[:, :, lo:hi], in_=out_rows[:])
+            grouped = keep.tile([P, width, PACK], BF16, name=f"out_grouped{lo}", align_bytes=64)
+            nc.vector.tensor_copy(out=grouped[:], in_=out_rows[:].rearrange("p d c -> p c d"))
+            nc.vector.quantize_mx(
+                out=out_codes[:, lo:hi].bitcast(FP8X4),
+                scales=out_plane[:, lo:hi],
+                in_=grouped[:].rearrange("p c d -> p (c d)"),
+            )
+            nc.sync.dma_start(out=codes_hbm[:, lo:hi], in_=out_codes[:, lo:hi].bitcast(I32))
+        for q in range(4):
+            queue = nc.sync if q % 2 == 0 else nc.scalar
+            queue.dma_start(
+                out=out_2[0, 4 * q : 4 * q + 4, :].bitcast(I32), in_=out_plane[32 * q : 32 * q + 4, :].bitcast(I32)
+            )

@@ -22,8 +22,8 @@ PACK = 4
 PASSES = N // (P * PACK)
 LIST_ROWS = 16
 GATHER_GROUPS = ((0, 2), (2, 6))
-SCATTER_GROUPS = ((0, 2), (2, 4), (4, 6))
-CHUNKS = ((0, 256, "vector"), (256, 512, "scalar"), (512, 640, "vector"), (640, 768, "vector"))
+SCATTER_GROUPS = ((0, 1), (1, 2), (2, 4), (4, 6))
+CHUNKS = ((0, 256, "vector"), (256, 512, "scalar"), (512, 768, "vector"))
 
 
 def tile_moe_sub_silu_kernel(
@@ -33,7 +33,8 @@ def tile_moe_sub_silu_kernel(
     with ExitStack() as ctx:
         keep = ctx.enter_context(tc.tile_pool(name="keep", bufs=1))
         ring = ctx.enter_context(tc.tile_pool(name="ring", bufs=2))
-        psum = ctx.enter_context(tc.psum_pool(name="psum", bufs=8))
+        psum = ctx.enter_context(tc.psum_pool(name="psum", bufs=1))
+        psum_out = ctx.enter_context(tc.psum_pool(name="psum_out", bufs=4))
 
         def offsets_of(first, last):
             return offsets[:, first * C // LIST_ROWS : last * C // LIST_ROWS]
@@ -50,18 +51,21 @@ def tile_moe_sub_silu_kernel(
 
         dy_plane = keep.tile([P, PASSES, T], U8, name="dy_plane", align_bytes=64)
         nc.gpsimd.memset(dy_plane[:].rearrange("p s t -> p (s t)").bitcast(I32), 0)
-        dy_w = []
-        for s in range(PASSES):
-            w = keep.tile([P, T], I32, name=f"dy_w{s}", align_bytes=64)
-            nc.sync.dma_start(out=w[:], in_=dy_words[s].rearrange("p t d -> p (t d)").bitcast(I32))
-            dy_w.append(w)
         load_scale_rows(dy_plane, dy_scales)
+        dy_w = keep.tile([P, PASSES, T], I32, name="dy_w", align_bytes=64)
+        nc.sync.dma_start(out=dy_w[:], in_=dy_words.rearrange("s p t d -> p s (t d)").bitcast(I32))
 
         w2_plane = keep.tile([P, E * PASSES, H], U8, name="w2_plane", align_bytes=64)
         nc.vector.memset(w2_plane[:].rearrange("p g i -> p (g i)").bitcast(I32), 0)
+        w1_plane_raw = keep.tile([P, 1, K], U8, name="w1_plane_raw", align_bytes=64)
+        nc.vector.memset(w1_plane_raw[:].rearrange("p g k -> p (g k)").bitcast(I32), 0)
         gate_rows = keep.tile([P, C], F32, name="gate_rows")
+        a_rows = keep.tile([P, PACK, T], F32, name="a_rows")
+        a_hbm = a.rearrange("(p t) c -> p t c", t=PACK)
+        w1_raw = keep.tile([P, K], I32, name="w1_raw")
         w2_w = []
-        for first, last in SCATTER_GROUPS:
+
+        def load_experts(first, last):
             w = keep.tile([P, (last - first) * PASSES, 2 * H], U8, name=f"w2_w{first}", align_bytes=64)
             nc.sync.dma_start(
                 out=w[:].bitcast(I32),
@@ -69,46 +73,63 @@ def tile_moe_sub_silu_kernel(
             )
             for e in range(first, last):
                 w2_w.append([w[:, (e - first) * PASSES + s, :] for s in range(PASSES)])
-            if first == 0:
-                load_scale_rows(w2_plane, w2t_scales.rearrange("e s b i -> (e s) b i"))
-                nc.sync.dma_start(out=gate_rows[:], in_=gate.rearrange("p (e u) -> (p e) u", u=C)[0:P, :])
-        a_rows = []
-        for t in range(PACK):
-            rows = keep.tile([P, T], F32, name=f"a_rows{t}")
-            nc.sync.dma_start(out=rows[:], in_=a[t:H:PACK, :])
-            a_rows.append(rows)
-        w1_raw = keep.tile([P, K], I32, name="w1_raw")
-        nc.sync.dma_start(out=w1_raw[:], in_=w1t_words[0].rearrange("p k d -> p (k d)").bitcast(I32))
-        w1_plane_raw = keep.tile([P, 1, K], U8, name="w1_plane_raw", align_bytes=64)
-        nc.vector.memset(w1_plane_raw[:].rearrange("p g k -> p (g k)").bitcast(I32), 0)
-        load_scale_rows(w1_plane_raw, w1t_scales)
 
+        load_experts(0, 2)
+        nc.sync.dma_start(out=gate_rows[:], in_=gate.rearrange("p (e u) -> (p e) u", u=C)[0:P, :])
+        load_scale_rows(w2_plane, w2t_scales.rearrange("e s b i -> (e s) b i"))
+        nc.sync.dma_start(out=a_rows[:, :, 0 : T // 2], in_=a_hbm[:, :, 0 : T // 2])
+        nc.sync.dma_start(out=w1_raw[:], in_=w1t_words[0].rearrange("p k d -> p (k d)").bitcast(I32))
+        load_scale_rows(w1_plane_raw, w1t_scales)
+        load_experts(2, 4)
+        nc.sync.dma_start(out=a_rows[:, :, T // 2 : T], in_=a_hbm[:, :, T // 2 : T])
+        load_experts(4, 6)
+
+        warm = keep.tile([P, 8], F32, name="warm")
+        nc.gpsimd.memset(warm[:], 0.0)
+        nc.scalar.activation(out=warm[:, 0:1], in_=warm[:, 1:2], func=ACT.Sigmoid)
         identity = keep.tile([P, P], F32, name="identity")
         make_identity(nc, identity[:])
-        gate_ps = psum.tile([P, PACK, C], F32, name="gate_ps", tag="bank")
+        gate_ps = psum_out.tile([P, PACK, C], F32, name="gate_ps", tag="acc")
         nc.tensor.transpose(gate_ps[:, 0, :], gate_rows[:], identity[:])
         gate_col = keep.tile([P, E], F32, name="gate_col")
         nc.scalar.copy(out=gate_col[:], in_=gate_ps[:, 0, 0:E])
 
         slot_w, slot_plane = {}, {}
-        for first, last in GATHER_GROUPS:
-            width = (last - first) * C
-            for s in range(PASSES):
-                words = keep.tile([P, width], U32, name=f"slot_w{first}_{s}", align_bytes=64)
-                nc.vector.tensor_copy(out=words[:], in_=dy_w[s][:].bitcast(U32).indirect(offsets_of(first, last)))
-                for e in range(first, last):
-                    slot_w[e, s] = words[:, (e - first) * C : (e - first + 1) * C]
-            for s in range(PASSES):
-                plane = keep.tile([P, width], U8, name=f"slot_plane{first}_{s}", align_bytes=64)
-                nc.vector.tensor_copy(out=plane[:], in_=dy_plane[:, s, :].indirect(offsets_of(first, last)))
-                for e in range(first, last):
-                    slot_plane[e, s] = plane[:, (e - first) * C : (e - first + 1) * C]
 
+        def gather(window_of_pass, first, last, dtype, name, tag, into):
+            width = (last - first) * C
+            gathered = keep.tile([P, PASSES, width], dtype, name=name, tag=tag, align_bytes=64)
+            for s in range(PASSES):
+                nc.vector.tensor_copy(out=gathered[:, s, :], in_=window_of_pass(s).indirect(offsets_of(first, last)))
+                for e in range(first, last):
+                    into[e, s] = gathered[:, s, (e - first) * C : (e - first + 1) * C]
+
+        def words_of_pass(s):
+            return dy_w[:, s, :].bitcast(U32)
+
+        def scales_of_pass(s):
+            return dy_plane[:, s, :]
+
+        gather(scales_of_pass, 0, 2, U8, "early_plane", "early_plane", slot_plane)
+        gather(words_of_pass, 0, 2, U32, "early_words", "early_words", slot_w)
+        gather(words_of_pass, 2, E, U32, "late_words", "late_words", slot_w)
+
+        w1_w = keep.tile([P, PACK, P], I32, name="w1_w", align_bytes=64)
+        nc.vector.tensor_copy(out=w1_w[:], in_=w1_raw[:].rearrange("p (m d) -> p d m", d=PACK))
+        w1_plane = keep.tile([P, PACK, P], U8, name="w1_plane", align_bytes=64)
+        nc.vector.tensor_copy(out=w1_plane[:], in_=w1_plane_raw[:, 0, :].rearrange("p (m d) -> p d m", d=PACK))
+
+        sig = keep.tile([P, PACK, T], F32, name="sig")
+        for q in range(PACK):
+            cols = slice(q * T // PACK, (q + 1) * T // PACK)
+            nc.scalar.activation(out=sig[:, :, cols], in_=a_rows[:, :, cols], func=ACT.Sigmoid)
         dh = [keep.tile([P, T], F32, name=f"dh{t}") for t in range(PACK)]
         for first, last in SCATTER_GROUPS:
             y_rows = keep.tile([P, PACK, (last - first) * C], F32, name=f"y_rows{first}")
             for e in range(first, last):
-                y_ps = psum.tile([P, H], F32, name="y_ps", tag="bank")
+                if e == 2:
+                    gather(scales_of_pass, 2, E, U8, "late_plane", "early_words", slot_plane)
+                y_ps = psum.tile([P, H], F32, name="y_ps", tag=f"bank{e % 4}")
                 for s in range(PASSES):
                     nc.tensor.matmul_mx(
                         out=y_ps[:],
@@ -126,40 +147,26 @@ def tile_moe_sub_silu_kernel(
                     func=ACT.Copy,
                     scale=gate_col[:, e : e + 1],
                 )
-                turned = psum.tile([P, PACK, C], F32, name="turned", tag="bank")
+                turned = psum.tile([P, PACK, C], F32, name="turned", tag=f"bank{(e + 2) % 4}")
                 for t in range(PACK):
                     nc.tensor.transpose(turned[:, t, :], y_gated[:, t, :], identity[:])
                 nc.scalar.copy(out=y_rows[:, :, (e - first) * C : (e - first + 1) * C], in_=turned[:])
             for t in range(PACK):
                 nc.vector.tensor_copy(out=dh[t][:].indirect(offsets_of(first, last)), in_=y_rows[:, t, :])
 
-        sig, neg_silu, neg_d = [], [], []
+        d_silu = []
         for t in range(PACK):
-            x = keep.tile([P, T], F32, name=f"sig{t}")
-            nc.scalar.activation(out=x[:], in_=a_rows[t][:], func=ACT.Sigmoid)
-            sig.append(x)
-        for t in range(PACK):
-            x = keep.tile([P, T], F32, name=f"neg_silu{t}")
-            nc.scalar.activation(out=x[:], in_=a_rows[t][:], func=ACT.Silu, scale=-1.0)
-            neg_silu.append(x)
-        for t in range(PACK):
-            x = keep.tile([P, T], F32, name=f"neg_d{t}")
-            nc.vector.scalar_tensor_tensor(
-                out=x[:], in0=neg_silu[t][:], scalar=1.0, in1=sig[t][:], op0=ALU.subtract, op1=ALU.mult
-            )
-            neg_d.append(x)
-
-        w1_w = keep.tile([P, PACK, P], I32, name="w1_w", align_bytes=64)
-        nc.vector.tensor_copy(out=w1_w[:], in_=w1_raw[:].rearrange("p (m d) -> p d m", d=PACK))
-        w1_plane = keep.tile([P, PACK, P], U8, name="w1_plane", align_bytes=64)
-        nc.vector.tensor_copy(out=w1_plane[:], in_=w1_plane_raw[:, 0, :].rearrange("p (m d) -> p d m", d=PACK))
+            nc.scalar.activation(out=a_rows[:, t, :], in_=a_rows[:, t, :], func=ACT.Silu, scale=-1.0)
+            rest = ring.tile([P, T], F32, name="rest")
+            nc.scalar.activation(out=rest[:], in_=a_rows[:, t, :], func=ACT.Copy, scale=-1.0, bias=1.0)
+            x = keep.tile([P, T], F32, name=f"d_silu{t}")
+            nc.gpsimd.tensor_tensor(out=x[:], in0=sig[:, t, :], in1=rest[:], op=ALU.mult)
+            d_silu.append(x)
 
         da_rows = keep.tile([P, PACK, T], BF16, name="da_rows")
 
         def make_da(t, cols):
-            nc.vector.scalar_tensor_tensor(
-                out=da_rows[:, t, cols], in0=dh[t][:, cols], scalar=-1.0, in1=neg_d[t][:, cols], op0=ALU.mult, op1=ALU.mult
-            )
+            nc.vector.tensor_tensor(out=da_rows[:, t, cols], in0=dh[t][:, cols], in1=d_silu[t][:, cols], op=ALU.mult)
 
         for t in range(PACK - 1):
             make_da(t, slice(0, T))
@@ -189,7 +196,7 @@ def tile_moe_sub_silu_kernel(
             per_bank = 512 // width
             out_rows = keep.tile([P, PACK, width], F32, name=f"out_rows{lo}")
             for d0 in range(0, PACK, per_bank):
-                acc = psum.tile([P, per_bank, width], F32, name="acc", tag="bank")
+                acc = psum_out.tile([P, per_bank, width], F32, name="acc", tag="acc")
                 for j in range(per_bank):
                     nc.tensor.matmul_mx(
                         out=acc[:, j, :],
@@ -211,7 +218,6 @@ def tile_moe_sub_silu_kernel(
             )
             nc.sync.dma_start(out=codes_hbm[:, lo:hi], in_=out_codes[:, lo:hi].bitcast(I32))
         for q in range(4):
-            queue = nc.sync if q % 2 == 0 else nc.scalar
-            queue.dma_start(
+            nc.sync.dma_start(
                 out=out_2[0, 4 * q : 4 * q + 4, :].bitcast(I32), in_=out_plane[32 * q : 32 * q + 4, :].bitcast(I32)
             )

@@ -21,9 +21,10 @@ P = 128
 PACK = 4
 PASSES = N // (P * PACK)
 LIST_ROWS = 16
-GATHER_GROUPS = ((0, 2), (2, 6))
+EARLY = 2
 SCATTER_GROUPS = ((0, 1), (1, 2), (2, 4), (4, 6))
-CHUNKS = ((0, 256, "vector"), (256, 512, "scalar"), (512, 768, "vector"))
+IN_CHUNKS = ((0, 128, "vector"), (128, 384, "scalar"), (384, 640, "vector"), (640, 768, "vector"))
+OUT_CHUNKS = ((0, 256, "vector"), (256, 512, "vector"), (512, 640, "vector"), (640, 768, "vector"))
 
 
 def tile_moe_sub_silu_kernel(
@@ -32,9 +33,8 @@ def tile_moe_sub_silu_kernel(
     nc = tc.nc
     with ExitStack() as ctx:
         keep = ctx.enter_context(tc.tile_pool(name="keep", bufs=1))
-        ring = ctx.enter_context(tc.tile_pool(name="ring", bufs=2))
         psum = ctx.enter_context(tc.psum_pool(name="psum", bufs=1))
-        psum_out = ctx.enter_context(tc.psum_pool(name="psum_out", bufs=4))
+
 
         def offsets_of(first, last):
             return offsets[:, first * C // LIST_ROWS : last * C // LIST_ROWS]
@@ -52,11 +52,19 @@ def tile_moe_sub_silu_kernel(
         dy_plane = keep.tile([P, PASSES, T], U8, name="dy_plane", align_bytes=64)
         nc.gpsimd.memset(dy_plane[:].rearrange("p s t -> p (s t)").bitcast(I32), 0)
         load_scale_rows(dy_plane, dy_scales)
-        dy_w = keep.tile([P, PASSES, T], I32, name="dy_w", align_bytes=64)
-        nc.sync.dma_start(out=dy_w[:], in_=dy_words.rearrange("s p t d -> p s (t d)").bitcast(I32))
+        dy_w = []
+        for s in range(PASSES):
+            w = keep.tile([P, T], I32, name=f"dy_w{s}", align_bytes=64)
+            nc.sync.dma_start(out=w[:], in_=dy_words[s].rearrange("p t d -> p (t d)").bitcast(I32))
+            dy_w.append(w)
 
-        w2_plane = keep.tile([P, E * PASSES, H], U8, name="w2_plane", align_bytes=64)
-        nc.vector.memset(w2_plane[:].rearrange("p g i -> p (g i)").bitcast(I32), 0)
+        w2_scale_rows = w2t_scales.rearrange("e s b i -> (e s) b i")
+        w2_plane_early = keep.tile([P, EARLY * PASSES, H], U8, name="w2_plane_early", align_bytes=64)
+        nc.vector.memset(w2_plane_early[:].rearrange("p g i -> p (g i)").bitcast(I32), 0)
+        w2_plane_late = keep.tile([P, (E - EARLY) * PASSES, H], U8, name="w2_plane_late", align_bytes=64)
+        nc.vector.memset(w2_plane_late[:].rearrange("p g i -> p (g i)").bitcast(I32), 0)
+        w2_plane = [w2_plane_early[:, g, :] for g in range(EARLY * PASSES)]
+        w2_plane.extend(w2_plane_late[:, g, :] for g in range((E - EARLY) * PASSES))
         w1_plane_raw = keep.tile([P, 1, K], U8, name="w1_plane_raw", align_bytes=64)
         nc.vector.memset(w1_plane_raw[:].rearrange("p g k -> p (g k)").bitcast(I32), 0)
         gate_rows = keep.tile([P, C], F32, name="gate_rows")
@@ -76,23 +84,23 @@ def tile_moe_sub_silu_kernel(
 
         load_experts(0, 2)
         nc.sync.dma_start(out=gate_rows[:], in_=gate.rearrange("p (e u) -> (p e) u", u=C)[0:P, :])
-        load_scale_rows(w2_plane, w2t_scales.rearrange("e s b i -> (e s) b i"))
-        nc.sync.dma_start(out=a_rows[:, :, 0 : T // 2], in_=a_hbm[:, :, 0 : T // 2])
+        load_scale_rows(w2_plane_early, w2_scale_rows[0 : EARLY * PASSES])
         nc.sync.dma_start(out=w1_raw[:], in_=w1t_words[0].rearrange("p k d -> p (k d)").bitcast(I32))
         load_scale_rows(w1_plane_raw, w1t_scales)
+        load_scale_rows(w2_plane_late, w2_scale_rows[EARLY * PASSES : E * PASSES])
         load_experts(2, 4)
-        nc.sync.dma_start(out=a_rows[:, :, T // 2 : T], in_=a_hbm[:, :, T // 2 : T])
         load_experts(4, 6)
+        nc.sync.dma_start(out=a_rows[:], in_=a_hbm)
 
         warm = keep.tile([P, 8], F32, name="warm")
         nc.gpsimd.memset(warm[:], 0.0)
         nc.scalar.activation(out=warm[:, 0:1], in_=warm[:, 1:2], func=ACT.Sigmoid)
         identity = keep.tile([P, P], F32, name="identity")
         make_identity(nc, identity[:])
-        gate_ps = psum_out.tile([P, PACK, C], F32, name="gate_ps", tag="acc")
+        gate_ps = psum.tile([P, PACK, C], F32, name="gate_ps", tag="bank7")
         nc.tensor.transpose(gate_ps[:, 0, :], gate_rows[:], identity[:])
         gate_col = keep.tile([P, E], F32, name="gate_col")
-        nc.scalar.copy(out=gate_col[:], in_=gate_ps[:, 0, 0:E])
+        nc.scalar.activation(out=gate_col[:], in_=gate_ps[:, 0, 0:E], func=ACT.Copy, scale=-1.0)
 
         slot_w, slot_plane = {}, {}
 
@@ -105,7 +113,7 @@ def tile_moe_sub_silu_kernel(
                     into[e, s] = gathered[:, s, (e - first) * C : (e - first + 1) * C]
 
         def words_of_pass(s):
-            return dy_w[:, s, :].bitcast(U32)
+            return dy_w[s][:].bitcast(U32)
 
         def scales_of_pass(s):
             return dy_plane[:, s, :]
@@ -119,10 +127,6 @@ def tile_moe_sub_silu_kernel(
         w1_plane = keep.tile([P, PACK, P], U8, name="w1_plane", align_bytes=64)
         nc.vector.tensor_copy(out=w1_plane[:], in_=w1_plane_raw[:, 0, :].rearrange("p (m d) -> p d m", d=PACK))
 
-        sig = keep.tile([P, PACK, T], F32, name="sig")
-        for q in range(PACK):
-            cols = slice(q * T // PACK, (q + 1) * T // PACK)
-            nc.scalar.activation(out=sig[:, :, cols], in_=a_rows[:, :, cols], func=ACT.Sigmoid)
         dh = [keep.tile([P, T], F32, name=f"dh{t}") for t in range(PACK)]
         for first, last in SCATTER_GROUPS:
             y_rows = keep.tile([P, PACK, (last - first) * C], F32, name=f"y_rows{first}")
@@ -136,11 +140,11 @@ def tile_moe_sub_silu_kernel(
                         lhsT=slot_w[e, s].bitcast(FP8X4),
                         lhsT_scale=slot_plane[e, s],
                         rhs=w2_w[e][s].bitcast(FP4X4),
-                        rhs_scale=w2_plane[:, e * PASSES + s, :],
+                        rhs_scale=w2_plane[e * PASSES + s],
                         start=(s == 0),
                         stop=(s == PASSES - 1),
                     )
-                y_gated = ring.tile([P, PACK, P], F32, name="y_gated")
+                y_gated = keep.tile([P, PACK, P], F32, name="y_gated", tag=f"y_gated{e}")
                 nc.scalar.activation(
                     out=y_gated[:],
                     in_=y_ps[:].rearrange("u (m t) -> u t m", t=PACK),
@@ -154,13 +158,17 @@ def tile_moe_sub_silu_kernel(
             for t in range(PACK):
                 nc.vector.tensor_copy(out=dh[t][:].indirect(offsets_of(first, last)), in_=y_rows[:, t, :])
 
+        sig = keep.tile([P, PACK, T], F32, name="sig", tag="y_gated1")
+        for q in range(PACK):
+            cols = slice(q * T // PACK, (q + 1) * T // PACK)
+            nc.scalar.activation(out=sig[:, :, cols], in_=a_rows[:, :, cols], func=ACT.Sigmoid)
         d_silu = []
         for t in range(PACK):
             nc.scalar.activation(out=a_rows[:, t, :], in_=a_rows[:, t, :], func=ACT.Silu, scale=-1.0)
-            rest = ring.tile([P, T], F32, name="rest")
-            nc.scalar.activation(out=rest[:], in_=a_rows[:, t, :], func=ACT.Copy, scale=-1.0, bias=1.0)
             x = keep.tile([P, T], F32, name=f"d_silu{t}")
-            nc.gpsimd.tensor_tensor(out=x[:], in0=sig[:, t, :], in1=rest[:], op=ALU.mult)
+            nc.vector.scalar_tensor_tensor(
+                out=x[:], in0=a_rows[:, t, :], scalar=1.0, in1=sig[:, t, :], op0=ALU.subtract, op1=ALU.mult
+            )
             d_silu.append(x)
 
         da_rows = keep.tile([P, PACK, T], BF16, name="da_rows")
@@ -174,10 +182,10 @@ def tile_moe_sub_silu_kernel(
         out_plane = keep.tile([P, T], U8, name="out_plane", align_bytes=64)
         out_rows_hbm = out_0.rearrange("(p d) t -> p d t", d=PACK)
         codes_hbm = out_1[0].rearrange("p t d -> p (t d)").bitcast(I32)
-        for lo, hi, who in CHUNKS:
+        for lo, hi, who in IN_CHUNKS:
             make_da(PACK - 1, slice(lo, hi))
-        da_q = []
-        for lo, hi, who in CHUNKS:
+        da_codes, da_plane = [], []
+        for lo, hi, who in IN_CHUNKS:
             width = hi - lo
             grouped = keep.tile([P, width, PACK], BF16, name=f"da_grouped{lo}", align_bytes=64)
             weave = nc.vector.tensor_copy if who == "vector" else nc.scalar.copy
@@ -190,32 +198,38 @@ def tile_moe_sub_silu_kernel(
             nc.vector.quantize_mx(
                 out=codes[:].bitcast(FP8X4), scales=plane[:], in_=grouped[:].rearrange("p c t -> p (c t)")
             )
-            da_q.append((codes, plane))
-        for (lo, hi, who), (codes, plane) in zip(CHUNKS, da_q):
+            for c in range(0, width, P):
+                da_codes.append(codes[:, c : c + P])
+                da_plane.append(plane[:, c : c + P])
+        for lo, hi, who in OUT_CHUNKS:
             width = hi - lo
-            per_bank = 512 // width
             out_rows = keep.tile([P, PACK, width], F32, name=f"out_rows{lo}")
-            for d0 in range(0, PACK, per_bank):
-                acc = psum_out.tile([P, per_bank, width], F32, name="acc", tag="acc")
-                for j in range(per_bank):
+            grouped = keep.tile([P, width, PACK], BF16, name=f"out_grouped{lo}", align_bytes=64)
+            for c in range(0, width, P):
+                block = (lo + c) // P
+                acc = psum.tile([P, PACK, P], F32, name="acc", tag=f"bank{(block + 2) % 8}")
+                for d in range(PACK):
                     nc.tensor.matmul_mx(
-                        out=acc[:, j, :],
-                        lhsT=w1_w[:, d0 + j, :].bitcast(FP8X4),
-                        lhsT_scale=w1_plane[:, d0 + j, :],
-                        rhs=codes[:].bitcast(FP8X4),
-                        rhs_scale=plane[:],
+                        out=acc[:, d, :],
+                        lhsT=w1_w[:, d, :].bitcast(FP8X4),
+                        lhsT_scale=w1_plane[:, d, :],
+                        rhs=da_codes[block].bitcast(FP8X4),
+                        rhs_scale=da_plane[block],
                         start=True,
                         stop=True,
                     )
-                nc.scalar.copy(out=out_rows[:, d0 : d0 + per_bank, :], in_=acc[:])
+                nc.scalar.copy(out=out_rows[:, :, c : c + P], in_=acc[:])
+                if who == "scalar":
+                    nc.scalar.copy(out=grouped[:, c : c + P, :], in_=acc[:].rearrange("p d c -> p c d"))
             nc.sync.dma_start(out=out_rows_hbm[:, :, lo:hi], in_=out_rows[:])
-            grouped = keep.tile([P, width, PACK], BF16, name=f"out_grouped{lo}", align_bytes=64)
-            nc.vector.tensor_copy(out=grouped[:], in_=out_rows[:].rearrange("p d c -> p c d"))
+            if who == "vector":
+                nc.vector.tensor_copy(out=grouped[:], in_=out_rows[:].rearrange("p d c -> p c d"))
             nc.vector.quantize_mx(
                 out=out_codes[:, lo:hi].bitcast(FP8X4),
                 scales=out_plane[:, lo:hi],
                 in_=grouped[:].rearrange("p c d -> p (c d)"),
             )
+        for lo, hi in ((0, 512), (512, 768)):
             nc.sync.dma_start(out=codes_hbm[:, lo:hi], in_=out_codes[:, lo:hi].bitcast(I32))
         for q in range(4):
             nc.sync.dma_start(

@@ -23,8 +23,7 @@ PASSES = N // (P * PACK)
 LIST_ROWS = 16
 EARLY = 2
 SCATTER_GROUPS = ((0, 1), (1, 2), (2, 4), (4, 6))
-IN_CHUNKS = ((0, 128, "vector"), (128, 384, "scalar"), (384, 640, "vector"), (640, 768, "vector"))
-OUT_CHUNKS = ((0, 256, "vector"), (256, 512, "vector"), (512, 640, "vector"), (640, 768, "vector"))
+CHUNKS = ((0, 128, "scalar", "vector"), (128, 384, "scalar", "vector"), (384, 640, "scalar", "vector"), (640, 768, "vector", "scalar"))
 
 
 def tile_moe_sub_silu_kernel(
@@ -49,14 +48,23 @@ def tile_moe_sub_silu_kernel(
         offsets = keep.tile([P, E * C // LIST_ROWS], U16, name="offsets")
         nc.sync.dma_start(offsets[:], offs)
 
-        dy_plane = keep.tile([P, PASSES, T], U8, name="dy_plane", align_bytes=64)
-        nc.gpsimd.memset(dy_plane[:].rearrange("p s t -> p (s t)").bitcast(I32), 0)
-        load_scale_rows(dy_plane, dy_scales)
+        dy_both = keep.tile([P, 1024], U8, name="dy_both", tag="dy_both", align_bytes=64)
+        nc.gpsimd.memset(dy_both[:].bitcast(I32), 0)
+        for q in range(4):
+            nc.sync.dma_start(
+                out=dy_both[32 * q : 32 * q + 8, 0:T].bitcast(I32), in_=dy_scales[:, 4 * q : 4 * q + 4, :].bitcast(I32)
+            )
         dy_w = []
         for s in range(PASSES):
-            w = keep.tile([P, T], I32, name=f"dy_w{s}", align_bytes=64)
+            w = keep.tile([P, T], I32, name=f"dy_w{s}", tag=f"dy_w{s}", align_bytes=64)
             nc.sync.dma_start(out=w[:], in_=dy_words[s].rearrange("p t d -> p (t d)").bitcast(I32))
             dy_w.append(w)
+        gate_rows = keep.tile([P, C], F32, name="gate_rows", tag="gate_rows64", align_bytes=64)
+        nc.sync.dma_start(out=gate_rows[:], in_=gate.rearrange("p (e u) -> (p e) u", u=C)[0:P, :])
+
+        warm = keep.tile([P, 8], F32, name="warm", tag="warm", align_bytes=64)
+        nc.gpsimd.memset(warm[:], 0.0)
+        nc.scalar.activation(out=warm[:, 0:1], in_=warm[:, 1:2], func=ACT.Sigmoid)
 
         w2_scale_rows = w2t_scales.rearrange("e s b i -> (e s) b i")
         w2_plane_early = keep.tile([P, EARLY * PASSES, H], U8, name="w2_plane_early", align_bytes=64)
@@ -67,34 +75,20 @@ def tile_moe_sub_silu_kernel(
         w2_plane.extend(w2_plane_late[:, g, :] for g in range((E - EARLY) * PASSES))
         w1_plane_raw = keep.tile([P, 1, K], U8, name="w1_plane_raw", align_bytes=64)
         nc.vector.memset(w1_plane_raw[:].rearrange("p g k -> p (g k)").bitcast(I32), 0)
-        gate_rows = keep.tile([P, C], F32, name="gate_rows")
-        a_rows = keep.tile([P, PACK, T], F32, name="a_rows")
-        a_hbm = a.rearrange("(p t) c -> p t c", t=PACK)
-        w1_raw = keep.tile([P, K], I32, name="w1_raw")
-        w2_w = []
+        w2_w = {}
 
-        def load_experts(first, last):
-            w = keep.tile([P, (last - first) * PASSES, 2 * H], U8, name=f"w2_w{first}", align_bytes=64)
+        def load_experts(first, last, tag):
+            w = keep.tile([P, (last - first) * PASSES, 2 * H], U8, name=f"w2_w{first}", tag=tag, align_bytes=64)
             nc.sync.dma_start(
                 out=w[:].bitcast(I32),
                 in_=w2t_words[first:last].rearrange("e s p b -> p (e s) b").bitcast(I32),
             )
             for e in range(first, last):
-                w2_w.append([w[:, (e - first) * PASSES + s, :] for s in range(PASSES)])
+                w2_w[e] = [w[:, (e - first) * PASSES + s, :] for s in range(PASSES)]
 
-        load_experts(0, 2)
-        nc.sync.dma_start(out=gate_rows[:], in_=gate.rearrange("p (e u) -> (p e) u", u=C)[0:P, :])
         load_scale_rows(w2_plane_early, w2_scale_rows[0 : EARLY * PASSES])
-        nc.sync.dma_start(out=w1_raw[:], in_=w1t_words[0].rearrange("p k d -> p (k d)").bitcast(I32))
-        load_scale_rows(w1_plane_raw, w1t_scales)
-        load_scale_rows(w2_plane_late, w2_scale_rows[EARLY * PASSES : E * PASSES])
-        load_experts(2, 4)
-        load_experts(4, 6)
-        nc.sync.dma_start(out=a_rows[:], in_=a_hbm)
+        load_experts(0, 2, "warm")
 
-        warm = keep.tile([P, 8], F32, name="warm")
-        nc.gpsimd.memset(warm[:], 0.0)
-        nc.scalar.activation(out=warm[:, 0:1], in_=warm[:, 1:2], func=ACT.Sigmoid)
         identity = keep.tile([P, P], F32, name="identity")
         make_identity(nc, identity[:])
         gate_ps = psum.tile([P, PACK, C], F32, name="gate_ps", tag="bank7")
@@ -115,13 +109,29 @@ def tile_moe_sub_silu_kernel(
         def words_of_pass(s):
             return dy_w[s][:].bitcast(U32)
 
-        def scales_of_pass(s):
-            return dy_plane[:, s, :]
-
-        gather(scales_of_pass, 0, 2, U8, "early_plane", "early_plane", slot_plane)
+        slot_both = keep.tile([P, E * C], U8, name="slot_both", align_bytes=64)
+        nc.vector.tensor_copy(out=slot_both[:], in_=dy_both[:].indirect(offsets[:]))
+        slot_second = keep.tile([P, E * C], U8, name="slot_second", align_bytes=64)
+        nc.gpsimd.memset(slot_second[:].bitcast(I32), 0)
+        for q in range(4):
+            nc.sync.dma_start(
+                out=slot_second[32 * q : 32 * q + 4, :].bitcast(I32),
+                in_=slot_both[32 * q + 4 : 32 * q + 8, :].bitcast(I32),
+            )
+        for e in range(E):
+            slot_plane[e, 0] = slot_both[:, e * C : (e + 1) * C]
+            slot_plane[e, 1] = slot_second[:, e * C : (e + 1) * C]
         gather(words_of_pass, 0, 2, U32, "early_words", "early_words", slot_w)
         gather(words_of_pass, 2, E, U32, "late_words", "late_words", slot_w)
 
+        w1_raw = keep.tile([P, K], I32, name="w1_raw", tag="gate_rows64", align_bytes=64)
+        nc.sync.dma_start(out=w1_raw[:], in_=w1t_words[0].rearrange("p k d -> p (k d)").bitcast(I32))
+        load_scale_rows(w1_plane_raw, w1t_scales)
+        load_experts(2, 4, "dy_both")
+        load_scale_rows(w2_plane_late, w2_scale_rows[EARLY * PASSES : E * PASSES])
+        load_experts(4, 6, "dy_w0")
+        a_rows = keep.tile([P, PACK, T], F32, name="a_rows", tag="dy_w1", align_bytes=64)
+        nc.sync.dma_start(out=a_rows[:], in_=a.rearrange("(p t) c -> p t c", t=PACK))
         w1_w = keep.tile([P, PACK, P], I32, name="w1_w", align_bytes=64)
         nc.vector.tensor_copy(out=w1_w[:], in_=w1_raw[:].rearrange("p (m d) -> p d m", d=PACK))
         w1_plane = keep.tile([P, PACK, P], U8, name="w1_plane", align_bytes=64)
@@ -131,9 +141,7 @@ def tile_moe_sub_silu_kernel(
         for first, last in SCATTER_GROUPS:
             y_rows = keep.tile([P, PACK, (last - first) * C], F32, name=f"y_rows{first}")
             for e in range(first, last):
-                if e == 2:
-                    gather(scales_of_pass, 2, E, U8, "late_plane", "early_words", slot_plane)
-                y_ps = psum.tile([P, H], F32, name="y_ps", tag=f"bank{e % 4}")
+                y_ps = psum.tile([P, H], F32, name="y_ps", tag=f"bank{0 if e == 1 else e % 4}")
                 for s in range(PASSES):
                     nc.tensor.matmul_mx(
                         out=y_ps[:],
@@ -145,91 +153,85 @@ def tile_moe_sub_silu_kernel(
                         stop=(s == PASSES - 1),
                     )
                 y_gated = keep.tile([P, PACK, P], F32, name="y_gated", tag=f"y_gated{e}")
-                nc.scalar.activation(
-                    out=y_gated[:],
-                    in_=y_ps[:].rearrange("u (m t) -> u t m", t=PACK),
-                    func=ACT.Copy,
-                    scale=gate_col[:, e : e + 1],
-                )
-                turned = psum.tile([P, PACK, C], F32, name="turned", tag=f"bank{(e + 2) % 4}")
-                for t in range(PACK):
-                    nc.tensor.transpose(turned[:, t, :], y_gated[:, t, :], identity[:])
-                nc.scalar.copy(out=y_rows[:, :, (e - first) * C : (e - first + 1) * C], in_=turned[:])
+                pieces = ((0, 1, 4 + e), (1, PACK, 2 + e)) if e < EARLY else ((0, PACK, (e + 2) % 4),)
+                for t0, t1, bank in pieces:
+                    nc.scalar.activation(
+                        out=y_gated[:, t0:t1, :],
+                        in_=y_ps[:].rearrange("u (m t) -> u t m", t=PACK)[:, t0:t1, :],
+                        func=ACT.Copy,
+                        scale=gate_col[:, e : e + 1],
+                    )
+                for t0, t1, bank in pieces:
+                    turned = psum.tile([P, t1 - t0, C], F32, name="turned", tag=f"bank{bank}")
+                    for t in range(t0, t1):
+                        nc.tensor.transpose(turned[:, t - t0, :], y_gated[:, t, :], identity[:])
+                    nc.scalar.copy(out=y_rows[:, t0:t1, (e - first) * C : (e - first + 1) * C], in_=turned[:])
             for t in range(PACK):
                 nc.vector.tensor_copy(out=dh[t][:].indirect(offsets_of(first, last)), in_=y_rows[:, t, :])
 
         sig = keep.tile([P, PACK, T], F32, name="sig", tag="y_gated1")
-        for q in range(PACK):
-            cols = slice(q * T // PACK, (q + 1) * T // PACK)
-            nc.scalar.activation(out=sig[:, :, cols], in_=a_rows[:, :, cols], func=ACT.Sigmoid)
-        d_silu = []
         for t in range(PACK):
-            nc.scalar.activation(out=a_rows[:, t, :], in_=a_rows[:, t, :], func=ACT.Silu, scale=-1.0)
-            x = keep.tile([P, T], F32, name=f"d_silu{t}")
-            nc.vector.scalar_tensor_tensor(
-                out=x[:], in0=a_rows[:, t, :], scalar=1.0, in1=sig[:, t, :], op0=ALU.subtract, op1=ALU.mult
-            )
-            d_silu.append(x)
+            nc.scalar.activation(out=sig[:, t, :], in_=a_rows[:, t, :], func=ACT.Sigmoid)
+        nc.scalar.activation(out=a_rows[:], in_=a_rows[:], func=ACT.Silu, scale=-1.0)
 
-        da_rows = keep.tile([P, PACK, T], BF16, name="da_rows")
-
-        def make_da(t, cols):
-            nc.vector.tensor_tensor(out=da_rows[:, t, cols], in0=dh[t][:, cols], in1=d_silu[t][:, cols], op=ALU.mult)
-
-        for t in range(PACK - 1):
-            make_da(t, slice(0, T))
         out_codes = keep.tile([P, T], U32, name="out_codes", align_bytes=64)
         out_plane = keep.tile([P, T], U8, name="out_plane", align_bytes=64)
         out_rows_hbm = out_0.rearrange("(p d) t -> p d t", d=PACK)
         codes_hbm = out_1[0].rearrange("p t d -> p (t d)").bitcast(I32)
-        for lo, hi, who in IN_CHUNKS:
-            make_da(PACK - 1, slice(lo, hi))
-        da_codes, da_plane = [], []
-        for lo, hi, who in IN_CHUNKS:
+        da_q = []
+        for lo, hi, weaver, caster in CHUNKS:
             width = hi - lo
-            grouped = keep.tile([P, width, PACK], BF16, name=f"da_grouped{lo}", align_bytes=64)
-            weave = nc.vector.tensor_copy if who == "vector" else nc.scalar.copy
+            d_silu = keep.tile([P, PACK, width], F32, name=f"d_silu{lo}")
+            nc.vector.scalar_tensor_tensor(
+                out=d_silu[:], in0=a_rows[:, :, lo:hi], scalar=1.0, in1=sig[:, :, lo:hi], op0=ALU.subtract, op1=ALU.mult
+            )
+            da_rows = keep.tile([P, PACK, width], BF16, name=f"da_rows{lo}")
+            for t in range(PACK):
+                nc.vector.tensor_tensor(out=da_rows[:, t, :], in0=dh[t][:, lo:hi], in1=d_silu[:, t, :], op=ALU.mult)
+            da_grouped = keep.tile([P, width, PACK], BF16, name=f"da_grouped{lo}", align_bytes=64)
+            weave = nc.vector.tensor_copy if weaver == "vector" else nc.scalar.copy
             weave(
-                out=grouped[:].rearrange("p (c i) t -> p c t i", i=4),
-                in_=da_rows[:, :, lo:hi].rearrange("p t (c i) -> p c t i", i=4),
+                out=da_grouped[:].rearrange("p (c i) t -> p c t i", i=4),
+                in_=da_rows[:].rearrange("p t (c i) -> p c t i", i=4),
             )
             codes = keep.tile([P, width], U32, name=f"da_codes{lo}", align_bytes=64)
             plane = keep.tile([P, width], U8, name=f"da_plane{lo}", align_bytes=64)
             nc.vector.quantize_mx(
-                out=codes[:].bitcast(FP8X4), scales=plane[:], in_=grouped[:].rearrange("p c t -> p (c t)")
+                out=codes[:].bitcast(FP8X4), scales=plane[:], in_=da_grouped[:].rearrange("p c t -> p (c t)")
             )
-            for c in range(0, width, P):
-                da_codes.append(codes[:, c : c + P])
-                da_plane.append(plane[:, c : c + P])
-        for lo, hi, who in OUT_CHUNKS:
+            da_q.append((codes, plane))
+        for (lo, hi, weaver, caster), (codes, plane) in zip(CHUNKS, da_q):
             width = hi - lo
             out_rows = keep.tile([P, PACK, width], F32, name=f"out_rows{lo}")
             grouped = keep.tile([P, width, PACK], BF16, name=f"out_grouped{lo}", align_bytes=64)
             for c in range(0, width, P):
                 block = (lo + c) // P
-                acc = psum.tile([P, PACK, P], F32, name="acc", tag=f"bank{(block + 2) % 8}")
+                acc = psum.tile([P, PACK, P], F32, name="acc", tag=f"bank{block}")
                 for d in range(PACK):
                     nc.tensor.matmul_mx(
                         out=acc[:, d, :],
                         lhsT=w1_w[:, d, :].bitcast(FP8X4),
                         lhsT_scale=w1_plane[:, d, :],
-                        rhs=da_codes[block].bitcast(FP8X4),
-                        rhs_scale=da_plane[block],
+                        rhs=codes[:, c : c + P].bitcast(FP8X4),
+                        rhs_scale=plane[:, c : c + P],
                         start=True,
                         stop=True,
                     )
                 nc.scalar.copy(out=out_rows[:, :, c : c + P], in_=acc[:])
-                if who == "scalar":
+                if caster == "scalar":
                     nc.scalar.copy(out=grouped[:, c : c + P, :], in_=acc[:].rearrange("p d c -> p c d"))
             nc.sync.dma_start(out=out_rows_hbm[:, :, lo:hi], in_=out_rows[:])
-            if who == "vector":
-                nc.vector.tensor_copy(out=grouped[:], in_=out_rows[:].rearrange("p d c -> p c d"))
+            if caster == "vector":
+                nc.vector.tensor_copy(
+                    out=grouped[:].rearrange("p (c i) d -> p c d i", i=4),
+                    in_=out_rows[:].rearrange("p d (c i) -> p c d i", i=4),
+                )
             nc.vector.quantize_mx(
                 out=out_codes[:, lo:hi].bitcast(FP8X4),
                 scales=out_plane[:, lo:hi],
                 in_=grouped[:].rearrange("p c d -> p (c d)"),
             )
-        for lo, hi in ((0, 512), (512, 768)):
+        for lo, hi in ((0, 384), (384, 768)):
             nc.sync.dma_start(out=codes_hbm[:, lo:hi], in_=out_codes[:, lo:hi].bitcast(I32))
         for q in range(4):
             nc.sync.dma_start(

@@ -20,10 +20,17 @@ ALU = mybir.AluOpType
 P = 128
 PACK = 4
 PASSES = N // (P * PACK)
+QUADRANT = 32
+SCALE_ROWS = 16
 LIST_ROWS = 16
+SCALE_WINDOW = 1024
 EARLY = 2
 SCATTER_GROUPS = ((0, 1), (1, 2), (2, 4), (4, 6))
-CHUNKS = ((0, 128, "scalar", "vector"), (128, 384, "scalar", "vector"), (384, 640, "scalar", "vector"), (640, 768, "vector", "scalar"))
+BLOCKS = T // P
+FIRST_DA_BLOCK_ON_VECTOR = BLOCKS - 1
+FIRST_OUT_BLOCK_ON_VECTOR = BLOCKS // 2
+OUT_GROUPS = ((0, 2), (2, 4), (4, 5), (5, 6))
+CODE_STORES = ((0, 512), (512, T))
 
 
 def tile_moe_sub_silu_kernel(
@@ -34,32 +41,36 @@ def tile_moe_sub_silu_kernel(
         keep = ctx.enter_context(tc.tile_pool(name="keep", bufs=1))
         psum = ctx.enter_context(tc.psum_pool(name="psum", bufs=1))
 
-
         def offsets_of(first, last):
             return offsets[:, first * C // LIST_ROWS : last * C // LIST_ROWS]
 
-        def load_scale_rows(plane, rows):
+        def load_scale_planes(planes, rows):
             for r in range(4):
                 nc.sync.dma_start(
-                    out=plane[r:P:32, :, :].bitcast(I32),
-                    in_=rows[:, r:16:4, :].rearrange("g q n -> q g n").bitcast(I32),
+                    out=planes[r:P:QUADRANT, :, :].bitcast(I32),
+                    in_=rows[:, r:SCALE_ROWS:4, :].rearrange("g q n -> q g n").bitcast(I32),
                 )
+
+        def four_rows_side_by_side(copy, grouped, rows):
+            copy(
+                out=grouped.rearrange("p (c j) t -> p c t j", j=4),
+                in_=rows.rearrange("p t (c j) -> p c t j", j=4),
+            )
 
         offsets = keep.tile([P, E * C // LIST_ROWS], U16, name="offsets")
         nc.sync.dma_start(offsets[:], offs)
 
-        dy_both = keep.tile([P, 1024], U8, name="dy_both", tag="dy_both", align_bytes=64)
-        nc.gpsimd.memset(dy_both[:].bitcast(I32), 0)
+        token_scales = keep.tile([P, SCALE_WINDOW], U8, name="token_scales", tag="token_scales", align_bytes=64)
+        nc.gpsimd.memset(token_scales[:].bitcast(I32), 0)
         for q in range(4):
             nc.sync.dma_start(
-                out=dy_both[32 * q : 32 * q + 8, 0:T].bitcast(I32), in_=dy_scales[:, 4 * q : 4 * q + 4, :].bitcast(I32)
+                out=token_scales[QUADRANT * q : QUADRANT * q + 4 * PASSES, 0:T].bitcast(I32),
+                in_=dy_scales[:, 4 * q : 4 * q + 4, :].bitcast(I32),
             )
-        dy_w = []
-        for s in range(PASSES):
-            w = keep.tile([P, T], I32, name=f"dy_w{s}", tag=f"dy_w{s}", align_bytes=64)
-            nc.sync.dma_start(out=w[:], in_=dy_words[s].rearrange("p t d -> p (t d)").bitcast(I32))
-            dy_w.append(w)
-        gate_rows = keep.tile([P, C], F32, name="gate_rows", tag="gate_rows64", align_bytes=64)
+        token_words = keep.tile([P, PASSES, T], I32, name="token_words", tag="token_words", align_bytes=64)
+        nc.sync.dma_start(out=token_words[:], in_=dy_words.rearrange("s p t d -> p s (t d)").bitcast(I32))
+
+        gate_rows = keep.tile([P, C], F32, name="gate_rows", tag="gate_rows", align_bytes=64)
         nc.sync.dma_start(out=gate_rows[:], in_=gate.rearrange("p (e u) -> (p e) u", u=C)[0:P, :])
 
         warm = keep.tile([P, 8], F32, name="warm", tag="warm", align_bytes=64)
@@ -67,99 +78,95 @@ def tile_moe_sub_silu_kernel(
         nc.scalar.activation(out=warm[:, 0:1], in_=warm[:, 1:2], func=ACT.Sigmoid)
 
         w2_scale_rows = w2t_scales.rearrange("e s b i -> (e s) b i")
-        w2_plane_early = keep.tile([P, EARLY * PASSES, H], U8, name="w2_plane_early", align_bytes=64)
-        nc.vector.memset(w2_plane_early[:].rearrange("p g i -> p (g i)").bitcast(I32), 0)
-        w2_plane_late = keep.tile([P, (E - EARLY) * PASSES, H], U8, name="w2_plane_late", align_bytes=64)
-        nc.vector.memset(w2_plane_late[:].rearrange("p g i -> p (g i)").bitcast(I32), 0)
-        w2_plane = [w2_plane_early[:, g, :] for g in range(EARLY * PASSES)]
-        w2_plane.extend(w2_plane_late[:, g, :] for g in range((E - EARLY) * PASSES))
+        w2_planes_early = keep.tile([P, EARLY * PASSES, H], U8, name="w2_planes_early", align_bytes=64)
+        nc.vector.memset(w2_planes_early[:].rearrange("p g i -> p (g i)").bitcast(I32), 0)
+        w2_planes_late = keep.tile([P, (E - EARLY) * PASSES, H], U8, name="w2_planes_late", align_bytes=64)
+        nc.vector.memset(w2_planes_late[:].rearrange("p g i -> p (g i)").bitcast(I32), 0)
+        w2_plane = [w2_planes_early[:, g, :] for g in range(EARLY * PASSES)]
+        w2_plane.extend(w2_planes_late[:, g, :] for g in range((E - EARLY) * PASSES))
         w1_plane_raw = keep.tile([P, 1, K], U8, name="w1_plane_raw", align_bytes=64)
         nc.vector.memset(w1_plane_raw[:].rearrange("p g k -> p (g k)").bitcast(I32), 0)
-        w2_w = {}
+        w2_words = {}
 
-        def load_experts(first, last, tag):
-            w = keep.tile([P, (last - first) * PASSES, 2 * H], U8, name=f"w2_w{first}", tag=tag, align_bytes=64)
+        def load_expert_pair(first, tag):
+            pair = keep.tile([P, 2 * PASSES, 2 * H], U8, name=f"w2_words{first}", tag=tag, align_bytes=64)
             nc.sync.dma_start(
-                out=w[:].bitcast(I32),
-                in_=w2t_words[first:last].rearrange("e s p b -> p (e s) b").bitcast(I32),
+                out=pair[:].bitcast(I32),
+                in_=w2t_words[first : first + 2].rearrange("e s p b -> p (e s) b").bitcast(I32),
             )
-            for e in range(first, last):
-                w2_w[e] = [w[:, (e - first) * PASSES + s, :] for s in range(PASSES)]
+            for g in range(2 * PASSES):
+                w2_words[first * PASSES + g] = pair[:, g, :]
 
-        load_scale_rows(w2_plane_early, w2_scale_rows[0 : EARLY * PASSES])
-        load_experts(0, 2, "warm")
+        load_scale_planes(w2_planes_early, w2_scale_rows[0 : EARLY * PASSES])
+        load_expert_pair(0, "warm")
 
         identity = keep.tile([P, P], F32, name="identity")
         make_identity(nc, identity[:])
-        gate_ps = psum.tile([P, PACK, C], F32, name="gate_ps", tag="bank7")
-        nc.tensor.transpose(gate_ps[:, 0, :], gate_rows[:], identity[:])
-        gate_col = keep.tile([P, E], F32, name="gate_col")
-        nc.scalar.activation(out=gate_col[:], in_=gate_ps[:, 0, 0:E], func=ACT.Copy, scale=-1.0)
+        gate_turned = psum.tile([P, C], F32, name="gate_turned", tag="bank7")
+        nc.tensor.transpose(gate_turned[:], gate_rows[:], identity[:])
+        neg_gate = keep.tile([P, E], F32, name="neg_gate")
+        nc.scalar.activation(out=neg_gate[:], in_=gate_turned[:, 0:E], func=ACT.Copy, scale=-1.0)
 
-        slot_w, slot_plane = {}, {}
-
-        def gather(window_of_pass, first, last, dtype, name, tag, into):
-            width = (last - first) * C
-            gathered = keep.tile([P, PASSES, width], dtype, name=name, tag=tag, align_bytes=64)
-            for s in range(PASSES):
-                nc.vector.tensor_copy(out=gathered[:, s, :], in_=window_of_pass(s).indirect(offsets_of(first, last)))
-                for e in range(first, last):
-                    into[e, s] = gathered[:, s, (e - first) * C : (e - first + 1) * C]
-
-        def words_of_pass(s):
-            return dy_w[s][:].bitcast(U32)
-
-        slot_both = keep.tile([P, E * C], U8, name="slot_both", align_bytes=64)
-        nc.vector.tensor_copy(out=slot_both[:], in_=dy_both[:].indirect(offsets[:]))
-        slot_second = keep.tile([P, E * C], U8, name="slot_second", align_bytes=64)
-        nc.gpsimd.memset(slot_second[:].bitcast(I32), 0)
+        slot_scales = keep.tile([P, E * C], U8, name="slot_scales", align_bytes=64)
+        nc.vector.tensor_copy(out=slot_scales[:], in_=token_scales[:].indirect(offsets[:]))
+        slot_scales_second = keep.tile([P, E * C], U8, name="slot_scales_second", align_bytes=64)
+        nc.gpsimd.memset(slot_scales_second[:].bitcast(I32), 0)
         for q in range(4):
             nc.sync.dma_start(
-                out=slot_second[32 * q : 32 * q + 4, :].bitcast(I32),
-                in_=slot_both[32 * q + 4 : 32 * q + 8, :].bitcast(I32),
+                out=slot_scales_second[QUADRANT * q : QUADRANT * q + 4, :].bitcast(I32),
+                in_=slot_scales[QUADRANT * q + 4 : QUADRANT * q + 8, :].bitcast(I32),
             )
-        for e in range(E):
-            slot_plane[e, 0] = slot_both[:, e * C : (e + 1) * C]
-            slot_plane[e, 1] = slot_second[:, e * C : (e + 1) * C]
-        gather(words_of_pass, 0, 2, U32, "early_words", "early_words", slot_w)
-        gather(words_of_pass, 2, E, U32, "late_words", "late_words", slot_w)
+        slot_plane = (slot_scales, slot_scales_second)
 
-        w1_raw = keep.tile([P, K], I32, name="w1_raw", tag="gate_rows64", align_bytes=64)
-        nc.sync.dma_start(out=w1_raw[:], in_=w1t_words[0].rearrange("p k d -> p (k d)").bitcast(I32))
-        load_scale_rows(w1_plane_raw, w1t_scales)
-        load_experts(2, 4, "dy_both")
-        load_scale_rows(w2_plane_late, w2_scale_rows[EARLY * PASSES : E * PASSES])
-        load_experts(4, 6, "dy_w0")
-        a_rows = keep.tile([P, PACK, T], F32, name="a_rows", tag="dy_w1", align_bytes=64)
+        slot_words = {}
+        for first, last, name in ((0, EARLY, "early_words"), (EARLY, E, "late_words")):
+            gathered = keep.tile([P, PASSES, (last - first) * C], U32, name=name, tag=name, align_bytes=64)
+            for s in range(PASSES):
+                nc.vector.tensor_copy(
+                    out=gathered[:, s, :], in_=token_words[:, s, :].bitcast(U32).indirect(offsets_of(first, last))
+                )
+                for e in range(first, last):
+                    slot_words[e, s] = gathered[:, s, (e - first) * C : (e - first + 1) * C]
+
+        w1_words_raw = keep.tile([P, K], I32, name="w1_words_raw", tag="gate_rows", align_bytes=64)
+        nc.sync.dma_start(out=w1_words_raw[:], in_=w1t_words[0].rearrange("p k d -> p (k d)").bitcast(I32))
+        load_scale_planes(w1_plane_raw, w1t_scales)
+        load_expert_pair(2, "token_scales")
+        load_scale_planes(w2_planes_late, w2_scale_rows[EARLY * PASSES : E * PASSES])
+        a_rows = keep.tile([P, PACK, T], F32, name="a_rows", tag="token_words", align_bytes=64)
         nc.sync.dma_start(out=a_rows[:], in_=a.rearrange("(p t) c -> p t c", t=PACK))
-        w1_w = keep.tile([P, PACK, P], I32, name="w1_w", align_bytes=64)
-        nc.vector.tensor_copy(out=w1_w[:], in_=w1_raw[:].rearrange("p (m d) -> p d m", d=PACK))
+
+        w1_words = keep.tile([P, PACK, P], I32, name="w1_words", align_bytes=64)
+        nc.vector.tensor_copy(out=w1_words[:], in_=w1_words_raw[:].rearrange("p (m d) -> p d m", d=PACK))
         w1_plane = keep.tile([P, PACK, P], U8, name="w1_plane", align_bytes=64)
         nc.vector.tensor_copy(out=w1_plane[:], in_=w1_plane_raw[:, 0, :].rearrange("p (m d) -> p d m", d=PACK))
 
-        dh = [keep.tile([P, T], F32, name=f"dh{t}") for t in range(PACK)]
+        neg_dh = [keep.tile([P, T], F32, name=f"neg_dh{t}") for t in range(PACK)]
         for first, last in SCATTER_GROUPS:
             y_rows = keep.tile([P, PACK, (last - first) * C], F32, name=f"y_rows{first}")
             for e in range(first, last):
-                y_ps = psum.tile([P, H], F32, name="y_ps", tag=f"bank{0 if e == 1 else e % 4}")
+                if e == EARLY:
+                    load_expert_pair(4, "early_words")
+                y_by_slot = psum.tile([P, H], F32, name="y_by_slot", tag=f"bank{0 if e < EARLY else e % 4}")
                 for s in range(PASSES):
                     nc.tensor.matmul_mx(
-                        out=y_ps[:],
-                        lhsT=slot_w[e, s].bitcast(FP8X4),
-                        lhsT_scale=slot_plane[e, s],
-                        rhs=w2_w[e][s].bitcast(FP4X4),
+                        out=y_by_slot[:],
+                        lhsT=slot_words[e, s].bitcast(FP8X4),
+                        lhsT_scale=slot_plane[s][:, e * C : (e + 1) * C],
+                        rhs=w2_words[e * PASSES + s].bitcast(FP4X4),
                         rhs_scale=w2_plane[e * PASSES + s],
                         start=(s == 0),
                         stop=(s == PASSES - 1),
                     )
                 y_gated = keep.tile([P, PACK, P], F32, name="y_gated", tag=f"y_gated{e}")
-                pieces = ((0, 1, 4 + e), (1, PACK, 2 + e)) if e < EARLY else ((0, PACK, (e + 2) % 4),)
+                ring_bank = (e + 2) % 4
+                pieces = ((0, 1, 4 + e), (1, PACK, ring_bank)) if e < EARLY else ((0, PACK, ring_bank),)
                 for t0, t1, bank in pieces:
                     nc.scalar.activation(
                         out=y_gated[:, t0:t1, :],
-                        in_=y_ps[:].rearrange("u (m t) -> u t m", t=PACK)[:, t0:t1, :],
+                        in_=y_by_slot[:].rearrange("u (m t) -> u t m", t=PACK)[:, t0:t1, :],
                         func=ACT.Copy,
-                        scale=gate_col[:, e : e + 1],
+                        scale=neg_gate[:, e : e + 1],
                     )
                 for t0, t1, bank in pieces:
                     turned = psum.tile([P, t1 - t0, C], F32, name="turned", tag=f"bank{bank}")
@@ -167,73 +174,91 @@ def tile_moe_sub_silu_kernel(
                         nc.tensor.transpose(turned[:, t - t0, :], y_gated[:, t, :], identity[:])
                     nc.scalar.copy(out=y_rows[:, t0:t1, (e - first) * C : (e - first + 1) * C], in_=turned[:])
             for t in range(PACK):
-                nc.vector.tensor_copy(out=dh[t][:].indirect(offsets_of(first, last)), in_=y_rows[:, t, :])
+                nc.vector.tensor_copy(out=neg_dh[t][:].indirect(offsets_of(first, last)), in_=y_rows[:, t, :])
 
         sig = keep.tile([P, PACK, T], F32, name="sig", tag="y_gated1")
         for t in range(PACK):
             nc.scalar.activation(out=sig[:, t, :], in_=a_rows[:, t, :], func=ACT.Sigmoid)
-        nc.scalar.activation(out=a_rows[:], in_=a_rows[:], func=ACT.Silu, scale=-1.0)
+        silu_of_neg_a = a_rows
+        nc.scalar.activation(out=silu_of_neg_a[:], in_=a_rows[:], func=ACT.Silu, scale=-1.0)
 
         out_codes = keep.tile([P, T], U32, name="out_codes", align_bytes=64)
         out_plane = keep.tile([P, T], U8, name="out_plane", align_bytes=64)
-        out_rows_hbm = out_0.rearrange("(p d) t -> p d t", d=PACK)
-        codes_hbm = out_1[0].rearrange("p t d -> p (t d)").bitcast(I32)
-        da_q = []
-        for lo, hi, weaver, caster in CHUNKS:
-            width = hi - lo
-            d_silu = keep.tile([P, PACK, width], F32, name=f"d_silu{lo}")
+
+        def make_neg_d_silu(block):
+            tokens = slice(block * P, (block + 1) * P)
+            neg_d_silu = keep.tile([P, PACK, P], F32, name=f"neg_d_silu{block}")
             nc.vector.scalar_tensor_tensor(
-                out=d_silu[:], in0=a_rows[:, :, lo:hi], scalar=1.0, in1=sig[:, :, lo:hi], op0=ALU.subtract, op1=ALU.mult
+                out=neg_d_silu[:],
+                in0=silu_of_neg_a[:, :, tokens],
+                scalar=1.0,
+                in1=sig[:, :, tokens],
+                op0=ALU.subtract,
+                op1=ALU.mult,
             )
-            da_rows = keep.tile([P, PACK, width], BF16, name=f"da_rows{lo}")
+            return neg_d_silu
+
+        def make_da(block, neg_d_silu):
+            tokens = slice(block * P, (block + 1) * P)
+            da_rows = keep.tile([P, PACK, P], BF16, name=f"da_rows{block}")
             for t in range(PACK):
-                nc.vector.tensor_tensor(out=da_rows[:, t, :], in0=dh[t][:, lo:hi], in1=d_silu[:, t, :], op=ALU.mult)
-            da_grouped = keep.tile([P, width, PACK], BF16, name=f"da_grouped{lo}", align_bytes=64)
-            weave = nc.vector.tensor_copy if weaver == "vector" else nc.scalar.copy
-            weave(
-                out=da_grouped[:].rearrange("p (c i) t -> p c t i", i=4),
-                in_=da_rows[:].rearrange("p t (c i) -> p c t i", i=4),
-            )
-            codes = keep.tile([P, width], U32, name=f"da_codes{lo}", align_bytes=64)
-            plane = keep.tile([P, width], U8, name=f"da_plane{lo}", align_bytes=64)
+                nc.vector.tensor_tensor(
+                    out=da_rows[:, t, :], in0=neg_dh[t][:, tokens], in1=neg_d_silu[:, t, :], op=ALU.mult
+                )
+            da_grouped = keep.tile([P, P, PACK], BF16, name=f"da_grouped{block}", align_bytes=64)
+            copy = nc.vector.tensor_copy if block >= FIRST_DA_BLOCK_ON_VECTOR else nc.scalar.copy
+            four_rows_side_by_side(copy, da_grouped[:], da_rows[:])
+            da_codes = keep.tile([P, P], U32, name=f"da_codes{block}", align_bytes=64)
+            da_plane = keep.tile([P, P], U8, name=f"da_plane{block}", align_bytes=64)
             nc.vector.quantize_mx(
-                out=codes[:].bitcast(FP8X4), scales=plane[:], in_=da_grouped[:].rearrange("p c t -> p (c t)")
+                out=da_codes[:].bitcast(FP8X4), scales=da_plane[:], in_=da_grouped[:].rearrange("p c t -> p (c t)")
             )
-            da_q.append((codes, plane))
-        for (lo, hi, weaver, caster), (codes, plane) in zip(CHUNKS, da_q):
-            width = hi - lo
-            out_rows = keep.tile([P, PACK, width], F32, name=f"out_rows{lo}")
-            grouped = keep.tile([P, width, PACK], BF16, name=f"out_grouped{lo}", align_bytes=64)
-            for c in range(0, width, P):
-                block = (lo + c) // P
+            return da_codes, da_plane
+
+        factors = [make_neg_d_silu(0)]
+        da_quantised = []
+        for block in range(BLOCKS):
+            if block + 1 < BLOCKS:
+                factors.append(make_neg_d_silu(block + 1))
+            da_quantised.append(make_da(block, factors[block]))
+
+        out_rows_hbm = out_0.rearrange("(p d) t -> p d t", d=PACK)
+        for first, last in OUT_GROUPS:
+            group = slice(first * P, last * P)
+            out_rows = keep.tile([P, PACK, (last - first) * P], F32, name=f"out_rows{first}")
+            out_grouped = keep.tile([P, (last - first) * P, PACK], BF16, name=f"out_grouped{first}", align_bytes=64)
+            for block in range(first, last):
+                da_codes, da_plane = da_quantised[block]
+                cols = slice((block - first) * P, (block - first + 1) * P)
                 acc = psum.tile([P, PACK, P], F32, name="acc", tag=f"bank{block}")
                 for d in range(PACK):
                     nc.tensor.matmul_mx(
                         out=acc[:, d, :],
-                        lhsT=w1_w[:, d, :].bitcast(FP8X4),
+                        lhsT=w1_words[:, d, :].bitcast(FP8X4),
                         lhsT_scale=w1_plane[:, d, :],
-                        rhs=codes[:, c : c + P].bitcast(FP8X4),
-                        rhs_scale=plane[:, c : c + P],
+                        rhs=da_codes[:].bitcast(FP8X4),
+                        rhs_scale=da_plane[:],
                         start=True,
                         stop=True,
                     )
-                nc.scalar.copy(out=out_rows[:, :, c : c + P], in_=acc[:])
-                if caster == "scalar":
-                    nc.scalar.copy(out=grouped[:, c : c + P, :], in_=acc[:].rearrange("p d c -> p c d"))
-            nc.sync.dma_start(out=out_rows_hbm[:, :, lo:hi], in_=out_rows[:])
-            if caster == "vector":
-                nc.vector.tensor_copy(
-                    out=grouped[:].rearrange("p (c i) d -> p c d i", i=4),
-                    in_=out_rows[:].rearrange("p d (c i) -> p c d i", i=4),
-                )
+                if block < FIRST_OUT_BLOCK_ON_VECTOR:
+                    nc.scalar.copy(out=out_grouped[:, cols, :], in_=acc[:].rearrange("p d c -> p c d"))
+                    nc.scalar.copy(out=out_rows[:, :, cols], in_=acc[:])
+                else:
+                    nc.scalar.copy(out=out_rows[:, :, cols], in_=acc[:])
+                    four_rows_side_by_side(nc.vector.tensor_copy, out_grouped[:, cols, :], out_rows[:, :, cols])
+            nc.sync.dma_start(out=out_rows_hbm[:, :, group], in_=out_rows[:])
             nc.vector.quantize_mx(
-                out=out_codes[:, lo:hi].bitcast(FP8X4),
-                scales=out_plane[:, lo:hi],
-                in_=grouped[:].rearrange("p c d -> p (c d)"),
+                out=out_codes[:, group].bitcast(FP8X4),
+                scales=out_plane[:, group],
+                in_=out_grouped[:].rearrange("p c d -> p (c d)"),
             )
-        for lo, hi in ((0, 384), (384, 768)):
+
+        codes_hbm = out_1[0].rearrange("p t d -> p (t d)").bitcast(I32)
+        for lo, hi in CODE_STORES:
             nc.sync.dma_start(out=codes_hbm[:, lo:hi], in_=out_codes[:, lo:hi].bitcast(I32))
         for q in range(4):
             nc.sync.dma_start(
-                out=out_2[0, 4 * q : 4 * q + 4, :].bitcast(I32), in_=out_plane[32 * q : 32 * q + 4, :].bitcast(I32)
+                out=out_2[0, 4 * q : 4 * q + 4, :].bitcast(I32),
+                in_=out_plane[QUADRANT * q : QUADRANT * q + 4, :].bitcast(I32),
             )

@@ -27,8 +27,8 @@ SCALE_WINDOW = 1024
 EARLY = 2
 SCATTER_GROUPS = ((0, 1), (1, 2), (2, 4), (4, 6))
 BLOCKS = T // P
-FIRST_DA_BLOCK_ON_VECTOR = BLOCKS - 1
-FIRST_OUT_BLOCK_ON_VECTOR = BLOCKS // 2
+RUN = 4
+PRODUCT_GROUPS = ((0, 2), (2, 4), (4, 5), (5, 6))
 OUT_GROUPS = ((0, 2), (2, 4), (4, 5), (5, 6))
 CODE_STORES = ((0, 512), (512, T))
 
@@ -50,12 +50,6 @@ def tile_moe_sub_silu_kernel(
                     out=planes[r:P:QUADRANT, :, :].bitcast(I32),
                     in_=rows[:, r:SCALE_ROWS:4, :].rearrange("g q n -> q g n").bitcast(I32),
                 )
-
-        def four_rows_side_by_side(copy, grouped, rows):
-            copy(
-                out=grouped.rearrange("p (c j) t -> p c t j", j=4),
-                in_=rows.rearrange("p t (c j) -> p c t j", j=4),
-            )
 
         offsets = keep.tile([P, E * C // LIST_ROWS], U16, name="offsets")
         nc.sync.dma_start(offsets[:], offs)
@@ -176,38 +170,43 @@ def tile_moe_sub_silu_kernel(
             for t in range(PACK):
                 nc.vector.tensor_copy(out=neg_dh[t][:].indirect(offsets_of(first, last)), in_=y_rows[:, t, :])
 
-        sig = keep.tile([P, PACK, T], F32, name="sig", tag="y_gated1")
-        for t in range(PACK):
-            nc.scalar.activation(out=sig[:, t, :], in_=a_rows[:, t, :], func=ACT.Sigmoid)
+        sig = keep.tile([P, T // RUN, PACK, RUN], F32, name="sig", tag="y_gated1")
+        a_in_runs = a_rows[:].rearrange("p t (c j) -> p c t j", j=RUN)
+        for piece in range(PACK):
+            runs = slice(piece * T // RUN // PACK, (piece + 1) * T // RUN // PACK)
+            nc.scalar.activation(out=sig[:, runs, :, :], in_=a_in_runs[:, runs, :, :], func=ACT.Sigmoid)
         silu_of_neg_a = a_rows
         nc.scalar.activation(out=silu_of_neg_a[:], in_=a_rows[:], func=ACT.Silu, scale=-1.0)
 
         out_codes = keep.tile([P, T], U32, name="out_codes", align_bytes=64)
         out_plane = keep.tile([P, T], U8, name="out_plane", align_bytes=64)
 
-        def make_neg_d_silu(block):
-            tokens = slice(block * P, (block + 1) * P)
-            neg_d_silu = keep.tile([P, PACK, P], F32, name=f"neg_d_silu{block}")
-            nc.vector.scalar_tensor_tensor(
-                out=neg_d_silu[:],
-                in0=silu_of_neg_a[:, :, tokens],
-                scalar=1.0,
-                in1=sig[:, :, tokens],
-                op0=ALU.subtract,
-                op1=ALU.mult,
-            )
-            return neg_d_silu
+        half_da = keep.tile([P, T // RUN, PACK, RUN], F32, name="half_da")
 
-        def make_da(block, neg_d_silu):
-            tokens = slice(block * P, (block + 1) * P)
-            da_rows = keep.tile([P, PACK, P], BF16, name=f"da_rows{block}")
+        def first_products(first, last):
+            tokens = slice(first * P, last * P)
             for t in range(PACK):
-                nc.vector.tensor_tensor(
-                    out=da_rows[:, t, :], in0=neg_dh[t][:, tokens], in1=neg_d_silu[:, t, :], op=ALU.mult
+                nc.vector.scalar_tensor_tensor(
+                    out=half_da[:, first * P // RUN : last * P // RUN, t, :],
+                    in0=silu_of_neg_a[:, t, tokens].rearrange("p (c j) -> p c j", j=RUN),
+                    scalar=1.0,
+                    in1=neg_dh[t][:, tokens].rearrange("p (c j) -> p c j", j=RUN),
+                    op0=ALU.subtract,
+                    op1=ALU.mult,
                 )
+
+        def second_product(block):
+            runs = slice(block * P // RUN, (block + 1) * P // RUN)
             da_grouped = keep.tile([P, P, PACK], BF16, name=f"da_grouped{block}", align_bytes=64)
-            copy = nc.vector.tensor_copy if block >= FIRST_DA_BLOCK_ON_VECTOR else nc.scalar.copy
-            four_rows_side_by_side(copy, da_grouped[:], da_rows[:])
+            nc.vector.tensor_tensor(
+                out=da_grouped[:].rearrange("p (c j) t -> p c t j", j=RUN),
+                in0=half_da[:, runs, :, :],
+                in1=sig[:, runs, :, :],
+                op=ALU.mult,
+            )
+            return da_grouped
+
+        def quantise_da(block, da_grouped):
             da_codes = keep.tile([P, P], U32, name=f"da_codes{block}", align_bytes=64)
             da_plane = keep.tile([P, P], U8, name=f"da_plane{block}", align_bytes=64)
             nc.vector.quantize_mx(
@@ -215,12 +214,11 @@ def tile_moe_sub_silu_kernel(
             )
             return da_codes, da_plane
 
-        factors = [make_neg_d_silu(0)]
         da_quantised = []
-        for block in range(BLOCKS):
-            if block + 1 < BLOCKS:
-                factors.append(make_neg_d_silu(block + 1))
-            da_quantised.append(make_da(block, factors[block]))
+        for first, last in PRODUCT_GROUPS:
+            first_products(first, last)
+            for block in range(first, last):
+                da_quantised.append(quantise_da(block, second_product(block)))
 
         out_rows_hbm = out_0.rearrange("(p d) t -> p d t", d=PACK)
         for first, last in OUT_GROUPS:
@@ -241,12 +239,8 @@ def tile_moe_sub_silu_kernel(
                         start=True,
                         stop=True,
                     )
-                if block < FIRST_OUT_BLOCK_ON_VECTOR:
-                    nc.scalar.copy(out=out_grouped[:, cols, :], in_=acc[:].rearrange("p d c -> p c d"))
-                    nc.scalar.copy(out=out_rows[:, :, cols], in_=acc[:])
-                else:
-                    nc.scalar.copy(out=out_rows[:, :, cols], in_=acc[:])
-                    four_rows_side_by_side(nc.vector.tensor_copy, out_grouped[:, cols, :], out_rows[:, :, cols])
+                nc.scalar.copy(out=out_grouped[:, cols, :], in_=acc[:].rearrange("p d c -> p c d"))
+                nc.scalar.copy(out=out_rows[:, :, cols], in_=acc[:])
             nc.sync.dma_start(out=out_rows_hbm[:, :, group], in_=out_rows[:])
             nc.vector.quantize_mx(
                 out=out_codes[:, group].bitcast(FP8X4),

@@ -26,11 +26,13 @@ LIST_ROWS = 16
 SCALE_WINDOW = 1024
 EARLY = 2
 SCATTER_GROUPS = ((0, 1), (1, 2), (2, 4), (4, 6))
-BLOCKS = T // P
 RUN = 4
-PRODUCT_GROUPS = ((0, 2), (2, 4), (4, 5), (5, 6))
-OUT_GROUPS = ((0, 2), (2, 4), (4, 5), (5, 6))
-CODE_STORES = ((0, 512), (512, T))
+BLOCK_EDGES = [0, 128, 256, 384, 512, 640, 768]
+PRODUCT_EDGES = [0, 128, 384, 640, 768]
+OUT_EDGES = [0, 256, 512, 640, 768]
+STORE_EDGES = [0, 128, 256, 384, 512, 640, 768]
+ROUND_FIRST_FROM = 640
+CODE_STORES = [0, 256, 512, 640, 768]
 
 
 def tile_moe_sub_silu_kernel(
@@ -141,7 +143,7 @@ def tile_moe_sub_silu_kernel(
             for e in range(first, last):
                 if e == EARLY:
                     load_expert_pair(4, "early_words")
-                y_by_slot = psum.tile([P, H], F32, name="y_by_slot", tag=f"bank{0 if e < EARLY else e % 4}")
+                y_by_slot = psum.tile([P, H], F32, name="y_by_slot", tag=f"bank{e % 2}")
                 for s in range(PASSES):
                     nc.tensor.matmul_mx(
                         out=y_by_slot[:],
@@ -153,7 +155,7 @@ def tile_moe_sub_silu_kernel(
                         stop=(s == PASSES - 1),
                     )
                 y_gated = keep.tile([P, PACK, P], F32, name="y_gated", tag=f"y_gated{e}")
-                ring_bank = (e + 2) % 4
+                ring_bank = 2 + e % 2
                 pieces = ((0, 1, 4 + e), (1, PACK, ring_bank)) if e < EARLY else ((0, PACK, ring_bank),)
                 for t0, t1, bank in pieces:
                     nc.scalar.activation(
@@ -170,7 +172,7 @@ def tile_moe_sub_silu_kernel(
             for t in range(PACK):
                 nc.vector.tensor_copy(out=neg_dh[t][:].indirect(offsets_of(first, last)), in_=y_rows[:, t, :])
 
-        sig = keep.tile([P, T // RUN, PACK, RUN], F32, name="sig", tag="y_gated1")
+        sig = keep.tile([P, T // RUN, PACK, RUN], F32, name="sig", tag="y_gated5")
         a_in_runs = a_rows[:].rearrange("p t (c j) -> p c t j", j=RUN)
         for piece in range(PACK):
             runs = slice(piece * T // RUN // PACK, (piece + 1) * T // RUN // PACK)
@@ -183,11 +185,10 @@ def tile_moe_sub_silu_kernel(
 
         half_da = keep.tile([P, T // RUN, PACK, RUN], F32, name="half_da")
 
-        def first_products(first, last):
-            tokens = slice(first * P, last * P)
+        def first_products(tokens):
             for t in range(PACK):
                 nc.vector.scalar_tensor_tensor(
-                    out=half_da[:, first * P // RUN : last * P // RUN, t, :],
+                    out=half_da[:, tokens.start // RUN : tokens.stop // RUN, t, :],
                     in0=silu_of_neg_a[:, t, tokens].rearrange("p (c j) -> p c j", j=RUN),
                     scalar=1.0,
                     in1=neg_dh[t][:, tokens].rearrange("p (c j) -> p c j", j=RUN),
@@ -195,64 +196,88 @@ def tile_moe_sub_silu_kernel(
                     op1=ALU.mult,
                 )
 
-        def second_product(block):
-            runs = slice(block * P // RUN, (block + 1) * P // RUN)
-            da_grouped = keep.tile([P, P, PACK], BF16, name=f"da_grouped{block}", align_bytes=64)
+        def quantised_da(tokens):
+            runs = slice(tokens.start // RUN, tokens.stop // RUN)
+            width = tokens.stop - tokens.start
+            da_grouped = keep.tile([P, width, PACK], BF16, name=f"da_grouped{tokens.start}", align_bytes=64)
             nc.vector.tensor_tensor(
                 out=da_grouped[:].rearrange("p (c j) t -> p c t j", j=RUN),
                 in0=half_da[:, runs, :, :],
                 in1=sig[:, runs, :, :],
                 op=ALU.mult,
             )
-            return da_grouped
-
-        def quantise_da(block, da_grouped):
-            da_codes = keep.tile([P, P], U32, name=f"da_codes{block}", align_bytes=64)
-            da_plane = keep.tile([P, P], U8, name=f"da_plane{block}", align_bytes=64)
+            da_codes = keep.tile([P, width], U32, name=f"da_codes{tokens.start}", align_bytes=64)
+            da_plane = keep.tile([P, width], U8, name=f"da_plane{tokens.start}", align_bytes=64)
             nc.vector.quantize_mx(
                 out=da_codes[:].bitcast(FP8X4), scales=da_plane[:], in_=da_grouped[:].rearrange("p c t -> p (c t)")
             )
             return da_codes, da_plane
 
-        da_quantised = []
-        for first, last in PRODUCT_GROUPS:
-            first_products(first, last)
-            for block in range(first, last):
-                da_quantised.append(quantise_da(block, second_product(block)))
+        def blocks_in(lo, hi):
+            return [slice(a0, a1) for a0, a1 in zip(BLOCK_EDGES, BLOCK_EDGES[1:]) if lo <= a0 and a1 <= hi]
+
+        da_quantised = {}
+        for lo, hi in zip(PRODUCT_EDGES, PRODUCT_EDGES[1:]):
+            first_products(slice(lo, hi))
+            for tokens in blocks_in(lo, hi):
+                da_quantised[tokens.start] = quantised_da(tokens)
+
+        def shared_layer(da_codes, da_plane, bank):
+            acc = psum.tile([P, PACK, da_plane.shape[1]], F32, name="acc", tag=f"bank{bank}")
+            for d in range(PACK):
+                nc.tensor.matmul_mx(
+                    out=acc[:, d, :],
+                    lhsT=w1_words[:, d, :].bitcast(FP8X4),
+                    lhsT_scale=w1_plane[:, d, :],
+                    rhs=da_codes.bitcast(FP8X4),
+                    rhs_scale=da_plane,
+                    start=True,
+                    stop=True,
+                )
+            return acc
 
         out_rows_hbm = out_0.rearrange("(p d) t -> p d t", d=PACK)
-        for first, last in OUT_GROUPS:
-            group = slice(first * P, last * P)
-            out_rows = keep.tile([P, PACK, (last - first) * P], F32, name=f"out_rows{first}")
-            out_grouped = keep.tile([P, (last - first) * P, PACK], BF16, name=f"out_grouped{first}", align_bytes=64)
-            for block in range(first, last):
-                da_codes, da_plane = da_quantised[block]
-                cols = slice((block - first) * P, (block - first + 1) * P)
-                acc = psum.tile([P, PACK, P], F32, name="acc", tag=f"bank{block}")
-                for d in range(PACK):
-                    nc.tensor.matmul_mx(
-                        out=acc[:, d, :],
-                        lhsT=w1_words[:, d, :].bitcast(FP8X4),
-                        lhsT_scale=w1_plane[:, d, :],
-                        rhs=da_codes[:].bitcast(FP8X4),
-                        rhs_scale=da_plane[:],
-                        start=True,
-                        stop=True,
-                    )
-                nc.scalar.copy(out=out_grouped[:, cols, :], in_=acc[:].rearrange("p d c -> p c d"))
-                nc.scalar.copy(out=out_rows[:, :, cols], in_=acc[:])
-            nc.sync.dma_start(out=out_rows_hbm[:, :, group], in_=out_rows[:])
-            nc.vector.quantize_mx(
-                out=out_codes[:, group].bitcast(FP8X4),
-                scales=out_plane[:, group],
-                in_=out_grouped[:].rearrange("p c d -> p (c d)"),
-            )
-
         codes_hbm = out_1[0].rearrange("p t d -> p (t d)").bitcast(I32)
-        for lo, hi in CODE_STORES:
-            nc.sync.dma_start(out=codes_hbm[:, lo:hi], in_=out_codes[:, lo:hi].bitcast(I32))
+        out_rows = keep.tile([P, PACK, T], F32, name="out_rows")
+        out_grouped = keep.tile([P, T, PACK], BF16, name="out_grouped", align_bytes=64)
+
+        def since_last(edges, stop):
+            return slice(edges[edges.index(stop) - 1], stop)
+
+        for bank, tokens in enumerate(blocks_in(0, T)):
+            da_codes, da_plane = da_quantised[tokens.start]
+            if tokens.stop < T:
+                acc = shared_layer(da_codes[:], da_plane[:], bank)
+                if tokens.start < ROUND_FIRST_FROM:
+                    nc.scalar.copy(out=out_rows[:, :, tokens], in_=acc[:])
+                    nc.scalar.copy(out=out_grouped[:, tokens, :], in_=acc[:].rearrange("p d c -> p c d"))
+                else:
+                    nc.scalar.copy(out=out_grouped[:, tokens, :], in_=acc[:].rearrange("p d c -> p c d"))
+                    nc.scalar.copy(out=out_rows[:, :, tokens], in_=acc[:])
+            else:
+                halves = (slice(0, P // 2), slice(P // 2, P))
+                accs = [shared_layer(da_codes[:, h], da_plane[:, h], bank + n) for n, h in enumerate(halves)]
+                for n in range(2):
+                    nc.vector.tensor_copy(
+                        out=out_grouped[:, tokens, :][:, halves[n], :], in_=accs[n][:].rearrange("p d c -> p c d")
+                    )
+                    nc.scalar.copy(out=out_rows[:, :, tokens][:, :, halves[1 - n]], in_=accs[1 - n][:])
+            if tokens.stop in STORE_EDGES:
+                group = since_last(STORE_EDGES, tokens.stop)
+                nc.sync.dma_start(out=out_rows_hbm[:, :, group], in_=out_rows[:, :, group])
+            if tokens.stop in OUT_EDGES:
+                group = since_last(OUT_EDGES, tokens.stop)
+                nc.vector.quantize_mx(
+                    out=out_codes[:, group].bitcast(FP8X4),
+                    scales=out_plane[:, group],
+                    in_=out_grouped[:, group, :].rearrange("p c d -> p (c d)"),
+                )
+            if tokens.stop in CODE_STORES:
+                group = since_last(CODE_STORES, tokens.stop)
+                nc.sync.dma_start(out=codes_hbm[:, group], in_=out_codes[:, group].bitcast(I32))
+
         for q in range(4):
-            nc.sync.dma_start(
+            (nc.sync if q % 2 == 0 else nc.scalar).dma_start(
                 out=out_2[0, 4 * q : 4 * q + 4, :].bitcast(I32),
                 in_=out_plane[QUADRANT * q : QUADRANT * q + 4, :].bitcast(I32),
             )

@@ -31,7 +31,7 @@ BLOCK_EDGES = [0, 128, 256, 384, 512, 640, 768]
 PRODUCT_EDGES = [0, 128, 384, 640, 768]
 OUT_EDGES = [0, 256, 512, 640, 768]
 STORE_EDGES = [0, 128, 256, 384, 512, 640, 768]
-ROUND_FIRST_FROM = 640
+ROUND_FIRST_FROM = 512
 CODE_STORES = [0, 256, 512, 640, 768]
 
 
@@ -156,7 +156,7 @@ def tile_moe_sub_silu_kernel(
                     )
                 y_gated = keep.tile([P, PACK, P], F32, name="y_gated", tag=f"y_gated{e}")
                 ring_bank = 2 + e % 2
-                pieces = ((0, 1, 4 + e), (1, PACK, ring_bank)) if e < EARLY else ((0, PACK, ring_bank),)
+                pieces = ((0, 1, 4 + e), (1, PACK, ring_bank)) if e == 0 else ((0, PACK, ring_bank),)
                 for t0, t1, bank in pieces:
                     nc.scalar.activation(
                         out=y_gated[:, t0:t1, :],
@@ -168,7 +168,8 @@ def tile_moe_sub_silu_kernel(
                     turned = psum.tile([P, t1 - t0, C], F32, name="turned", tag=f"bank{bank}")
                     for t in range(t0, t1):
                         nc.tensor.transpose(turned[:, t - t0, :], y_gated[:, t, :], identity[:])
-                    nc.scalar.copy(out=y_rows[:, t0:t1, (e - first) * C : (e - first + 1) * C], in_=turned[:])
+                    copy = nc.vector.tensor_copy if (e, t0) == (0, 0) else nc.scalar.copy
+                    copy(out=y_rows[:, t0:t1, (e - first) * C : (e - first + 1) * C], in_=turned[:])
             for t in range(PACK):
                 nc.vector.tensor_copy(out=neg_dh[t][:].indirect(offsets_of(first, last)), in_=y_rows[:, t, :])
 
@@ -222,11 +223,11 @@ def tile_moe_sub_silu_kernel(
             for tokens in blocks_in(lo, hi):
                 da_quantised[tokens.start] = quantised_da(tokens)
 
-        def shared_layer(da_codes, da_plane, bank):
-            acc = psum.tile([P, PACK, da_plane.shape[1]], F32, name="acc", tag=f"bank{bank}")
-            for d in range(PACK):
+        def shared_layer(da_codes, da_plane, bank, rows=slice(0, PACK)):
+            acc = psum.tile([P, rows.stop - rows.start, P], F32, name="acc", tag=f"bank{bank}")
+            for d in range(rows.start, rows.stop):
                 nc.tensor.matmul_mx(
-                    out=acc[:, d, :],
+                    out=acc[:, d - rows.start, :],
                     lhsT=w1_words[:, d, :].bitcast(FP8X4),
                     lhsT_scale=w1_plane[:, d, :],
                     rhs=da_codes.bitcast(FP8X4),
@@ -252,16 +253,20 @@ def tile_moe_sub_silu_kernel(
                     nc.scalar.copy(out=out_rows[:, :, tokens], in_=acc[:])
                     nc.scalar.copy(out=out_grouped[:, tokens, :], in_=acc[:].rearrange("p d c -> p c d"))
                 else:
-                    nc.scalar.copy(out=out_grouped[:, tokens, :], in_=acc[:].rearrange("p d c -> p c d"))
                     nc.scalar.copy(out=out_rows[:, :, tokens], in_=acc[:])
-            else:
-                halves = (slice(0, P // 2), slice(P // 2, P))
-                accs = [shared_layer(da_codes[:, h], da_plane[:, h], bank + n) for n, h in enumerate(halves)]
-                for n in range(2):
                     nc.vector.tensor_copy(
-                        out=out_grouped[:, tokens, :][:, halves[n], :], in_=accs[n][:].rearrange("p d c -> p c d")
+                        out=out_grouped[:, tokens, :].rearrange("p (c j) d -> p c d j", j=RUN),
+                        in_=out_rows[:, :, tokens].rearrange("p d (c j) -> p c d j", j=RUN),
                     )
-                    nc.scalar.copy(out=out_rows[:, :, tokens][:, :, halves[1 - n]], in_=accs[1 - n][:])
+            else:
+                for half in range(2):
+                    rows = slice(2 * half, 2 * half + 2)
+                    acc = shared_layer(da_codes[:], da_plane[:], bank + half, rows)
+                    nc.scalar.copy(out=out_rows[:, rows, tokens], in_=acc[:])
+                nc.vector.tensor_copy(
+                    out=out_grouped[:, tokens, :].rearrange("p (c j) d -> p c d j", j=RUN),
+                    in_=out_rows[:, :, tokens].rearrange("p d (c j) -> p c d j", j=RUN),
+                )
             if tokens.stop in STORE_EDGES:
                 group = since_last(STORE_EDGES, tokens.stop)
                 nc.sync.dma_start(out=out_rows_hbm[:, :, group], in_=out_rows[:, :, group])

@@ -26,7 +26,7 @@ LIST_ROWS = 16
 SCALE_WINDOW = 1024
 EARLY = 2
 SCATTER_GROUPS = ((0, 1), (1, 2), (2, 4), (4, 6))
-RUN = 4
+RUN = 2
 BLOCK_EDGES = [0, 128, 256, 384, 512, 640, 768]
 PRODUCT_EDGES = [0, 128, 384, 640, 768]
 OUT_EDGES = [0, 256, 512, 640, 768]
@@ -124,16 +124,12 @@ def tile_moe_sub_silu_kernel(
                 for e in range(first, last):
                     slot_words[e, s] = gathered[:, s, (e - first) * C : (e - first + 1) * C]
 
-        w1_words_raw = keep.tile([P, K], I32, name="w1_words_raw", tag="gate_rows", align_bytes=64)
-        nc.sync.dma_start(out=w1_words_raw[:], in_=w1t_words[0].rearrange("p k d -> p (k d)").bitcast(I32))
         load_scale_planes(w1_plane_raw, w1t_scales)
         load_expert_pair(2, "token_scales")
         load_scale_planes(w2_planes_late, w2_scale_rows[EARLY * PASSES : E * PASSES])
         a_rows = keep.tile([P, PACK, T], F32, name="a_rows", tag="token_words", align_bytes=64)
         nc.sync.dma_start(out=a_rows[:], in_=a.rearrange("(p t) c -> p t c", t=PACK))
 
-        w1_words = keep.tile([P, PACK, P], I32, name="w1_words", align_bytes=64)
-        nc.vector.tensor_copy(out=w1_words[:], in_=w1_words_raw[:].rearrange("p (m d) -> p d m", d=PACK))
         w1_plane = keep.tile([P, PACK, P], U8, name="w1_plane", align_bytes=64)
         nc.vector.tensor_copy(out=w1_plane[:], in_=w1_plane_raw[:, 0, :].rearrange("p (m d) -> p d m", d=PACK))
 
@@ -173,38 +169,40 @@ def tile_moe_sub_silu_kernel(
             for t in range(PACK):
                 nc.vector.tensor_copy(out=neg_dh[t][:].indirect(offsets_of(first, last)), in_=y_rows[:, t, :])
 
-        sig = keep.tile([P, T // RUN, PACK, RUN], F32, name="sig", tag="y_gated5")
-        a_in_runs = a_rows[:].rearrange("p t (c j) -> p c t j", j=RUN)
-        for piece in range(PACK):
-            runs = slice(piece * T // RUN // PACK, (piece + 1) * T // RUN // PACK)
-            nc.scalar.activation(out=sig[:, runs, :, :], in_=a_in_runs[:, runs, :, :], func=ACT.Sigmoid)
+        w1_words_raw = keep.tile([P, K], I32, name="w1_words_raw", tag="late_words", align_bytes=64)
+        nc.sync.dma_start(out=w1_words_raw[:], in_=w1t_words[0].rearrange("p k d -> p (k d)").bitcast(I32))
+        w1_words = keep.tile([P, PACK, P], U32, name="w1_words", align_bytes=64)
+        nc.scalar.copy(out=w1_words[:], in_=w1_words_raw[:].bitcast(U32).rearrange("p (m d) -> p d m", d=PACK))
+
+        sig = keep.tile([P, PACK, T], F32, name="sig", tag="y_gated5")
+        for t in range(PACK):
+            nc.scalar.activation(out=sig[:, t, :], in_=a_rows[:, t, :], func=ACT.Sigmoid)
         silu_of_neg_a = a_rows
         nc.scalar.activation(out=silu_of_neg_a[:], in_=a_rows[:], func=ACT.Silu, scale=-1.0)
 
         out_codes = keep.tile([P, T], U32, name="out_codes", align_bytes=64)
         out_plane = keep.tile([P, T], U8, name="out_plane", align_bytes=64)
 
-        half_da = keep.tile([P, T // RUN, PACK, RUN], F32, name="half_da")
+        half_da = keep.tile([P, PACK, T], F32, name="half_da")
 
         def first_products(tokens):
             for t in range(PACK):
                 nc.vector.scalar_tensor_tensor(
-                    out=half_da[:, tokens.start // RUN : tokens.stop // RUN, t, :],
-                    in0=silu_of_neg_a[:, t, tokens].rearrange("p (c j) -> p c j", j=RUN),
+                    out=half_da[:, t, tokens],
+                    in0=silu_of_neg_a[:, t, tokens],
                     scalar=1.0,
-                    in1=neg_dh[t][:, tokens].rearrange("p (c j) -> p c j", j=RUN),
+                    in1=neg_dh[t][:, tokens],
                     op0=ALU.subtract,
                     op1=ALU.mult,
                 )
 
         def quantised_da(tokens):
-            runs = slice(tokens.start // RUN, tokens.stop // RUN)
             width = tokens.stop - tokens.start
             da_grouped = keep.tile([P, width, PACK], BF16, name=f"da_grouped{tokens.start}", align_bytes=64)
             nc.vector.tensor_tensor(
                 out=da_grouped[:].rearrange("p (c j) t -> p c t j", j=RUN),
-                in0=half_da[:, runs, :, :],
-                in1=sig[:, runs, :, :],
+                in0=half_da[:, :, tokens].rearrange("p t (c j) -> p c t j", j=RUN),
+                in1=sig[:, :, tokens].rearrange("p t (c j) -> p c t j", j=RUN),
                 op=ALU.mult,
             )
             da_codes = keep.tile([P, width], U32, name=f"da_codes{tokens.start}", align_bytes=64)

@@ -23,16 +23,16 @@ PASSES = N // (P * PACK)
 QUADRANT = 32
 SCALE_ROWS = 16
 LIST_ROWS = 16
-SCALE_WINDOW = 1024
+SCALE_WINDOW = T
 EARLY = 2
-SCATTER_GROUPS = ((0, 1), (1, 2), (2, 4), (4, 6))
-RUN = 2
+SCATTER_GROUPS = ((0, 1), (1, 2), (2, 3), (3, 6))
+RUN = 4
 BLOCK_EDGES = [0, 128, 256, 384, 512, 640, 768]
 PRODUCT_EDGES = [0, 128, 384, 640, 768]
-OUT_EDGES = [0, 256, 512, 640, 768]
+OUT_EDGES = [0, 256, 512, 768]
 STORE_EDGES = [0, 128, 256, 384, 512, 640, 768]
 ROUND_FIRST_FROM = 512
-CODE_STORES = [0, 256, 512, 640, 768]
+CODE_STORES = [0, 512, 768]
 
 
 def tile_moe_sub_silu_kernel(
@@ -41,13 +41,14 @@ def tile_moe_sub_silu_kernel(
     nc = tc.nc
     with ExitStack() as ctx:
         keep = ctx.enter_context(tc.tile_pool(name="keep", bufs=1))
+        head = ctx.enter_context(tc.tile_pool(name="head", bufs=1))
         psum = ctx.enter_context(tc.psum_pool(name="psum", bufs=1))
 
         def offsets_of(first, last):
             return offsets[:, first * C // LIST_ROWS : last * C // LIST_ROWS]
 
-        def load_scale_planes(planes, rows):
-            for r in range(4):
+        def load_scale_planes(planes, rows, which=range(4)):
+            for r in which:
                 nc.sync.dma_start(
                     out=planes[r:P:QUADRANT, :, :].bitcast(I32),
                     in_=rows[:, r:SCALE_ROWS:4, :].rearrange("g q n -> q g n").bitcast(I32),
@@ -56,19 +57,13 @@ def tile_moe_sub_silu_kernel(
         offsets = keep.tile([P, E * C // LIST_ROWS], U16, name="offsets")
         nc.sync.dma_start(offsets[:], offs)
 
-        token_scales = keep.tile([P, SCALE_WINDOW], U8, name="token_scales", tag="token_scales", align_bytes=64)
+        token_scales = head.tile([P, SCALE_WINDOW], U8, name="token_scales", offset=1664, align_bytes=64)
         nc.gpsimd.memset(token_scales[:].bitcast(I32), 0)
         for q in range(4):
             nc.sync.dma_start(
                 out=token_scales[QUADRANT * q : QUADRANT * q + 4 * PASSES, 0:T].bitcast(I32),
                 in_=dy_scales[:, 4 * q : 4 * q + 4, :].bitcast(I32),
             )
-        token_words = keep.tile([P, PASSES, T], I32, name="token_words", tag="token_words", align_bytes=64)
-        nc.sync.dma_start(out=token_words[:], in_=dy_words.rearrange("s p t d -> p s (t d)").bitcast(I32))
-
-        gate_rows = keep.tile([P, C], F32, name="gate_rows", tag="gate_rows", align_bytes=64)
-        nc.sync.dma_start(out=gate_rows[:], in_=gate.rearrange("p (e u) -> (p e) u", u=C)[0:P, :])
-
         warm = keep.tile([P, 8], F32, name="warm", tag="warm", align_bytes=64)
         nc.gpsimd.memset(warm[:], 0.0)
         nc.scalar.activation(out=warm[:, 0:1], in_=warm[:, 1:2], func=ACT.Sigmoid)
@@ -84,67 +79,85 @@ def tile_moe_sub_silu_kernel(
         nc.vector.memset(w1_plane_raw[:].rearrange("p g k -> p (g k)").bitcast(I32), 0)
         w2_words = {}
 
-        def load_expert_pair(first, tag):
-            pair = keep.tile([P, 2 * PASSES, 2 * H], U8, name=f"w2_words{first}", tag=tag, align_bytes=64)
+        def load_experts(first, last, pool, **place):
+            count = (last - first) * PASSES
+            words = pool.tile([P, count, 2 * H], U8, name=f"w2_words{first}", align_bytes=64, **place)
             nc.sync.dma_start(
-                out=pair[:].bitcast(I32),
-                in_=w2t_words[first : first + 2].rearrange("e s p b -> p (e s) b").bitcast(I32),
+                out=words[:].bitcast(I32),
+                in_=w2t_words[first:last].rearrange("e s p b -> p (e s) b").bitcast(I32),
             )
-            for g in range(2 * PASSES):
-                w2_words[first * PASSES + g] = pair[:, g, :]
+            for g in range(count):
+                w2_words[first * PASSES + g] = words[:, g, :]
 
-        load_scale_planes(w2_planes_early, w2_scale_rows[0 : EARLY * PASSES])
-        load_expert_pair(0, "warm")
+        load_scale_planes(w2_planes_early, w2_scale_rows[0 : EARLY * PASSES], range(2))
+        token_words = keep.tile([P, PASSES, T], I32, name="token_words", tag="token_words", align_bytes=64)
+        nc.sync.dma_start(out=token_words[:], in_=dy_words.rearrange("s p t d -> p s (t d)").bitcast(I32))
+        load_scale_planes(w2_planes_early, w2_scale_rows[0 : EARLY * PASSES], range(2, 4))
+        load_experts(0, 1, keep, tag="warm")
 
         identity = keep.tile([P, P], F32, name="identity")
         make_identity(nc, identity[:])
-        gate_turned = psum.tile([P, C], F32, name="gate_turned", tag="bank7")
-        nc.tensor.transpose(gate_turned[:], gate_rows[:], identity[:])
-        neg_gate = keep.tile([P, E], F32, name="neg_gate")
-        nc.scalar.activation(out=neg_gate[:], in_=gate_turned[:, 0:E], func=ACT.Copy, scale=-1.0)
 
-        slot_scales = keep.tile([P, E * C], U8, name="slot_scales", align_bytes=64)
-        nc.vector.tensor_copy(out=slot_scales[:], in_=token_scales[:].indirect(offsets[:]))
-        slot_scales_second = keep.tile([P, E * C], U8, name="slot_scales_second", align_bytes=64)
-        nc.gpsimd.memset(slot_scales_second[:].bitcast(I32), 0)
-        for q in range(4):
-            nc.sync.dma_start(
-                out=slot_scales_second[QUADRANT * q : QUADRANT * q + 4, :].bitcast(I32),
-                in_=slot_scales[QUADRANT * q + 4 : QUADRANT * q + 8, :].bitcast(I32),
-            )
-        slot_plane = (slot_scales, slot_scales_second)
+        groups = ((0, EARLY, "early"), (EARLY, E, "late"))
+        slot_scales = {}
+        slot_plane = {}
+
+        def move_second_pass(first, last, name):
+            second = keep.tile([P, (last - first) * C], U8, name=f"{name}_scales_second", align_bytes=64)
+            nc.gpsimd.memset(second[:].bitcast(I32), 0)
+            for q in range(4):
+                nc.sync.dma_start(
+                    out=second[QUADRANT * q : QUADRANT * q + 4, :].bitcast(I32),
+                    in_=slot_scales[name][QUADRANT * q + 4 : QUADRANT * q + 8, :].bitcast(I32),
+                )
+            for e in range(first, last):
+                columns = slice((e - first) * C, (e - first + 1) * C)
+                slot_plane[e, 0] = slot_scales[name][:, columns]
+                slot_plane[e, 1] = second[:, columns]
+
+        for first, last, name in groups:
+            slot_scales[name] = keep.tile([P, (last - first) * C], U8, name=f"{name}_scales", align_bytes=64)
+            nc.vector.tensor_copy(out=slot_scales[name][:], in_=token_scales[:].indirect(offsets_of(first, last)))
+        move_second_pass(*groups[0])
+        load_experts(1, 2, head, offset=0)
+        early_gates = head.tile([P, EARLY * C], F32, name="early_gates", offset=2048, align_bytes=64)
+        nc.sync.dma_start(out=early_gates[:], in_=gate[:, 0 : EARLY * C])
+        move_second_pass(*groups[1])
 
         slot_words = {}
-        for first, last, name in ((0, EARLY, "early_words"), (EARLY, E, "late_words")):
-            gathered = keep.tile([P, PASSES, (last - first) * C], U32, name=name, tag=name, align_bytes=64)
+        for first, last in ((0, 1), (1, 2), (2, E)):
             for s in range(PASSES):
+                name = f"words{first}_{s}"
+                gathered = keep.tile([P, (last - first) * C], U32, name=name, tag=name, align_bytes=64)
                 nc.vector.tensor_copy(
-                    out=gathered[:, s, :], in_=token_words[:, s, :].bitcast(U32).indirect(offsets_of(first, last))
+                    out=gathered[:], in_=token_words[:, s, :].bitcast(U32).indirect(offsets_of(first, last))
                 )
                 for e in range(first, last):
-                    slot_words[e, s] = gathered[:, s, (e - first) * C : (e - first + 1) * C]
+                    slot_words[e, s] = gathered[:, (e - first) * C : (e - first + 1) * C]
 
-        load_scale_planes(w1_plane_raw, w1t_scales)
-        load_expert_pair(2, "token_scales")
         load_scale_planes(w2_planes_late, w2_scale_rows[EARLY * PASSES : E * PASSES])
-        a_rows = keep.tile([P, PACK, T], F32, name="a_rows", tag="token_words", align_bytes=64)
-        nc.sync.dma_start(out=a_rows[:], in_=a.rearrange("(p t) c -> p t c", t=PACK))
 
-        w1_plane = keep.tile([P, PACK, P], U8, name="w1_plane", align_bytes=64)
-        nc.vector.tensor_copy(out=w1_plane[:], in_=w1_plane_raw[:, 0, :].rearrange("p (m d) -> p d m", d=PACK))
 
         neg_dh = [keep.tile([P, T], F32, name=f"neg_dh{t}") for t in range(PACK)]
+        rows_of = {}
         for first, last in SCATTER_GROUPS:
             y_rows = keep.tile([P, PACK, (last - first) * C], F32, name=f"y_rows{first}")
+            rows_of[first] = y_rows
             for e in range(first, last):
+                if e == 1:
+                    load_experts(2, 4, keep, tag="words0_0")
+                    late_gates = keep.tile([P, (E - EARLY) * C], F32, name="late_gates", tag="words0_1", align_bytes=64)
+                    nc.sync.dma_start(out=late_gates[:], in_=gate[:, EARLY * C : E * C])
                 if e == EARLY:
-                    load_expert_pair(4, "early_words")
-                y_by_slot = psum.tile([P, H], F32, name="y_by_slot", tag=f"bank{e % 2}")
+                    load_experts(4, 6, keep, tag="words1_0")
+                    a_rows = keep.tile([P, PACK, T], F32, name="a_rows", tag="words1_1", align_bytes=64)
+                    nc.sync.dma_start(out=a_rows[:], in_=a.rearrange("(p t) c -> p t c", t=PACK))
+                y_by_slot = psum.tile([P, H], F32, name="y_by_slot", tag=f"bank{4 if e == 1 else e % 2}")
                 for s in range(PASSES):
                     nc.tensor.matmul_mx(
                         out=y_by_slot[:],
                         lhsT=slot_words[e, s].bitcast(FP8X4),
-                        lhsT_scale=slot_plane[s][:, e * C : (e + 1) * C],
+                        lhsT_scale=slot_plane[e, s],
                         rhs=w2_words[e * PASSES + s].bitcast(FP4X4),
                         rhs_scale=w2_plane[e * PASSES + s],
                         start=(s == 0),
@@ -152,57 +165,72 @@ def tile_moe_sub_silu_kernel(
                     )
                 y_gated = keep.tile([P, PACK, P], F32, name="y_gated", tag=f"y_gated{e}")
                 ring_bank = 2 + e % 2
-                pieces = ((0, 1, 4 + e), (1, PACK, ring_bank)) if e == 0 else ((0, PACK, ring_bank),)
+                pieces = ((0, 1, 4 + e), (1, PACK, ring_bank)) if e < EARLY else ((0, PACK, ring_bank),)
                 for t0, t1, bank in pieces:
                     nc.scalar.activation(
                         out=y_gated[:, t0:t1, :],
                         in_=y_by_slot[:].rearrange("u (m t) -> u t m", t=PACK)[:, t0:t1, :],
                         func=ACT.Copy,
-                        scale=neg_gate[:, e : e + 1],
+                        scale=-1.0,
                     )
                 for t0, t1, bank in pieces:
                     turned = psum.tile([P, t1 - t0, C], F32, name="turned", tag=f"bank{bank}")
                     for t in range(t0, t1):
                         nc.tensor.transpose(turned[:, t - t0, :], y_gated[:, t, :], identity[:])
-                    copy = nc.vector.tensor_copy if (e, t0) == (0, 0) else nc.scalar.copy
-                    copy(out=y_rows[:, t0:t1, (e - first) * C : (e - first + 1) * C], in_=turned[:])
+                    nc.scalar.copy(out=y_rows[:, t0:t1, (e - first) * C : (e - first + 1) * C], in_=turned[:])
             for t in range(PACK):
-                nc.vector.tensor_copy(out=neg_dh[t][:].indirect(offsets_of(first, last)), in_=y_rows[:, t, :])
+                nc.vector.tensor_tensor(
+                    out=neg_dh[t][:].indirect(offsets_of(first, last)),
+                    in0=y_rows[:, t, :],
+                    in1=(
+                        early_gates[:, first * C : last * C]
+                        if first < EARLY
+                        else late_gates[:, (first - EARLY) * C : (last - EARLY) * C]
+                    ),
+                    op=ALU.mult,
+                )
 
-        w1_words_raw = keep.tile([P, K], I32, name="w1_words_raw", tag="late_words", align_bytes=64)
+        w1_words_raw = keep.tile([P, K], I32, name="w1_words_raw", tag="words2_1", align_bytes=64)
         nc.sync.dma_start(out=w1_words_raw[:], in_=w1t_words[0].rearrange("p k d -> p (k d)").bitcast(I32))
         w1_words = keep.tile([P, PACK, P], U32, name="w1_words", align_bytes=64)
         nc.scalar.copy(out=w1_words[:], in_=w1_words_raw[:].bitcast(U32).rearrange("p (m d) -> p d m", d=PACK))
 
-        sig = keep.tile([P, PACK, T], F32, name="sig", tag="y_gated5")
-        for t in range(PACK):
-            nc.scalar.activation(out=sig[:, t, :], in_=a_rows[:, t, :], func=ACT.Sigmoid)
+        load_scale_planes(w1_plane_raw, w1t_scales)
+        w1_plane = keep.tile([P, PACK, P], U8, name="w1_plane", align_bytes=64)
+        nc.vector.tensor_copy(out=w1_plane[:], in_=w1_plane_raw[:, 0, :].rearrange("p (m d) -> p d m", d=PACK))
+
+        sig = keep.tile([P, T // RUN, PACK, RUN], F32, name="sig", tag="y_gated5")
+        a_in_runs = a_rows[:].rearrange("p t (c j) -> p c t j", j=RUN)
+        for piece in range(PACK):
+            runs = slice(piece * T // RUN // PACK, (piece + 1) * T // RUN // PACK)
+            nc.scalar.activation(out=sig[:, runs, :, :], in_=a_in_runs[:, runs, :, :], func=ACT.Sigmoid)
         silu_of_neg_a = a_rows
         nc.scalar.activation(out=silu_of_neg_a[:], in_=a_rows[:], func=ACT.Silu, scale=-1.0)
 
         out_codes = keep.tile([P, T], U32, name="out_codes", align_bytes=64)
         out_plane = keep.tile([P, T], U8, name="out_plane", align_bytes=64)
 
-        half_da = keep.tile([P, PACK, T], F32, name="half_da")
+        half_da = keep.tile([P, T // RUN, PACK, RUN], F32, name="half_da")
 
         def first_products(tokens):
             for t in range(PACK):
                 nc.vector.scalar_tensor_tensor(
-                    out=half_da[:, t, tokens],
-                    in0=silu_of_neg_a[:, t, tokens],
+                    out=half_da[:, tokens.start // RUN : tokens.stop // RUN, t, :],
+                    in0=silu_of_neg_a[:, t, tokens].rearrange("p (c j) -> p c j", j=RUN),
                     scalar=1.0,
-                    in1=neg_dh[t][:, tokens],
+                    in1=neg_dh[t][:, tokens].rearrange("p (c j) -> p c j", j=RUN),
                     op0=ALU.subtract,
                     op1=ALU.mult,
                 )
 
         def quantised_da(tokens):
+            runs = slice(tokens.start // RUN, tokens.stop // RUN)
             width = tokens.stop - tokens.start
             da_grouped = keep.tile([P, width, PACK], BF16, name=f"da_grouped{tokens.start}", align_bytes=64)
             nc.vector.tensor_tensor(
                 out=da_grouped[:].rearrange("p (c j) t -> p c t j", j=RUN),
-                in0=half_da[:, :, tokens].rearrange("p t (c j) -> p c t j", j=RUN),
-                in1=sig[:, :, tokens].rearrange("p t (c j) -> p c t j", j=RUN),
+                in0=half_da[:, runs, :, :],
+                in1=sig[:, runs, :, :],
                 op=ALU.mult,
             )
             da_codes = keep.tile([P, width], U32, name=f"da_codes{tokens.start}", align_bytes=64)

@@ -23,16 +23,16 @@ PASSES = N // (P * PACK)
 QUADRANT = 32
 SCALE_ROWS = 16
 LIST_ROWS = 16
-SCALE_WINDOW = T
+SCALE_WINDOW = 1024
 EARLY = 2
 SCATTER_GROUPS = ((0, 1), (1, 2), (2, 3), (3, 6))
 RUN = 4
 BLOCK_EDGES = [0, 128, 256, 384, 512, 640, 768]
 PRODUCT_EDGES = [0, 128, 384, 640, 768]
-OUT_EDGES = [0, 256, 512, 768]
-STORE_EDGES = [0, 128, 256, 384, 512, 640, 768]
+OUT_EDGES = [0, 256, 512, 640, 768]
+STORE_EDGES = [0, 128, 256, 384, 512, 640]
 ROUND_FIRST_FROM = 512
-CODE_STORES = [0, 512, 768]
+CODE_STORES = [0, 256, 768]
 
 
 def tile_moe_sub_silu_kernel(
@@ -98,7 +98,7 @@ def tile_moe_sub_silu_kernel(
         identity = keep.tile([P, P], F32, name="identity")
         make_identity(nc, identity[:])
 
-        groups = ((0, EARLY, "early"), (EARLY, E, "late"))
+        groups = ((0, 1, "early"), (1, E, "late"))
         slot_scales = {}
         slot_plane = {}
 
@@ -119,9 +119,9 @@ def tile_moe_sub_silu_kernel(
             slot_scales[name] = keep.tile([P, (last - first) * C], U8, name=f"{name}_scales", align_bytes=64)
             nc.vector.tensor_copy(out=slot_scales[name][:], in_=token_scales[:].indirect(offsets_of(first, last)))
         move_second_pass(*groups[0])
-        load_experts(1, 2, head, offset=0)
         early_gates = head.tile([P, EARLY * C], F32, name="early_gates", offset=2048, align_bytes=64)
         nc.sync.dma_start(out=early_gates[:], in_=gate[:, 0 : EARLY * C])
+        load_experts(1, 2, head, offset=0)
         move_second_pass(*groups[1])
 
         slot_words = {}
@@ -285,14 +285,13 @@ def tile_moe_sub_silu_kernel(
                         in_=out_rows[:, :, tokens].rearrange("p d (c j) -> p c d j", j=RUN),
                     )
             else:
+                acc = shared_layer(da_codes[:], da_plane[:], bank)
+                nc.vector.tensor_copy(out=out_grouped[:, tokens, :], in_=acc[:].rearrange("p d c -> p c d"))
                 for half in range(2):
                     rows = slice(2 * half, 2 * half + 2)
-                    acc = shared_layer(da_codes[:], da_plane[:], bank + half, rows)
+                    acc = shared_layer(da_codes[:], da_plane[:], bank + 1 + half, rows)
                     nc.scalar.copy(out=out_rows[:, rows, tokens], in_=acc[:])
-                nc.vector.tensor_copy(
-                    out=out_grouped[:, tokens, :].rearrange("p (c j) d -> p c d j", j=RUN),
-                    in_=out_rows[:, :, tokens].rearrange("p d (c j) -> p c d j", j=RUN),
-                )
+                    nc.sync.dma_start(out=out_rows_hbm[:, rows, tokens], in_=out_rows[:, rows, tokens])
             if tokens.stop in STORE_EDGES:
                 group = since_last(STORE_EDGES, tokens.stop)
                 nc.sync.dma_start(out=out_rows_hbm[:, :, group], in_=out_rows[:, :, group])

@@ -22,17 +22,24 @@ PACK = 4
 PASSES = N // (P * PACK)
 QUADRANT = 32
 SCALE_ROWS = 16
+QUADRANT_ROWS = 4
 LIST_ROWS = 16
 SCALE_WINDOW = 1024
+SCALE_GROUPS = ((0, 1, "early"), (1, E, "late"))
+WORD_GROUPS = ((0, 1), (1, 2), (2, E))
 EARLY = 2
-SCATTER_GROUPS = ((0, 1), (1, 2), (2, 3), (3, 6))
+SCATTER_GROUPS = ((0, 1), (1, 2), (2, 3), (3, 4), (4, 6))
+EXPERT_1_AT = 0
+EARLY_GATES_AT = PASSES * 2 * H
+TOKEN_SCALES_AT = EARLY_GATES_AT - 384
+FIRST_SLICE_BANK = 4
+ACTIVATIONS_BEHIND = 3
 RUN = 4
-BLOCK_EDGES = [0, 128, 256, 384, 512, 640, 768]
+BLOCK = 128
 PRODUCT_EDGES = [0, 128, 384, 640, 768]
-OUT_EDGES = [0, 256, 512, 640, 768]
-STORE_EDGES = [0, 128, 256, 384, 512, 640]
-ROUND_FIRST_FROM = 512
-CODE_STORES = [0, 256, 768]
+PLANE_EDGES = [0, 256, 512, 640, 768]
+CODE_STORE_EDGES = [0, 256, 768]
+VECTOR_ROUNDS_FROM = 512
 
 
 def tile_moe_sub_silu_kernel(
@@ -47,23 +54,24 @@ def tile_moe_sub_silu_kernel(
         def offsets_of(first, last):
             return offsets[:, first * C // LIST_ROWS : last * C // LIST_ROWS]
 
-        def load_scale_planes(planes, rows, which=range(4)):
+        def load_scale_planes(planes, rows, which=range(QUADRANT_ROWS)):
             for r in which:
                 nc.sync.dma_start(
                     out=planes[r:P:QUADRANT, :, :].bitcast(I32),
-                    in_=rows[:, r:SCALE_ROWS:4, :].rearrange("g q n -> q g n").bitcast(I32),
+                    in_=rows[:, r:SCALE_ROWS:QUADRANT_ROWS, :].rearrange("g q n -> q g n").bitcast(I32),
                 )
 
         offsets = keep.tile([P, E * C // LIST_ROWS], U16, name="offsets")
         nc.sync.dma_start(offsets[:], offs)
 
-        token_scales = head.tile([P, SCALE_WINDOW], U8, name="token_scales", offset=1664, align_bytes=64)
+        token_scales = head.tile([P, SCALE_WINDOW], U8, name="token_scales", offset=TOKEN_SCALES_AT, align_bytes=64)
         nc.gpsimd.memset(token_scales[:].bitcast(I32), 0)
-        for q in range(4):
+        for q in range(P // QUADRANT):
             nc.sync.dma_start(
-                out=token_scales[QUADRANT * q : QUADRANT * q + 4 * PASSES, 0:T].bitcast(I32),
-                in_=dy_scales[:, 4 * q : 4 * q + 4, :].bitcast(I32),
+                out=token_scales[QUADRANT * q : QUADRANT * q + QUADRANT_ROWS * PASSES, 0:T].bitcast(I32),
+                in_=dy_scales[:, QUADRANT_ROWS * q : QUADRANT_ROWS * (q + 1), :].bitcast(I32),
             )
+
         warm = keep.tile([P, 8], F32, name="warm", tag="warm", align_bytes=64)
         nc.gpsimd.memset(warm[:], 0.0)
         nc.scalar.activation(out=warm[:, 0:1], in_=warm[:, 1:2], func=ACT.Sigmoid)
@@ -90,42 +98,41 @@ def tile_moe_sub_silu_kernel(
                 w2_words[first * PASSES + g] = words[:, g, :]
 
         load_scale_planes(w2_planes_early, w2_scale_rows[0 : EARLY * PASSES], range(2))
-        token_words = keep.tile([P, PASSES, T], I32, name="token_words", tag="token_words", align_bytes=64)
+        token_words = keep.tile([P, PASSES, T], I32, name="token_words", align_bytes=64)
         nc.sync.dma_start(out=token_words[:], in_=dy_words.rearrange("s p t d -> p s (t d)").bitcast(I32))
-        load_scale_planes(w2_planes_early, w2_scale_rows[0 : EARLY * PASSES], range(2, 4))
+        load_scale_planes(w2_planes_early, w2_scale_rows[0 : EARLY * PASSES], range(2, QUADRANT_ROWS))
         load_experts(0, 1, keep, tag="warm")
 
         identity = keep.tile([P, P], F32, name="identity")
         make_identity(nc, identity[:])
 
-        groups = ((0, 1, "early"), (1, E, "late"))
         slot_scales = {}
         slot_plane = {}
 
         def move_second_pass(first, last, name):
             second = keep.tile([P, (last - first) * C], U8, name=f"{name}_scales_second", align_bytes=64)
             nc.gpsimd.memset(second[:].bitcast(I32), 0)
-            for q in range(4):
+            for base in range(0, P, QUADRANT):
                 nc.sync.dma_start(
-                    out=second[QUADRANT * q : QUADRANT * q + 4, :].bitcast(I32),
-                    in_=slot_scales[name][QUADRANT * q + 4 : QUADRANT * q + 8, :].bitcast(I32),
+                    out=second[base : base + QUADRANT_ROWS, :].bitcast(I32),
+                    in_=slot_scales[name][base + QUADRANT_ROWS : base + 2 * QUADRANT_ROWS, :].bitcast(I32),
                 )
             for e in range(first, last):
                 columns = slice((e - first) * C, (e - first + 1) * C)
                 slot_plane[e, 0] = slot_scales[name][:, columns]
                 slot_plane[e, 1] = second[:, columns]
 
-        for first, last, name in groups:
+        for first, last, name in SCALE_GROUPS:
             slot_scales[name] = keep.tile([P, (last - first) * C], U8, name=f"{name}_scales", align_bytes=64)
             nc.vector.tensor_copy(out=slot_scales[name][:], in_=token_scales[:].indirect(offsets_of(first, last)))
-        move_second_pass(*groups[0])
-        early_gates = head.tile([P, EARLY * C], F32, name="early_gates", offset=2048, align_bytes=64)
+        move_second_pass(*SCALE_GROUPS[0])
+        early_gates = head.tile([P, EARLY * C], F32, name="early_gates", offset=EARLY_GATES_AT, align_bytes=64)
         nc.sync.dma_start(out=early_gates[:], in_=gate[:, 0 : EARLY * C])
-        load_experts(1, 2, head, offset=0)
-        move_second_pass(*groups[1])
+        load_experts(1, 2, head, offset=EXPERT_1_AT)
+        move_second_pass(*SCALE_GROUPS[1])
 
         slot_words = {}
-        for first, last in ((0, 1), (1, 2), (2, E)):
+        for first, last in WORD_GROUPS:
             for s in range(PASSES):
                 name = f"words{first}_{s}"
                 gathered = keep.tile([P, (last - first) * C], U32, name=name, tag=name, align_bytes=64)
@@ -137,22 +144,20 @@ def tile_moe_sub_silu_kernel(
 
         load_scale_planes(w2_planes_late, w2_scale_rows[EARLY * PASSES : E * PASSES])
 
-
         neg_dh = [keep.tile([P, T], F32, name=f"neg_dh{t}") for t in range(PACK)]
-        rows_of = {}
         for first, last in SCATTER_GROUPS:
             y_rows = keep.tile([P, PACK, (last - first) * C], F32, name=f"y_rows{first}")
-            rows_of[first] = y_rows
             for e in range(first, last):
                 if e == 1:
                     load_experts(2, 4, keep, tag="words0_0")
                     late_gates = keep.tile([P, (E - EARLY) * C], F32, name="late_gates", tag="words0_1", align_bytes=64)
                     nc.sync.dma_start(out=late_gates[:], in_=gate[:, EARLY * C : E * C])
-                if e == EARLY:
+                if e == 2:
                     load_experts(4, 6, keep, tag="words1_0")
                     a_rows = keep.tile([P, PACK, T], F32, name="a_rows", tag="words1_1", align_bytes=64)
                     nc.sync.dma_start(out=a_rows[:], in_=a.rearrange("(p t) c -> p t c", t=PACK))
-                y_by_slot = psum.tile([P, H], F32, name="y_by_slot", tag=f"bank{4 if e == 1 else e % 2}")
+                product_bank = FIRST_SLICE_BANK if e == 1 else e % 2
+                y_by_slot = psum.tile([P, H], F32, name="y_by_slot", tag=f"bank{product_bank}")
                 for s in range(PASSES):
                     nc.tensor.matmul_mx(
                         out=y_by_slot[:],
@@ -163,12 +168,15 @@ def tile_moe_sub_silu_kernel(
                         start=(s == 0),
                         stop=(s == PASSES - 1),
                     )
-                y_gated = keep.tile([P, PACK, P], F32, name="y_gated", tag=f"y_gated{e}")
+                y_dealt = keep.tile([P, PACK, P], F32, name="y_dealt", tag=f"y_dealt{e}")
                 ring_bank = 2 + e % 2
-                pieces = ((0, 1, 4 + e), (1, PACK, ring_bank)) if e < EARLY else ((0, PACK, ring_bank),)
+                if e < EARLY:
+                    pieces = ((0, 1, FIRST_SLICE_BANK + e), (1, PACK, ring_bank))
+                else:
+                    pieces = ((0, PACK, ring_bank),)
                 for t0, t1, bank in pieces:
                     nc.scalar.activation(
-                        out=y_gated[:, t0:t1, :],
+                        out=y_dealt[:, t0:t1, :],
                         in_=y_by_slot[:].rearrange("u (m t) -> u t m", t=PACK)[:, t0:t1, :],
                         func=ACT.Copy,
                         scale=-1.0,
@@ -176,18 +184,15 @@ def tile_moe_sub_silu_kernel(
                 for t0, t1, bank in pieces:
                     turned = psum.tile([P, t1 - t0, C], F32, name="turned", tag=f"bank{bank}")
                     for t in range(t0, t1):
-                        nc.tensor.transpose(turned[:, t - t0, :], y_gated[:, t, :], identity[:])
+                        nc.tensor.transpose(turned[:, t - t0, :], y_dealt[:, t, :], identity[:])
                     nc.scalar.copy(out=y_rows[:, t0:t1, (e - first) * C : (e - first + 1) * C], in_=turned[:])
+            if first < EARLY:
+                gates = early_gates[:, first * C : last * C]
+            else:
+                gates = late_gates[:, (first - EARLY) * C : (last - EARLY) * C]
             for t in range(PACK):
                 nc.vector.tensor_tensor(
-                    out=neg_dh[t][:].indirect(offsets_of(first, last)),
-                    in0=y_rows[:, t, :],
-                    in1=(
-                        early_gates[:, first * C : last * C]
-                        if first < EARLY
-                        else late_gates[:, (first - EARLY) * C : (last - EARLY) * C]
-                    ),
-                    op=ALU.mult,
+                    out=neg_dh[t][:].indirect(offsets_of(first, last)), in0=y_rows[:, t, :], in1=gates, op=ALU.mult
                 )
 
         w1_words_raw = keep.tile([P, K], I32, name="w1_words_raw", tag="words2_1", align_bytes=64)
@@ -199,7 +204,7 @@ def tile_moe_sub_silu_kernel(
         w1_plane = keep.tile([P, PACK, P], U8, name="w1_plane", align_bytes=64)
         nc.vector.tensor_copy(out=w1_plane[:], in_=w1_plane_raw[:, 0, :].rearrange("p (m d) -> p d m", d=PACK))
 
-        sig = keep.tile([P, T // RUN, PACK, RUN], F32, name="sig", tag="y_gated5")
+        sig = keep.tile([P, T // RUN, PACK, RUN], F32, name="sig", tag=f"y_dealt{ACTIVATIONS_BEHIND}")
         a_in_runs = a_rows[:].rearrange("p t (c j) -> p c t j", j=RUN)
         for piece in range(PACK):
             runs = slice(piece * T // RUN // PACK, (piece + 1) * T // RUN // PACK)
@@ -241,7 +246,7 @@ def tile_moe_sub_silu_kernel(
             return da_codes, da_plane
 
         def blocks_in(lo, hi):
-            return [slice(a0, a1) for a0, a1 in zip(BLOCK_EDGES, BLOCK_EDGES[1:]) if lo <= a0 and a1 <= hi]
+            return [slice(start, start + BLOCK) for start in range(lo, hi, BLOCK)]
 
         da_quantised = {}
         for lo, hi in zip(PRODUCT_EDGES, PRODUCT_EDGES[1:]):
@@ -250,7 +255,7 @@ def tile_moe_sub_silu_kernel(
                 da_quantised[tokens.start] = quantised_da(tokens)
 
         def shared_layer(da_codes, da_plane, bank, rows=slice(0, PACK)):
-            acc = psum.tile([P, rows.stop - rows.start, P], F32, name="acc", tag=f"bank{bank}")
+            acc = psum.tile([P, rows.stop - rows.start, BLOCK], F32, name="acc", tag=f"bank{bank}")
             for d in range(rows.start, rows.stop):
                 nc.tensor.matmul_mx(
                     out=acc[:, d - rows.start, :],
@@ -273,41 +278,37 @@ def tile_moe_sub_silu_kernel(
 
         for bank, tokens in enumerate(blocks_in(0, T)):
             da_codes, da_plane = da_quantised[tokens.start]
+            acc = shared_layer(da_codes[:], da_plane[:], bank)
             if tokens.stop < T:
-                acc = shared_layer(da_codes[:], da_plane[:], bank)
-                if tokens.start < ROUND_FIRST_FROM:
-                    nc.scalar.copy(out=out_rows[:, :, tokens], in_=acc[:])
+                nc.scalar.copy(out=out_rows[:, :, tokens], in_=acc[:])
+                if tokens.start < VECTOR_ROUNDS_FROM:
                     nc.scalar.copy(out=out_grouped[:, tokens, :], in_=acc[:].rearrange("p d c -> p c d"))
                 else:
-                    nc.scalar.copy(out=out_rows[:, :, tokens], in_=acc[:])
                     nc.vector.tensor_copy(
                         out=out_grouped[:, tokens, :].rearrange("p (c j) d -> p c d j", j=RUN),
                         in_=out_rows[:, :, tokens].rearrange("p d (c j) -> p c d j", j=RUN),
                     )
+                nc.sync.dma_start(out=out_rows_hbm[:, :, tokens], in_=out_rows[:, :, tokens])
             else:
-                acc = shared_layer(da_codes[:], da_plane[:], bank)
                 nc.vector.tensor_copy(out=out_grouped[:, tokens, :], in_=acc[:].rearrange("p d c -> p c d"))
                 for half in range(2):
                     rows = slice(2 * half, 2 * half + 2)
-                    acc = shared_layer(da_codes[:], da_plane[:], bank + 1 + half, rows)
-                    nc.scalar.copy(out=out_rows[:, rows, tokens], in_=acc[:])
+                    acc_again = shared_layer(da_codes[:], da_plane[:], bank + 1 + half, rows)
+                    nc.scalar.copy(out=out_rows[:, rows, tokens], in_=acc_again[:])
                     nc.sync.dma_start(out=out_rows_hbm[:, rows, tokens], in_=out_rows[:, rows, tokens])
-            if tokens.stop in STORE_EDGES:
-                group = since_last(STORE_EDGES, tokens.stop)
-                nc.sync.dma_start(out=out_rows_hbm[:, :, group], in_=out_rows[:, :, group])
-            if tokens.stop in OUT_EDGES:
-                group = since_last(OUT_EDGES, tokens.stop)
+            if tokens.stop in PLANE_EDGES:
+                group = since_last(PLANE_EDGES, tokens.stop)
                 nc.vector.quantize_mx(
                     out=out_codes[:, group].bitcast(FP8X4),
                     scales=out_plane[:, group],
                     in_=out_grouped[:, group, :].rearrange("p c d -> p (c d)"),
                 )
-            if tokens.stop in CODE_STORES:
-                group = since_last(CODE_STORES, tokens.stop)
+            if tokens.stop in CODE_STORE_EDGES:
+                group = since_last(CODE_STORE_EDGES, tokens.stop)
                 nc.sync.dma_start(out=codes_hbm[:, group], in_=out_codes[:, group].bitcast(I32))
 
-        for q in range(4):
+        for q in range(P // QUADRANT):
             (nc.sync if q % 2 == 0 else nc.scalar).dma_start(
-                out=out_2[0, 4 * q : 4 * q + 4, :].bitcast(I32),
-                in_=out_plane[QUADRANT * q : QUADRANT * q + 4, :].bitcast(I32),
+                out=out_2[0, QUADRANT_ROWS * q : QUADRANT_ROWS * (q + 1), :].bitcast(I32),
+                in_=out_plane[QUADRANT * q : QUADRANT * q + QUADRANT_ROWS, :].bitcast(I32),
             )

@@ -26,9 +26,11 @@ QUADRANT_ROWS = 4
 LIST_ROWS = 16
 SCALE_WINDOW = 1024
 SCALE_GROUPS = ((0, 1, "early"), (1, E, "late"))
-WORD_GROUPS = ((0, 1), (1, 2), (2, E))
+WORD_GROUPS = ((0, 1), (1, 3), (3, E))
 EARLY = 2
-SCATTER_GROUPS = ((0, 1), (1, 2), (2, 3), (3, 4), (4, 6))
+SCATTER_GROUPS = ((0, 2), (2, 4), (4, 6))
+VECTOR_SLICES = 2
+SCALAR_GROUPS = ((3, 6), (0, 3))
 EXPERT_1_AT = 0
 EARLY_GATES_AT = PASSES * 2 * H
 TOKEN_SCALES_AT = EARLY_GATES_AT - 384
@@ -48,7 +50,6 @@ def tile_moe_sub_silu_kernel(
     nc = tc.nc
     with ExitStack() as ctx:
         keep = ctx.enter_context(tc.tile_pool(name="keep", bufs=1))
-        head = ctx.enter_context(tc.tile_pool(name="head", bufs=1))
         psum = ctx.enter_context(tc.psum_pool(name="psum", bufs=1))
 
         def offsets_of(first, last):
@@ -64,32 +65,21 @@ def tile_moe_sub_silu_kernel(
         offsets = keep.tile([P, E * C // LIST_ROWS], U16, name="offsets")
         nc.sync.dma_start(offsets[:], offs)
 
-        token_scales = head.tile([P, SCALE_WINDOW], U8, name="token_scales", offset=TOKEN_SCALES_AT, align_bytes=64)
-        nc.gpsimd.memset(token_scales[:].bitcast(I32), 0)
-        for q in range(P // QUADRANT):
-            nc.sync.dma_start(
-                out=token_scales[QUADRANT * q : QUADRANT * q + QUADRANT_ROWS * PASSES, 0:T].bitcast(I32),
-                in_=dy_scales[:, QUADRANT_ROWS * q : QUADRANT_ROWS * (q + 1), :].bitcast(I32),
-            )
+        token_scales = keep.tile([P, PASSES, T], U8, name="token_scales", align_bytes=64)
+        nc.gpsimd.memset(token_scales[:].rearrange("p s t -> p (s t)").bitcast(I32), 0)
+        load_scale_planes(token_scales, dy_scales)
 
         warm = keep.tile([P, 8], F32, name="warm", tag="warm", align_bytes=64)
         nc.gpsimd.memset(warm[:], 0.0)
         nc.scalar.activation(out=warm[:, 0:1], in_=warm[:, 1:2], func=ACT.Sigmoid)
 
         w2_scale_rows = w2t_scales.rearrange("e s b i -> (e s) b i")
-        w2_planes_early = keep.tile([P, EARLY * PASSES, H], U8, name="w2_planes_early", align_bytes=64)
-        nc.vector.memset(w2_planes_early[:].rearrange("p g i -> p (g i)").bitcast(I32), 0)
-        w2_planes_late = keep.tile([P, (E - EARLY) * PASSES, H], U8, name="w2_planes_late", align_bytes=64)
-        nc.vector.memset(w2_planes_late[:].rearrange("p g i -> p (g i)").bitcast(I32), 0)
-        w2_plane = [w2_planes_early[:, g, :] for g in range(EARLY * PASSES)]
-        w2_plane.extend(w2_planes_late[:, g, :] for g in range((E - EARLY) * PASSES))
-        w1_plane_raw = keep.tile([P, 1, K], U8, name="w1_plane_raw", align_bytes=64)
-        nc.vector.memset(w1_plane_raw[:].rearrange("p g k -> p (g k)").bitcast(I32), 0)
+        w2_planes = keep.tile([P, E * PASSES, H], U8, name="w2_planes", align_bytes=64)
         w2_words = {}
 
-        def load_experts(first, last, pool, **place):
+        def load_experts(first, last, **place):
             count = (last - first) * PASSES
-            words = pool.tile([P, count, 2 * H], U8, name=f"w2_words{first}", align_bytes=64, **place)
+            words = keep.tile([P, count, 2 * H], U8, name=f"w2_words{first}", align_bytes=64, **place)
             nc.sync.dma_start(
                 out=words[:].bitcast(I32),
                 in_=w2t_words[first:last].rearrange("e s p b -> p (e s) b").bitcast(I32),
@@ -97,42 +87,36 @@ def tile_moe_sub_silu_kernel(
             for g in range(count):
                 w2_words[first * PASSES + g] = words[:, g, :]
 
-        load_scale_planes(w2_planes_early, w2_scale_rows[0 : EARLY * PASSES], range(2))
+        load_scale_planes(w2_planes, w2_scale_rows, range(2))
         token_words = keep.tile([P, PASSES, T], I32, name="token_words", align_bytes=64)
         nc.sync.dma_start(out=token_words[:], in_=dy_words.rearrange("s p t d -> p s (t d)").bitcast(I32))
-        load_scale_planes(w2_planes_early, w2_scale_rows[0 : EARLY * PASSES], range(2, QUADRANT_ROWS))
-        load_experts(0, 1, keep, tag="warm")
+        load_scale_planes(w2_planes, w2_scale_rows, range(2, QUADRANT_ROWS))
+        load_experts(0, 1)
+        gate_columns = keep.tile([P, E], F32, name="gate_columns")
+        with nc.allow_non_contiguous_dma(reason="one gate a partition"):
+            nc.sync.dma_start(out=gate_columns[:], in_=gate[0, :].rearrange("(e u) -> u e", u=C))
+        load_experts(1, 2)
+        load_experts(2, 4)
+        load_experts(4, 6)
+        a_rows = keep.tile([P, PACK, T], F32, name="a_rows", align_bytes=64)
+        nc.sync.dma_start(out=a_rows[:], in_=a.rearrange("(p t) c -> p t c", t=PACK))
 
         identity = keep.tile([P, P], F32, name="identity")
         make_identity(nc, identity[:])
 
-        slot_scales = {}
         slot_plane = {}
-
-        def move_second_pass(first, last, name):
-            second = keep.tile([P, (last - first) * C], U8, name=f"{name}_scales_second", align_bytes=64)
-            nc.gpsimd.memset(second[:].bitcast(I32), 0)
-            for base in range(0, P, QUADRANT):
-                nc.sync.dma_start(
-                    out=second[base : base + QUADRANT_ROWS, :].bitcast(I32),
-                    in_=slot_scales[name][base + QUADRANT_ROWS : base + 2 * QUADRANT_ROWS, :].bitcast(I32),
-                )
-            for e in range(first, last):
-                columns = slice((e - first) * C, (e - first + 1) * C)
-                slot_plane[e, 0] = slot_scales[name][:, columns]
-                slot_plane[e, 1] = second[:, columns]
-
-        for first, last, name in SCALE_GROUPS:
-            slot_scales[name] = keep.tile([P, (last - first) * C], U8, name=f"{name}_scales", align_bytes=64)
-            nc.vector.tensor_copy(out=slot_scales[name][:], in_=token_scales[:].indirect(offsets_of(first, last)))
-        move_second_pass(*SCALE_GROUPS[0])
-        early_gates = head.tile([P, EARLY * C], F32, name="early_gates", offset=EARLY_GATES_AT, align_bytes=64)
-        nc.sync.dma_start(out=early_gates[:], in_=gate[:, 0 : EARLY * C])
-        load_experts(1, 2, head, offset=EXPERT_1_AT)
-        move_second_pass(*SCALE_GROUPS[1])
-
         slot_words = {}
-        for first, last in WORD_GROUPS:
+
+        def gather_scales(first, last, tag):
+            for s in range(PASSES):
+                gathered = keep.tile(
+                    [P, (last - first) * C], U8, name=f"scales{first}_{s}", tag=f"{tag}_{s}", align_bytes=64
+                )
+                nc.vector.tensor_copy(out=gathered[:], in_=token_scales[:, s, :].indirect(offsets_of(first, last)))
+                for e in range(first, last):
+                    slot_plane[e, s] = gathered[:, (e - first) * C : (e - first + 1) * C]
+
+        def gather_words(first, last):
             for s in range(PASSES):
                 name = f"words{first}_{s}"
                 gathered = keep.tile([P, (last - first) * C], U32, name=name, tag=name, align_bytes=64)
@@ -142,83 +126,79 @@ def tile_moe_sub_silu_kernel(
                 for e in range(first, last):
                     slot_words[e, s] = gathered[:, (e - first) * C : (e - first + 1) * C]
 
-        load_scale_planes(w2_planes_late, w2_scale_rows[EARLY * PASSES : E * PASSES])
+        gather_scales(0, 3, "scales0")
+        for first, last in WORD_GROUPS:
+            gather_words(first, last)
 
         neg_dh = [keep.tile([P, T], F32, name=f"neg_dh{t}") for t in range(PACK)]
+        y_rows = keep.tile([P, PACK, E * C], F32, name="y_rows", tag="y_rows", align_bytes=64)
         for first, last in SCATTER_GROUPS:
-            y_rows = keep.tile([P, PACK, (last - first) * C], F32, name=f"y_rows{first}")
             for e in range(first, last):
                 if e == 1:
-                    load_experts(2, 4, keep, tag="words0_0")
-                    late_gates = keep.tile([P, (E - EARLY) * C], F32, name="late_gates", tag="words0_1", align_bytes=64)
-                    nc.sync.dma_start(out=late_gates[:], in_=gate[:, EARLY * C : E * C])
-                if e == 2:
-                    load_experts(4, 6, keep, tag="words1_0")
-                    a_rows = keep.tile([P, PACK, T], F32, name="a_rows", tag="words1_1", align_bytes=64)
-                    nc.sync.dma_start(out=a_rows[:], in_=a.rearrange("(p t) c -> p t c", t=PACK))
-                product_bank = FIRST_SLICE_BANK if e == 1 else e % 2
-                y_by_slot = psum.tile([P, H], F32, name="y_by_slot", tag=f"bank{product_bank}")
+                    gather_scales(3, E, "words0")
+                y_by_slot = psum.tile([P, H], F32, name="y_by_slot", tag=f"bank{e % 2}")
                 for s in range(PASSES):
                     nc.tensor.matmul_mx(
                         out=y_by_slot[:],
                         lhsT=slot_words[e, s].bitcast(FP8X4),
                         lhsT_scale=slot_plane[e, s],
                         rhs=w2_words[e * PASSES + s].bitcast(FP4X4),
-                        rhs_scale=w2_plane[e * PASSES + s],
+                        rhs_scale=w2_planes[:, e * PASSES + s, :],
                         start=(s == 0),
                         stop=(s == PASSES - 1),
                     )
                 y_dealt = keep.tile([P, PACK, P], F32, name="y_dealt", tag=f"y_dealt{e}")
-                ring_bank = 2 + e % 2
-                if e < EARLY:
-                    pieces = ((0, 1, FIRST_SLICE_BANK + e), (1, PACK, ring_bank))
-                else:
-                    pieces = ((0, PACK, ring_bank),)
-                for t0, t1, bank in pieces:
-                    nc.scalar.activation(
-                        out=y_dealt[:, t0:t1, :],
-                        in_=y_by_slot[:].rearrange("u (m t) -> u t m", t=PACK)[:, t0:t1, :],
-                        func=ACT.Copy,
-                        scale=-1.0,
-                    )
-                for t0, t1, bank in pieces:
-                    turned = psum.tile([P, t1 - t0, C], F32, name="turned", tag=f"bank{bank}")
-                    for t in range(t0, t1):
-                        nc.tensor.transpose(turned[:, t - t0, :], y_dealt[:, t, :], identity[:])
-                    nc.scalar.copy(out=y_rows[:, t0:t1, (e - first) * C : (e - first + 1) * C], in_=turned[:])
-            if first < EARLY:
-                gates = early_gates[:, first * C : last * C]
-            else:
-                gates = late_gates[:, (first - EARLY) * C : (last - EARLY) * C]
-            for t in range(PACK):
-                nc.vector.tensor_tensor(
-                    out=neg_dh[t][:].indirect(offsets_of(first, last)), in0=y_rows[:, t, :], in1=gates, op=ALU.mult
+                nc.scalar.activation(
+                    out=y_dealt[:],
+                    in_=y_by_slot[:].rearrange("u (m t) -> u t m", t=PACK),
+                    func=ACT.Copy,
+                    scale=gate_columns[:, e : e + 1],
+                )
+                turned = psum.tile([P, PACK, C], F32, name="turned", tag=f"bank{2 + e % 2}")
+                for t in range(PACK):
+                    nc.tensor.transpose(turned[:, t, :], y_dealt[:, t, :], identity[:])
+                nc.scalar.activation(out=y_rows[:, :, e * C : (e + 1) * C], in_=turned[:], func=ACT.Copy, scale=-1.0)
+            for t in range(VECTOR_SLICES):
+                nc.vector.tensor_copy(
+                    out=neg_dh[t][:].indirect(offsets_of(first, last)), in_=y_rows[:, t, first * C : last * C]
                 )
 
-        w1_words_raw = keep.tile([P, K], I32, name="w1_words_raw", tag="words2_1", align_bytes=64)
+        w1_words_raw = keep.tile([P, K], I32, name="w1_words_raw", tag="words3_1", align_bytes=64)
         nc.sync.dma_start(out=w1_words_raw[:], in_=w1t_words[0].rearrange("p k d -> p (k d)").bitcast(I32))
-        w1_words = keep.tile([P, PACK, P], U32, name="w1_words", align_bytes=64)
-        nc.scalar.copy(out=w1_words[:], in_=w1_words_raw[:].bitcast(U32).rearrange("p (m d) -> p d m", d=PACK))
-
+        w1_plane_raw = keep.tile([P, 1, K], U8, name="w1_plane_raw", tag="words3_0", align_bytes=64)
+        nc.gpsimd.memset(w1_plane_raw[:].rearrange("p g k -> p (g k)").bitcast(I32), 0)
         load_scale_planes(w1_plane_raw, w1t_scales)
         w1_plane = keep.tile([P, PACK, P], U8, name="w1_plane", align_bytes=64)
         nc.vector.tensor_copy(out=w1_plane[:], in_=w1_plane_raw[:, 0, :].rearrange("p (m d) -> p d m", d=PACK))
 
-        sig = keep.tile([P, T // RUN, PACK, RUN], F32, name="sig", tag=f"y_dealt{ACTIVATIONS_BEHIND}")
+        sig = keep.tile([P, T // RUN, PACK, RUN], F32, name="sig")
         a_in_runs = a_rows[:].rearrange("p t (c j) -> p c t j", j=RUN)
         for piece in range(PACK):
             runs = slice(piece * T // RUN // PACK, (piece + 1) * T // RUN // PACK)
             nc.scalar.activation(out=sig[:, runs, :, :], in_=a_in_runs[:, runs, :, :], func=ACT.Sigmoid)
+        for t in range(VECTOR_SLICES, PACK):
+            for first, last in SCALAR_GROUPS:
+                nc.scalar.activation(
+                    out=neg_dh[t][:].indirect(offsets_of(first, last)),
+                    in_=y_rows[:, t, first * C : last * C],
+                    func=ACT.Copy,
+                )
+        w1_words = keep.tile([P, PACK, P], U32, name="w1_words", tag="y_rows", align_bytes=64)
+        nc.scalar.copy(out=w1_words[:], in_=w1_words_raw[:].bitcast(U32).rearrange("p (m d) -> p d m", d=PACK))
         silu_of_neg_a = a_rows
-        nc.scalar.activation(out=silu_of_neg_a[:], in_=a_rows[:], func=ACT.Silu, scale=-1.0)
+        for t in range(PACK):
+            a_row = a_rows[:, t, :].rearrange("p (c j) -> p c j", j=RUN)
+            nc.vector.scalar_tensor_tensor(
+                out=a_row, in0=sig[:, :, t, :], scalar=1.0, in1=a_row, op0=ALU.subtract, op1=ALU.mult
+            )
 
         out_codes = keep.tile([P, T], U32, name="out_codes", align_bytes=64)
         out_plane = keep.tile([P, T], U8, name="out_plane", align_bytes=64)
 
         half_da = keep.tile([P, T // RUN, PACK, RUN], F32, name="half_da")
 
-        def first_products(tokens):
-            for t in range(PACK):
+        def first_products(tokens, slices):
+            for t in slices:
                 nc.vector.scalar_tensor_tensor(
                     out=half_da[:, tokens.start // RUN : tokens.stop // RUN, t, :],
                     in0=silu_of_neg_a[:, t, tokens].rearrange("p (c j) -> p c j", j=RUN),
@@ -249,8 +229,9 @@ def tile_moe_sub_silu_kernel(
             return [slice(start, start + BLOCK) for start in range(lo, hi, BLOCK)]
 
         da_quantised = {}
+        first_products(slice(0, T), range(PACK - 1))
         for lo, hi in zip(PRODUCT_EDGES, PRODUCT_EDGES[1:]):
-            first_products(slice(lo, hi))
+            first_products(slice(lo, hi), [PACK - 1])
             for tokens in blocks_in(lo, hi):
                 da_quantised[tokens.start] = quantised_da(tokens)
 

@@ -28,9 +28,10 @@ SCALE_WINDOW = 1024
 SCALE_GROUPS = ((0, 1, "early"), (1, E, "late"))
 WORD_GROUPS = ((0, 1), (1, 3), (3, E))
 EARLY = 2
-SCATTER_GROUPS = ((0, 2), (2, 4), (4, 6))
+SCATTER_GROUPS = ((0, 1), (1, 2), (2, 4), (4, 6))
 VECTOR_SLICES = 2
-SCALAR_GROUPS = ((3, 6), (0, 3))
+SHARED_SPLIT = 192
+SCALAR_GROUPS = {2: ((384, 768), (SHARED_SPLIT, 384)), 3: ((384, 768), (0, 384))}
 EXPERT_1_AT = 0
 EARLY_GATES_AT = PASSES * 2 * H
 TOKEN_SCALES_AT = EARLY_GATES_AT - 384
@@ -39,9 +40,9 @@ ACTIVATIONS_BEHIND = 3
 RUN = 4
 BLOCK = 128
 PRODUCT_EDGES = [0, 128, 384, 640, 768]
-PLANE_EDGES = [0, 256, 512, 640, 768]
+PLANE_EDGES = [0, 256, 512, 768]
 CODE_STORE_EDGES = [0, 256, 768]
-VECTOR_ROUNDS_FROM = 512
+VECTOR_ROUNDS_FROM = 128
 
 
 def tile_moe_sub_silu_kernel(
@@ -54,6 +55,9 @@ def tile_moe_sub_silu_kernel(
 
         def offsets_of(first, last):
             return offsets[:, first * C // LIST_ROWS : last * C // LIST_ROWS]
+
+        def scatter_target(t, first, last):
+            return neg_dh[t][:].indirect(offsets[:, first // LIST_ROWS : last // LIST_ROWS])
 
         def load_scale_planes(planes, rows, which=range(QUADRANT_ROWS)):
             for r in which:
@@ -160,7 +164,11 @@ def tile_moe_sub_silu_kernel(
                 nc.scalar.activation(out=y_rows[:, :, e * C : (e + 1) * C], in_=turned[:], func=ACT.Copy, scale=-1.0)
             for t in range(VECTOR_SLICES):
                 nc.vector.tensor_copy(
-                    out=neg_dh[t][:].indirect(offsets_of(first, last)), in_=y_rows[:, t, first * C : last * C]
+                    out=scatter_target(t, first * C, last * C), in_=y_rows[:, t, first * C : last * C]
+                )
+            if first == 1:
+                nc.vector.tensor_copy(
+                    out=scatter_target(VECTOR_SLICES, 0, SHARED_SPLIT), in_=y_rows[:, VECTOR_SLICES, 0:SHARED_SPLIT]
                 )
 
         w1_words_raw = keep.tile([P, K], I32, name="w1_words_raw", tag="words3_1", align_bytes=64)
@@ -177,10 +185,10 @@ def tile_moe_sub_silu_kernel(
             runs = slice(piece * T // RUN // PACK, (piece + 1) * T // RUN // PACK)
             nc.scalar.activation(out=sig[:, runs, :, :], in_=a_in_runs[:, runs, :, :], func=ACT.Sigmoid)
         for t in range(VECTOR_SLICES, PACK):
-            for first, last in SCALAR_GROUPS:
+            for first, last in SCALAR_GROUPS[t]:
                 nc.scalar.activation(
-                    out=neg_dh[t][:].indirect(offsets_of(first, last)),
-                    in_=y_rows[:, t, first * C : last * C],
+                    out=scatter_target(t, first, last),
+                    in_=y_rows[:, t, first:last],
                     func=ACT.Copy,
                 )
         w1_words = keep.tile([P, PACK, P], U32, name="w1_words", tag="y_rows", align_bytes=64)

@@ -26,11 +26,12 @@ QUADRANT_ROWS = 4
 LIST_ROWS = 16
 SCALE_WINDOW = 1024
 SCALE_GROUPS = ((0, 1, "early"), (1, E, "late"))
-WORD_GROUPS = ((0, 1), (1, 3), (3, E))
+WORD_GROUPS = ((0, 1), (1, 2), (2, 4), (4, E))
 EARLY = 2
 SCATTER_GROUPS = ((0, 1), (1, 2), (2, 4), (4, 6))
 VECTOR_SLICES = 2
-SHARED_SPLIT = 192
+FIRST_TOKENS = 128
+SHARED_SPLIT = 128
 SCALAR_GROUPS = {2: ((384, 768), (SHARED_SPLIT, 384)), 3: ((384, 768), (0, 384))}
 EXPERT_1_AT = 0
 EARLY_GATES_AT = PASSES * 2 * H
@@ -40,8 +41,8 @@ ACTIVATIONS_BEHIND = 3
 RUN = 4
 BLOCK = 128
 PRODUCT_EDGES = [0, 128, 384, 640, 768]
-PLANE_EDGES = [0, 256, 512, 768]
-CODE_STORE_EDGES = [0, 256, 768]
+PLANE_EDGES = [0, 256, 512, 640, 768]
+CODE_STORE_EDGES = [0, 256, 640, 768]
 VECTOR_ROUNDS_FROM = 128
 
 
@@ -73,12 +74,9 @@ def tile_moe_sub_silu_kernel(
         nc.gpsimd.memset(token_scales[:].rearrange("p s t -> p (s t)").bitcast(I32), 0)
         load_scale_planes(token_scales, dy_scales)
 
-        warm = keep.tile([P, 8], F32, name="warm", tag="warm", align_bytes=64)
-        nc.gpsimd.memset(warm[:], 0.0)
-        nc.scalar.activation(out=warm[:, 0:1], in_=warm[:, 1:2], func=ACT.Sigmoid)
-
         w2_scale_rows = w2t_scales.rearrange("e s b i -> (e s) b i")
         w2_planes = keep.tile([P, E * PASSES, H], U8, name="w2_planes", align_bytes=64)
+        w2_plane = [w2_planes[:, g, :] for g in range(E * PASSES)]
         w2_words = {}
 
         def load_experts(first, last, **place):
@@ -91,10 +89,14 @@ def tile_moe_sub_silu_kernel(
             for g in range(count):
                 w2_words[first * PASSES + g] = words[:, g, :]
 
-        load_scale_planes(w2_planes, w2_scale_rows, range(2))
+        a_rows = keep.tile([P, PACK, T], F32, name="a_rows", align_bytes=64)
+        a_flat = a_rows[:].rearrange("p t c -> p (t c)")
+        a_hbm = a.rearrange("(p t) c -> p (t c)", t=PACK)
+        nc.sync.dma_start(out=a_flat[:, 0:FIRST_TOKENS], in_=a_hbm[:, 0:FIRST_TOKENS])
+        load_scale_planes(w2_planes, w2_scale_rows, range(1))
         token_words = keep.tile([P, PASSES, T], I32, name="token_words", align_bytes=64)
         nc.sync.dma_start(out=token_words[:], in_=dy_words.rearrange("s p t d -> p s (t d)").bitcast(I32))
-        load_scale_planes(w2_planes, w2_scale_rows, range(2, QUADRANT_ROWS))
+        load_scale_planes(w2_planes, w2_scale_rows, range(1, QUADRANT_ROWS))
         load_experts(0, 1)
         gate_columns = keep.tile([P, E], F32, name="gate_columns")
         with nc.allow_non_contiguous_dma(reason="one gate a partition"):
@@ -102,8 +104,7 @@ def tile_moe_sub_silu_kernel(
         load_experts(1, 2)
         load_experts(2, 4)
         load_experts(4, 6)
-        a_rows = keep.tile([P, PACK, T], F32, name="a_rows", align_bytes=64)
-        nc.sync.dma_start(out=a_rows[:], in_=a.rearrange("(p t) c -> p t c", t=PACK))
+        nc.sync.dma_start(out=a_flat[:, FIRST_TOKENS : PACK * T], in_=a_hbm[:, FIRST_TOKENS : PACK * T])
 
         identity = keep.tile([P, P], F32, name="identity")
         make_identity(nc, identity[:])
@@ -130,50 +131,59 @@ def tile_moe_sub_silu_kernel(
                 for e in range(first, last):
                     slot_words[e, s] = gathered[:, (e - first) * C : (e - first + 1) * C]
 
-        gather_scales(0, 3, "scales0")
+        gather_scales(0, 4, "scales0")
         for first, last in WORD_GROUPS:
             gather_words(first, last)
 
         neg_dh = [keep.tile([P, T], F32, name=f"neg_dh{t}") for t in range(PACK)]
         y_rows = keep.tile([P, PACK, E * C], F32, name="y_rows", tag="y_rows", align_bytes=64)
+        y_dealt = {}
+
+        def multiply(e):
+            y_by_slot = psum.tile([P, H], F32, name="y_by_slot", tag=f"bank{e % 2}")
+            for s in range(PASSES):
+                nc.tensor.matmul_mx(
+                    out=y_by_slot[:],
+                    lhsT=slot_words[e, s].bitcast(FP8X4),
+                    lhsT_scale=slot_plane[e, s],
+                    rhs=w2_words[e * PASSES + s].bitcast(FP4X4),
+                    rhs_scale=w2_plane[e * PASSES + s],
+                    start=(s == 0),
+                    stop=(s == PASSES - 1),
+                )
+            y_dealt[e] = keep.tile([P, PACK, P], F32, name=f"y_dealt{e}")
+            nc.scalar.activation(
+                out=y_dealt[e][:],
+                in_=y_by_slot[:].rearrange("u (m t) -> u t m", t=PACK),
+                func=ACT.Copy,
+                scale=gate_columns[:, e : e + 1],
+            )
+
+        def turn(e):
+            turned = psum.tile([P, PACK, C], F32, name="turned", tag=f"bank{2 + e % 2}")
+            for t in range(PACK):
+                nc.tensor.transpose(turned[:, t, :], y_dealt[e][:, t, :], identity[:])
+            nc.scalar.activation(out=y_rows[:, :, e * C : (e + 1) * C], in_=turned[:], func=ACT.Copy, scale=-1.0)
+
+        multiply(0)
+        gather_scales(4, E, "words0")
         for first, last in SCATTER_GROUPS:
             for e in range(first, last):
-                if e == 1:
-                    gather_scales(3, E, "words0")
-                y_by_slot = psum.tile([P, H], F32, name="y_by_slot", tag=f"bank{e % 2}")
-                for s in range(PASSES):
-                    nc.tensor.matmul_mx(
-                        out=y_by_slot[:],
-                        lhsT=slot_words[e, s].bitcast(FP8X4),
-                        lhsT_scale=slot_plane[e, s],
-                        rhs=w2_words[e * PASSES + s].bitcast(FP4X4),
-                        rhs_scale=w2_planes[:, e * PASSES + s, :],
-                        start=(s == 0),
-                        stop=(s == PASSES - 1),
-                    )
-                y_dealt = keep.tile([P, PACK, P], F32, name="y_dealt", tag=f"y_dealt{e}")
-                nc.scalar.activation(
-                    out=y_dealt[:],
-                    in_=y_by_slot[:].rearrange("u (m t) -> u t m", t=PACK),
-                    func=ACT.Copy,
-                    scale=gate_columns[:, e : e + 1],
-                )
-                turned = psum.tile([P, PACK, C], F32, name="turned", tag=f"bank{2 + e % 2}")
-                for t in range(PACK):
-                    nc.tensor.transpose(turned[:, t, :], y_dealt[:, t, :], identity[:])
-                nc.scalar.activation(out=y_rows[:, :, e * C : (e + 1) * C], in_=turned[:], func=ACT.Copy, scale=-1.0)
+                if e + 1 < E:
+                    multiply(e + 1)
+                turn(e)
             for t in range(VECTOR_SLICES):
                 nc.vector.tensor_copy(
                     out=scatter_target(t, first * C, last * C), in_=y_rows[:, t, first * C : last * C]
                 )
-            if first == 1:
+            if first == 0:
                 nc.vector.tensor_copy(
                     out=scatter_target(VECTOR_SLICES, 0, SHARED_SPLIT), in_=y_rows[:, VECTOR_SLICES, 0:SHARED_SPLIT]
                 )
 
-        w1_words_raw = keep.tile([P, K], I32, name="w1_words_raw", tag="words3_1", align_bytes=64)
+        w1_words_raw = keep.tile([P, K], I32, name="w1_words_raw", tag="words4_1", align_bytes=64)
         nc.sync.dma_start(out=w1_words_raw[:], in_=w1t_words[0].rearrange("p k d -> p (k d)").bitcast(I32))
-        w1_plane_raw = keep.tile([P, 1, K], U8, name="w1_plane_raw", tag="words3_0", align_bytes=64)
+        w1_plane_raw = keep.tile([P, 1, K], U8, name="w1_plane_raw", tag="words4_0", align_bytes=64)
         nc.gpsimd.memset(w1_plane_raw[:].rearrange("p g k -> p (g k)").bitcast(I32), 0)
         load_scale_planes(w1_plane_raw, w1t_scales)
         w1_plane = keep.tile([P, PACK, P], U8, name="w1_plane", align_bytes=64)
@@ -181,9 +191,10 @@ def tile_moe_sub_silu_kernel(
 
         sig = keep.tile([P, T // RUN, PACK, RUN], F32, name="sig")
         a_in_runs = a_rows[:].rearrange("p t (c j) -> p c t j", j=RUN)
-        for piece in range(PACK):
-            runs = slice(piece * T // RUN // PACK, (piece + 1) * T // RUN // PACK)
-            nc.scalar.activation(out=sig[:, runs, :, :], in_=a_in_runs[:, runs, :, :], func=ACT.Sigmoid)
+        pieces = [(0, 0, FIRST_TOKENS), (0, FIRST_TOKENS, T)] + [(t, 0, T) for t in range(1, PACK)]
+        for t, lo, hi in pieces:
+            runs = slice(lo // RUN, hi // RUN)
+            nc.scalar.activation(out=sig[:, runs, t, :], in_=a_in_runs[:, runs, t, :], func=ACT.Sigmoid)
         for t in range(VECTOR_SLICES, PACK):
             for first, last in SCALAR_GROUPS[t]:
                 nc.scalar.activation(
@@ -279,12 +290,9 @@ def tile_moe_sub_silu_kernel(
                     )
                 nc.sync.dma_start(out=out_rows_hbm[:, :, tokens], in_=out_rows[:, :, tokens])
             else:
-                nc.vector.tensor_copy(out=out_grouped[:, tokens, :], in_=acc[:].rearrange("p d c -> p c d"))
-                for half in range(2):
-                    rows = slice(2 * half, 2 * half + 2)
-                    acc_again = shared_layer(da_codes[:], da_plane[:], bank + 1 + half, rows)
-                    nc.scalar.copy(out=out_rows[:, rows, tokens], in_=acc_again[:])
-                    nc.sync.dma_start(out=out_rows_hbm[:, rows, tokens], in_=out_rows[:, rows, tokens])
+                nc.scalar.copy(out=out_grouped[:, tokens, :], in_=acc[:].rearrange("p d c -> p c d"))
+                nc.scalar.copy(out=out_rows[:, :, tokens], in_=acc[:])
+                nc.sync.dma_start(out=out_rows_hbm[:, :, tokens], in_=out_rows[:, :, tokens])
             if tokens.stop in PLANE_EDGES:
                 group = since_last(PLANE_EDGES, tokens.stop)
                 nc.vector.quantize_mx(

@@ -21,23 +21,16 @@ P = 128
 PACK = 4
 PASSES = N // (P * PACK)
 QUADRANT = 32
+QUADRANTS = P // QUADRANT
 SCALE_ROWS = 16
 QUADRANT_ROWS = 4
 LIST_ROWS = 16
-SCALE_WINDOW = 1024
-SCALE_GROUPS = ((0, 1, "early"), (1, E, "late"))
-WORD_GROUPS = ((0, 1), (1, 2), (2, 4), (4, E))
-EARLY = 2
-SCATTER_GROUPS = ((0, 1), (1, 2), (2, 4), (4, 6))
-VECTOR_SLICES = 2
 FIRST_TOKENS = 128
-SHARED_SPLIT = 128
-SCALAR_GROUPS = {2: ((384, 768), (SHARED_SPLIT, 384)), 3: ((384, 768), (0, 384))}
-EXPERT_1_AT = 0
-EARLY_GATES_AT = PASSES * 2 * H
-TOKEN_SCALES_AT = EARLY_GATES_AT - 384
-FIRST_SLICE_BANK = 4
-ACTIVATIONS_BEHIND = 3
+WORD_GROUPS = ((0, 1), (1, 2), (2, 4), (4, E))
+VECTOR_GROUPS = ((0, 1), (1, 2), (2, 4), (4, E))
+VECTOR_SLICES = 2
+SHARED_SPLIT = 512
+SCALAR_SCATTERS = ((3, 384, 768), (2, SHARED_SPLIT, 768), (3, 0, 384))
 RUN = 4
 BLOCK = 128
 PRODUCT_EDGES = [0, 128, 384, 640, 768]
@@ -52,13 +45,11 @@ def tile_moe_sub_silu_kernel(
     nc = tc.nc
     with ExitStack() as ctx:
         keep = ctx.enter_context(tc.tile_pool(name="keep", bufs=1))
+        shared = ctx.enter_context(tc.tile_pool(name="shared", bufs=1))
         psum = ctx.enter_context(tc.psum_pool(name="psum", bufs=1))
 
         def offsets_of(first, last):
-            return offsets[:, first * C // LIST_ROWS : last * C // LIST_ROWS]
-
-        def scatter_target(t, first, last):
-            return neg_dh[t][:].indirect(offsets[:, first // LIST_ROWS : last // LIST_ROWS])
+            return offsets[:, first // LIST_ROWS : last // LIST_ROWS]
 
         def load_scale_planes(planes, rows, which=range(QUADRANT_ROWS)):
             for r in which:
@@ -79,9 +70,9 @@ def tile_moe_sub_silu_kernel(
         w2_plane = [w2_planes[:, g, :] for g in range(E * PASSES)]
         w2_words = {}
 
-        def load_experts(first, last, **place):
+        def load_experts(first, last):
             count = (last - first) * PASSES
-            words = keep.tile([P, count, 2 * H], U8, name=f"w2_words{first}", align_bytes=64, **place)
+            words = keep.tile([P, count, 2 * H], U8, name=f"w2_words{first}", align_bytes=64)
             nc.sync.dma_start(
                 out=words[:].bitcast(I32),
                 in_=w2t_words[first:last].rearrange("e s p b -> p (e s) b").bitcast(I32),
@@ -117,7 +108,9 @@ def tile_moe_sub_silu_kernel(
                 gathered = keep.tile(
                     [P, (last - first) * C], U8, name=f"scales{first}_{s}", tag=f"{tag}_{s}", align_bytes=64
                 )
-                nc.vector.tensor_copy(out=gathered[:], in_=token_scales[:, s, :].indirect(offsets_of(first, last)))
+                nc.vector.tensor_copy(
+                    out=gathered[:], in_=token_scales[:, s, :].indirect(offsets_of(first * C, last * C))
+                )
                 for e in range(first, last):
                     slot_plane[e, s] = gathered[:, (e - first) * C : (e - first + 1) * C]
 
@@ -126,7 +119,7 @@ def tile_moe_sub_silu_kernel(
                 name = f"words{first}_{s}"
                 gathered = keep.tile([P, (last - first) * C], U32, name=name, tag=name, align_bytes=64)
                 nc.vector.tensor_copy(
-                    out=gathered[:], in_=token_words[:, s, :].bitcast(U32).indirect(offsets_of(first, last))
+                    out=gathered[:], in_=token_words[:, s, :].bitcast(U32).indirect(offsets_of(first * C, last * C))
                 )
                 for e in range(first, last):
                     slot_words[e, s] = gathered[:, (e - first) * C : (e - first + 1) * C]
@@ -136,7 +129,7 @@ def tile_moe_sub_silu_kernel(
             gather_words(first, last)
 
         neg_dh = [keep.tile([P, T], F32, name=f"neg_dh{t}") for t in range(PACK)]
-        y_rows = keep.tile([P, PACK, E * C], F32, name="y_rows", tag="y_rows", align_bytes=64)
+        y_rows = shared.tile([P, PACK, E * C], F32, name="y_rows", offset=0)
         y_dealt = {}
 
         def multiply(e):
@@ -163,22 +156,27 @@ def tile_moe_sub_silu_kernel(
             turned = psum.tile([P, PACK, C], F32, name="turned", tag=f"bank{2 + e % 2}")
             for t in range(PACK):
                 nc.tensor.transpose(turned[:, t, :], y_dealt[e][:, t, :], identity[:])
-            nc.scalar.activation(out=y_rows[:, :, e * C : (e + 1) * C], in_=turned[:], func=ACT.Copy, scale=-1.0)
+            nc.scalar.activation(out=y_rows[:, :, e * C : (e + 1) * C], in_=turned[:], func=ACT.Copy, scale=-0.5)
+
+        def scatter_target(t, first, last):
+            return neg_dh[t][:].indirect(offsets_of(first, last))
 
         multiply(0)
         gather_scales(4, E, "words0")
-        for first, last in SCATTER_GROUPS:
-            for e in range(first, last):
-                if e + 1 < E:
-                    multiply(e + 1)
-                turn(e)
+        for e in range(E):
+            if e + 1 < E:
+                multiply(e + 1)
+            turn(e)
+
+        for first, last in VECTOR_GROUPS:
+            if last * C <= SHARED_SPLIT:
+                nc.vector.tensor_copy(
+                    out=scatter_target(VECTOR_SLICES, first * C, last * C),
+                    in_=y_rows[:, VECTOR_SLICES, first * C : last * C],
+                )
             for t in range(VECTOR_SLICES):
                 nc.vector.tensor_copy(
                     out=scatter_target(t, first * C, last * C), in_=y_rows[:, t, first * C : last * C]
-                )
-            if first == 0:
-                nc.vector.tensor_copy(
-                    out=scatter_target(VECTOR_SLICES, 0, SHARED_SPLIT), in_=y_rows[:, VECTOR_SLICES, 0:SHARED_SPLIT]
                 )
 
         w1_words_raw = keep.tile([P, K], I32, name="w1_words_raw", tag="words4_1", align_bytes=64)
@@ -189,32 +187,33 @@ def tile_moe_sub_silu_kernel(
         w1_plane = keep.tile([P, PACK, P], U8, name="w1_plane", align_bytes=64)
         nc.vector.tensor_copy(out=w1_plane[:], in_=w1_plane_raw[:, 0, :].rearrange("p (m d) -> p d m", d=PACK))
 
-        sig = keep.tile([P, T // RUN, PACK, RUN], F32, name="sig")
-        a_in_runs = a_rows[:].rearrange("p t (c j) -> p c t j", j=RUN)
+        silu_of_neg_a = keep.tile([P, PACK, T], F32, name="silu_of_neg_a", align_bytes=64)
         pieces = [(0, 0, FIRST_TOKENS), (0, FIRST_TOKENS, T)] + [(t, 0, T) for t in range(1, PACK)]
         for t, lo, hi in pieces:
-            runs = slice(lo // RUN, hi // RUN)
-            nc.scalar.activation(out=sig[:, runs, t, :], in_=a_in_runs[:, runs, t, :], func=ACT.Sigmoid)
-        for t in range(VECTOR_SLICES, PACK):
-            for first, last in SCALAR_GROUPS[t]:
-                nc.scalar.activation(
-                    out=scatter_target(t, first, last),
-                    in_=y_rows[:, t, first:last],
-                    func=ACT.Copy,
-                )
-        w1_words = keep.tile([P, PACK, P], U32, name="w1_words", tag="y_rows", align_bytes=64)
+            nc.scalar.activation(out=silu_of_neg_a[:, t, lo:hi], in_=a_rows[:, t, lo:hi], func=ACT.Silu, scale=-1.0)
+
+        def in_runs(rows, tokens):
+            return rows[:, :, tokens].rearrange("p t (c j) -> p c t j", j=RUN)
+
+        tanh_of_half_a = {}
+
+        def take_tanh(block, pool, **place):
+            tokens = slice(block * BLOCK, (block + 1) * BLOCK)
+            values = pool.tile([P, BLOCK // RUN, PACK, RUN], F32, name=f"tanh_of_half_a{block}", **place)
+            nc.scalar.activation(out=values[:], in_=in_runs(a_rows, tokens), func=ACT.Tanh, scale=0.5)
+            tanh_of_half_a[tokens.start] = values
+
+        take_tanh(0, keep)
+        w1_words = keep.tile([P, PACK, P], U32, name="w1_words", align_bytes=64)
         nc.scalar.copy(out=w1_words[:], in_=w1_words_raw[:].bitcast(U32).rearrange("p (m d) -> p d m", d=PACK))
-        silu_of_neg_a = a_rows
-        for t in range(PACK):
-            a_row = a_rows[:, t, :].rearrange("p (c j) -> p c j", j=RUN)
-            nc.vector.scalar_tensor_tensor(
-                out=a_row, in0=sig[:, :, t, :], scalar=1.0, in1=a_row, op0=ALU.subtract, op1=ALU.mult
-            )
+        for t, first, last in SCALAR_SCATTERS:
+            nc.scalar.activation(out=scatter_target(t, first, last), in_=y_rows[:, t, first:last], func=ACT.Copy)
+        for block in range(1, T // BLOCK):
+            take_tanh(block, shared, offset=block * BLOCK * PACK * 4)
 
         out_codes = keep.tile([P, T], U32, name="out_codes", align_bytes=64)
         out_plane = keep.tile([P, T], U8, name="out_plane", align_bytes=64)
-
-        half_da = keep.tile([P, T // RUN, PACK, RUN], F32, name="half_da")
+        half_da = keep.tile([P, T // RUN, PACK, RUN], F32, name="half_da", align_bytes=64)
 
         def first_products(tokens, slices):
             for t in slices:
@@ -228,14 +227,15 @@ def tile_moe_sub_silu_kernel(
                 )
 
         def quantised_da(tokens):
-            runs = slice(tokens.start // RUN, tokens.stop // RUN)
             width = tokens.stop - tokens.start
             da_grouped = keep.tile([P, width, PACK], BF16, name=f"da_grouped{tokens.start}", align_bytes=64)
-            nc.vector.tensor_tensor(
-                out=da_grouped[:].rearrange("p (c j) t -> p c t j", j=RUN),
-                in0=half_da[:, runs, :, :],
-                in1=sig[:, runs, :, :],
-                op=ALU.mult,
+            nc.vector.scalar_tensor_tensor(
+                out=da_grouped[:].rearrange("p (j c) t -> p (c t) j", j=RUN),
+                in0=tanh_of_half_a[tokens.start][:].rearrange("p c t j -> p (c t) j"),
+                scalar=1.0,
+                in1=half_da[:, tokens.start // RUN : tokens.stop // RUN, :, :].rearrange("p c t j -> p (c t) j"),
+                op0=ALU.add,
+                op1=ALU.mult,
             )
             da_codes = keep.tile([P, width], U32, name=f"da_codes{tokens.start}", align_bytes=64)
             da_plane = keep.tile([P, width], U8, name=f"da_plane{tokens.start}", align_bytes=64)
@@ -280,9 +280,15 @@ def tile_moe_sub_silu_kernel(
             da_codes, da_plane = da_quantised[tokens.start]
             acc = shared_layer(da_codes[:], da_plane[:], bank)
             if tokens.stop < T:
-                nc.scalar.copy(out=out_rows[:, :, tokens], in_=acc[:])
+                nc.scalar.copy(
+                    out=out_rows[:, :, tokens].rearrange("p d (c j) -> p d c j", j=RUN),
+                    in_=acc[:].rearrange("p d (j c) -> p d c j", j=RUN),
+                )
                 if tokens.start < VECTOR_ROUNDS_FROM:
-                    nc.scalar.copy(out=out_grouped[:, tokens, :], in_=acc[:].rearrange("p d c -> p c d"))
+                    nc.scalar.copy(
+                        out=out_grouped[:, tokens, :].rearrange("p (c j) d -> p c j d", j=RUN),
+                        in_=acc[:].rearrange("p d (j c) -> p c j d", j=RUN),
+                    )
                 else:
                     nc.vector.tensor_copy(
                         out=out_grouped[:, tokens, :].rearrange("p (c j) d -> p c d j", j=RUN),
@@ -290,8 +296,14 @@ def tile_moe_sub_silu_kernel(
                     )
                 nc.sync.dma_start(out=out_rows_hbm[:, :, tokens], in_=out_rows[:, :, tokens])
             else:
-                nc.scalar.copy(out=out_grouped[:, tokens, :], in_=acc[:].rearrange("p d c -> p c d"))
-                nc.scalar.copy(out=out_rows[:, :, tokens], in_=acc[:])
+                nc.scalar.copy(
+                    out=out_grouped[:, tokens, :].rearrange("p (c j) d -> p c j d", j=RUN),
+                    in_=acc[:].rearrange("p d (j c) -> p c j d", j=RUN),
+                )
+                nc.scalar.copy(
+                    out=out_rows[:, :, tokens].rearrange("p d (c j) -> p d c j", j=RUN),
+                    in_=acc[:].rearrange("p d (j c) -> p d c j", j=RUN),
+                )
                 nc.sync.dma_start(out=out_rows_hbm[:, :, tokens], in_=out_rows[:, :, tokens])
             if tokens.stop in PLANE_EDGES:
                 group = since_last(PLANE_EDGES, tokens.stop)

@@ -26,6 +26,7 @@ SCALE_ROWS = 16
 QUADRANT_ROWS = 4
 LIST_ROWS = 16
 FIRST_TOKENS = 128
+EARLY = 2
 WORD_GROUPS = ((0, 1), (1, 2), (2, 4), (4, E))
 VECTOR_GROUPS = ((0, 1), (1, 2), (2, 4), (4, E))
 VECTOR_SLICES = 2
@@ -63,11 +64,16 @@ def tile_moe_sub_silu_kernel(
 
         token_scales = keep.tile([P, PASSES, T], U8, name="token_scales", align_bytes=64)
         nc.gpsimd.memset(token_scales[:].rearrange("p s t -> p (s t)").bitcast(I32), 0)
+        gate_columns = keep.tile([P, E], F32, name="gate_columns")
+        with nc.allow_non_contiguous_dma(reason="one gate a partition"):
+            nc.sync.dma_start(out=gate_columns[:], in_=gate[0, :].rearrange("(e u) -> u e", u=C))
         load_scale_planes(token_scales, dy_scales)
 
         w2_scale_rows = w2t_scales.rearrange("e s b i -> (e s) b i")
-        w2_planes = keep.tile([P, E * PASSES, H], U8, name="w2_planes", align_bytes=64)
-        w2_plane = [w2_planes[:, g, :] for g in range(E * PASSES)]
+        early_planes = keep.tile([P, EARLY * PASSES, H], U8, name="early_planes", align_bytes=64)
+        late_planes = keep.tile([P, (E - EARLY) * PASSES, H], U8, name="late_planes", align_bytes=64)
+        w2_plane = [early_planes[:, g, :] for g in range(EARLY * PASSES)]
+        w2_plane.extend(late_planes[:, g, :] for g in range((E - EARLY) * PASSES))
         w2_words = {}
 
         def load_experts(first, last):
@@ -83,16 +89,14 @@ def tile_moe_sub_silu_kernel(
         a_rows = keep.tile([P, PACK, T], F32, name="a_rows", align_bytes=64)
         a_flat = a_rows[:].rearrange("p t c -> p (t c)")
         a_hbm = a.rearrange("(p t) c -> p (t c)", t=PACK)
-        nc.sync.dma_start(out=a_flat[:, 0:FIRST_TOKENS], in_=a_hbm[:, 0:FIRST_TOKENS])
-        load_scale_planes(w2_planes, w2_scale_rows, range(1))
+        load_scale_planes(early_planes, w2_scale_rows[0 : EARLY * PASSES], range(1))
         token_words = keep.tile([P, PASSES, T], I32, name="token_words", align_bytes=64)
         nc.sync.dma_start(out=token_words[:], in_=dy_words.rearrange("s p t d -> p s (t d)").bitcast(I32))
-        load_scale_planes(w2_planes, w2_scale_rows, range(1, QUADRANT_ROWS))
+        load_scale_planes(early_planes, w2_scale_rows[0 : EARLY * PASSES], range(1, QUADRANT_ROWS))
         load_experts(0, 1)
-        gate_columns = keep.tile([P, E], F32, name="gate_columns")
-        with nc.allow_non_contiguous_dma(reason="one gate a partition"):
-            nc.sync.dma_start(out=gate_columns[:], in_=gate[0, :].rearrange("(e u) -> u e", u=C))
+        nc.sync.dma_start(out=a_flat[:, 0:FIRST_TOKENS], in_=a_hbm[:, 0:FIRST_TOKENS])
         load_experts(1, 2)
+        load_scale_planes(late_planes, w2_scale_rows[EARLY * PASSES : E * PASSES])
         load_experts(2, 4)
         load_experts(4, 6)
         nc.sync.dma_start(out=a_flat[:, FIRST_TOKENS : PACK * T], in_=a_hbm[:, FIRST_TOKENS : PACK * T])

@@ -25,7 +25,6 @@ QUADRANTS = P // QUADRANT
 SCALE_ROWS = 16
 QUADRANT_ROWS = 4
 LIST_ROWS = 16
-FIRST_TOKENS = 128
 EARLY = 2
 WORD_GROUPS = ((0, 1), (1, 2), (2, 4), (4, E))
 VECTOR_GROUPS = ((0, 1), (1, 2), (2, 4), (4, E))
@@ -86,20 +85,20 @@ def tile_moe_sub_silu_kernel(
             for g in range(count):
                 w2_words[first * PASSES + g] = words[:, g, :]
 
-        a_rows = keep.tile([P, PACK, T], F32, name="a_rows", align_bytes=64)
-        a_flat = a_rows[:].rearrange("p t c -> p (t c)")
-        a_hbm = a.rearrange("(p t) c -> p (t c)", t=PACK)
+        a_first = keep.tile([P, PACK, BLOCK], F32, name="a_first", align_bytes=64)
+        a_rest = keep.tile([P, PACK, T - BLOCK], F32, name="a_rest", align_bytes=64)
+        a_hbm = a.rearrange("(p t) c -> p t c", t=PACK)
         load_scale_planes(early_planes, w2_scale_rows[0 : EARLY * PASSES], range(1))
         token_words = keep.tile([P, PASSES, T], I32, name="token_words", align_bytes=64)
         nc.sync.dma_start(out=token_words[:], in_=dy_words.rearrange("s p t d -> p s (t d)").bitcast(I32))
         load_scale_planes(early_planes, w2_scale_rows[0 : EARLY * PASSES], range(1, QUADRANT_ROWS))
         load_experts(0, 1)
-        nc.sync.dma_start(out=a_flat[:, 0:FIRST_TOKENS], in_=a_hbm[:, 0:FIRST_TOKENS])
+        nc.sync.dma_start(out=a_first[:], in_=a_hbm[:, :, 0:BLOCK])
         load_experts(1, 2)
         load_scale_planes(late_planes, w2_scale_rows[EARLY * PASSES : E * PASSES])
         load_experts(2, 4)
         load_experts(4, 6)
-        nc.sync.dma_start(out=a_flat[:, FIRST_TOKENS : PACK * T], in_=a_hbm[:, FIRST_TOKENS : PACK * T])
+        nc.sync.dma_start(out=a_rest[:], in_=a_hbm[:, :, BLOCK:T])
 
         identity = keep.tile([P, P], F32, name="identity")
         make_identity(nc, identity[:])
@@ -173,10 +172,10 @@ def tile_moe_sub_silu_kernel(
             turn(e)
 
         for first, last in VECTOR_GROUPS:
-            if last * C <= SHARED_SPLIT:
+            if first * C < SHARED_SPLIT:
+                stop = min(last * C, SHARED_SPLIT)
                 nc.vector.tensor_copy(
-                    out=scatter_target(VECTOR_SLICES, first * C, last * C),
-                    in_=y_rows[:, VECTOR_SLICES, first * C : last * C],
+                    out=scatter_target(VECTOR_SLICES, first * C, stop), in_=y_rows[:, VECTOR_SLICES, first * C : stop]
                 )
             for t in range(VECTOR_SLICES):
                 nc.vector.tensor_copy(
@@ -192,20 +191,19 @@ def tile_moe_sub_silu_kernel(
         nc.vector.tensor_copy(out=w1_plane[:], in_=w1_plane_raw[:, 0, :].rearrange("p (m d) -> p d m", d=PACK))
 
         silu_of_neg_a = keep.tile([P, PACK, T], F32, name="silu_of_neg_a", align_bytes=64)
-        pieces = [(0, 0, FIRST_TOKENS), (0, FIRST_TOKENS, T)] + [(t, 0, T) for t in range(1, PACK)]
-        for t, lo, hi in pieces:
-            nc.scalar.activation(out=silu_of_neg_a[:, t, lo:hi], in_=a_rows[:, t, lo:hi], func=ACT.Silu, scale=-1.0)
-
-        def in_runs(rows, tokens):
-            return rows[:, :, tokens].rearrange("p t (c j) -> p c t j", j=RUN)
+        nc.scalar.activation(out=silu_of_neg_a[:, :, 0:BLOCK], in_=a_first[:], func=ACT.Silu, scale=-1.0)
+        for t in range(0, PACK, 2):
+            nc.scalar.activation(
+                out=silu_of_neg_a[:, t : t + 2, BLOCK:T], in_=a_rest[:, t : t + 2, :], func=ACT.Silu, scale=-1.0
+            )
 
         tanh_of_half_a = {}
 
         def take_tanh(block, pool, **place):
-            tokens = slice(block * BLOCK, (block + 1) * BLOCK)
+            rows = a_first[:] if block == 0 else a_rest[:, :, (block - 1) * BLOCK : block * BLOCK]
             values = pool.tile([P, BLOCK // RUN, PACK, RUN], F32, name=f"tanh_of_half_a{block}", **place)
-            nc.scalar.activation(out=values[:], in_=in_runs(a_rows, tokens), func=ACT.Tanh, scale=0.5)
-            tanh_of_half_a[tokens.start] = values
+            nc.scalar.activation(out=values[:], in_=rows.rearrange("p t (c j) -> p c t j", j=RUN), func=ACT.Tanh, scale=0.5)
+            tanh_of_half_a[block * BLOCK] = values
 
         take_tanh(0, keep)
         w1_words = keep.tile([P, PACK, P], U32, name="w1_words", align_bytes=64)

@@ -29,8 +29,8 @@ EARLY = 2
 WORD_GROUPS = ((0, 1), (1, 2), (2, 4), (4, E))
 VECTOR_GROUPS = ((0, 1), (1, 2), (2, 4), (4, E))
 VECTOR_SLICES = 2
-SHARED_SPLIT = 512
-SCALAR_SCATTERS = ((3, 384, 768), (2, SHARED_SPLIT, 768), (3, 0, 384))
+SHARED_SPLIT = 480
+SCALAR_SCATTERS = ((3, 0, 128), (3, 384, 768), (2, SHARED_SPLIT, 768), (3, 128, 384))
 RUN = 4
 BLOCK = 128
 PRODUCT_EDGES = [0, 128, 384, 640, 768]
@@ -136,7 +136,7 @@ def tile_moe_sub_silu_kernel(
         y_dealt = {}
 
         def multiply(e):
-            y_by_slot = psum.tile([P, H], F32, name="y_by_slot", tag=f"bank{e % 2}")
+            y_by_slot = psum.tile([P, H], F32, name="y_by_slot", tag=f"bank{e % 4}")
             for s in range(PASSES):
                 nc.tensor.matmul_mx(
                     out=y_by_slot[:],
@@ -147,7 +147,7 @@ def tile_moe_sub_silu_kernel(
                     start=(s == 0),
                     stop=(s == PASSES - 1),
                 )
-            y_dealt[e] = keep.tile([P, PACK, P], F32, name=f"y_dealt{e}")
+            y_dealt[e] = keep.tile([P, PACK, P], F32, name=f"y_dealt{e}", tag=f"y_dealt{e}")
             nc.scalar.activation(
                 out=y_dealt[e][:],
                 in_=y_by_slot[:].rearrange("u (m t) -> u t m", t=PACK),
@@ -156,13 +156,16 @@ def tile_moe_sub_silu_kernel(
             )
 
         def turn(e):
-            turned = psum.tile([P, PACK, C], F32, name="turned", tag=f"bank{2 + e % 2}")
+            turned = psum.tile([P, PACK, C], F32, name="turned", tag=f"bank{4 + e % 4}")
             for t in range(PACK):
                 nc.tensor.transpose(turned[:, t, :], y_dealt[e][:, t, :], identity[:])
             nc.scalar.activation(out=y_rows[:, :, e * C : (e + 1) * C], in_=turned[:], func=ACT.Copy, scale=-0.5)
 
         def scatter_target(t, first, last):
             return neg_dh[t][:].indirect(offsets_of(first, last))
+
+        def scalar_scatter(t, first, last):
+            nc.scalar.activation(out=scatter_target(t, first, last), in_=y_rows[:, t, first:last], func=ACT.Copy)
 
         multiply(0)
         gather_scales(4, E, "words0")
@@ -190,12 +193,13 @@ def tile_moe_sub_silu_kernel(
         w1_plane = keep.tile([P, PACK, P], U8, name="w1_plane", align_bytes=64)
         nc.vector.tensor_copy(out=w1_plane[:], in_=w1_plane_raw[:, 0, :].rearrange("p (m d) -> p d m", d=PACK))
 
-        silu_of_neg_a = keep.tile([P, PACK, T], F32, name="silu_of_neg_a", align_bytes=64)
-        nc.scalar.activation(out=silu_of_neg_a[:, :, 0:BLOCK], in_=a_first[:], func=ACT.Silu, scale=-1.0)
+        silu_first = keep.tile([P, PACK, BLOCK], F32, name="silu_first", align_bytes=64)
+        nc.scalar.activation(out=silu_first[:], in_=a_first[:], func=ACT.Silu, scale=-1.0)
+        for piece in SCALAR_SCATTERS[:2]:
+            scalar_scatter(*piece)
+        silu_rest = keep.tile([P, PACK, T - BLOCK], F32, name="silu_rest", tag=f"y_dealt{E - 1}")
         for t in range(0, PACK, 2):
-            nc.scalar.activation(
-                out=silu_of_neg_a[:, t : t + 2, BLOCK:T], in_=a_rest[:, t : t + 2, :], func=ACT.Silu, scale=-1.0
-            )
+            nc.scalar.activation(out=silu_rest[:, t : t + 2, :], in_=a_rest[:, t : t + 2, :], func=ACT.Silu, scale=-1.0)
 
         tanh_of_half_a = {}
 
@@ -208,8 +212,8 @@ def tile_moe_sub_silu_kernel(
         take_tanh(0, keep)
         w1_words = keep.tile([P, PACK, P], U32, name="w1_words", align_bytes=64)
         nc.scalar.copy(out=w1_words[:], in_=w1_words_raw[:].bitcast(U32).rearrange("p (m d) -> p d m", d=PACK))
-        for t, first, last in SCALAR_SCATTERS:
-            nc.scalar.activation(out=scatter_target(t, first, last), in_=y_rows[:, t, first:last], func=ACT.Copy)
+        for piece in SCALAR_SCATTERS[2:]:
+            scalar_scatter(*piece)
         for block in range(1, T // BLOCK):
             take_tanh(block, shared, offset=block * BLOCK * PACK * 4)
 
@@ -218,10 +222,14 @@ def tile_moe_sub_silu_kernel(
         half_da = keep.tile([P, T // RUN, PACK, RUN], F32, name="half_da", align_bytes=64)
 
         def first_products(tokens, slices):
+            if tokens.start == 0:
+                silu_of_neg_a = silu_first[:]
+            else:
+                silu_of_neg_a = silu_rest[:, :, tokens.start - BLOCK : tokens.stop - BLOCK]
             for t in slices:
                 nc.vector.scalar_tensor_tensor(
                     out=half_da[:, tokens.start // RUN : tokens.stop // RUN, t, :],
-                    in0=silu_of_neg_a[:, t, tokens].rearrange("p (c j) -> p c j", j=RUN),
+                    in0=silu_of_neg_a[:, t, :].rearrange("p (c j) -> p c j", j=RUN),
                     scalar=1.0,
                     in1=neg_dh[t][:, tokens].rearrange("p (c j) -> p c j", j=RUN),
                     op0=ALU.subtract,
@@ -250,7 +258,8 @@ def tile_moe_sub_silu_kernel(
             return [slice(start, start + BLOCK) for start in range(lo, hi, BLOCK)]
 
         da_quantised = {}
-        first_products(slice(0, T), range(PACK - 1))
+        first_products(slice(0, BLOCK), range(PACK - 1))
+        first_products(slice(BLOCK, T), range(PACK - 1))
         for lo, hi in zip(PRODUCT_EDGES, PRODUCT_EDGES[1:]):
             first_products(slice(lo, hi), [PACK - 1])
             for tokens in blocks_in(lo, hi):

@@ -21,22 +21,23 @@ P = 128
 PACK = 4
 PASSES = N // (P * PACK)
 QUADRANT = 32
-QUADRANTS = P // QUADRANT
 SCALE_ROWS = 16
 QUADRANT_ROWS = 4
 LIST_ROWS = 16
-EARLY = 2
-WORD_GROUPS = ((0, 1), (1, 2), (2, 4), (4, E))
-VECTOR_GROUPS = ((0, 1), (1, 2), (2, 4), (4, E))
-VECTOR_SLICES = 2
-SHARED_SPLIT = 480
-SCALAR_SCATTERS = ((3, 0, 128), (3, 384, 768), (2, SHARED_SPLIT, 768), (3, 128, 384))
+F32_BYTES = 4
+EARLY_PLANES = 2
+EARLY_SCALES = 4
+EXPERT_GROUPS = ((0, 1), (1, 2), (2, 4), (4, E))
+EXPERT_BANKS = 4
+SHARED_SLICE = 2
+SCALAR_SLICE = 3
+SHARED_SPLIT = 416
+SCALAR_SCATTER = 384
 RUN = 4
 BLOCK = 128
 PRODUCT_EDGES = [0, 128, 384, 640, 768]
 PLANE_EDGES = [0, 256, 512, 640, 768]
 CODE_STORE_EDGES = [0, 256, 640, 768]
-VECTOR_ROUNDS_FROM = 128
 
 
 def tile_moe_sub_silu_kernel(
@@ -69,10 +70,10 @@ def tile_moe_sub_silu_kernel(
         load_scale_planes(token_scales, dy_scales)
 
         w2_scale_rows = w2t_scales.rearrange("e s b i -> (e s) b i")
-        early_planes = keep.tile([P, EARLY * PASSES, H], U8, name="early_planes", align_bytes=64)
-        late_planes = keep.tile([P, (E - EARLY) * PASSES, H], U8, name="late_planes", align_bytes=64)
-        w2_plane = [early_planes[:, g, :] for g in range(EARLY * PASSES)]
-        w2_plane.extend(late_planes[:, g, :] for g in range((E - EARLY) * PASSES))
+        early_planes = keep.tile([P, EARLY_PLANES * PASSES, H], U8, name="early_planes", align_bytes=64)
+        late_planes = keep.tile([P, (E - EARLY_PLANES) * PASSES, H], U8, name="late_planes", align_bytes=64)
+        w2_plane = [early_planes[:, g, :] for g in range(EARLY_PLANES * PASSES)]
+        w2_plane.extend(late_planes[:, g, :] for g in range((E - EARLY_PLANES) * PASSES))
         w2_words = {}
 
         def load_experts(first, last):
@@ -88,16 +89,16 @@ def tile_moe_sub_silu_kernel(
         a_first = keep.tile([P, PACK, BLOCK], F32, name="a_first", align_bytes=64)
         a_rest = keep.tile([P, PACK, T - BLOCK], F32, name="a_rest", align_bytes=64)
         a_hbm = a.rearrange("(p t) c -> p t c", t=PACK)
-        load_scale_planes(early_planes, w2_scale_rows[0 : EARLY * PASSES], range(1))
+        load_scale_planes(early_planes, w2_scale_rows[0 : EARLY_PLANES * PASSES], range(1))
         token_words = keep.tile([P, PASSES, T], I32, name="token_words", align_bytes=64)
         nc.sync.dma_start(out=token_words[:], in_=dy_words.rearrange("s p t d -> p s (t d)").bitcast(I32))
-        load_scale_planes(early_planes, w2_scale_rows[0 : EARLY * PASSES], range(1, QUADRANT_ROWS))
-        load_experts(0, 1)
+        load_scale_planes(early_planes, w2_scale_rows[0 : EARLY_PLANES * PASSES], range(1, QUADRANT_ROWS))
+        load_experts(*EXPERT_GROUPS[0])
         nc.sync.dma_start(out=a_first[:], in_=a_hbm[:, :, 0:BLOCK])
-        load_experts(1, 2)
-        load_scale_planes(late_planes, w2_scale_rows[EARLY * PASSES : E * PASSES])
-        load_experts(2, 4)
-        load_experts(4, 6)
+        load_experts(*EXPERT_GROUPS[1])
+        load_scale_planes(late_planes, w2_scale_rows[EARLY_PLANES * PASSES : E * PASSES])
+        for first, last in EXPERT_GROUPS[2:]:
+            load_experts(first, last)
         nc.sync.dma_start(out=a_rest[:], in_=a_hbm[:, :, BLOCK:T])
 
         identity = keep.tile([P, P], F32, name="identity")
@@ -127,16 +128,16 @@ def tile_moe_sub_silu_kernel(
                 for e in range(first, last):
                     slot_words[e, s] = gathered[:, (e - first) * C : (e - first + 1) * C]
 
-        gather_scales(0, 4, "scales0")
-        for first, last in WORD_GROUPS:
+        gather_scales(0, EARLY_SCALES, "scales0")
+        for first, last in EXPERT_GROUPS:
             gather_words(first, last)
 
-        neg_dh = [keep.tile([P, T], F32, name=f"neg_dh{t}") for t in range(PACK)]
+        neg_half_dh = [keep.tile([P, T], F32, name=f"neg_half_dh{t}") for t in range(PACK)]
         y_rows = shared.tile([P, PACK, E * C], F32, name="y_rows", offset=0)
         y_dealt = {}
 
         def multiply(e):
-            y_by_slot = psum.tile([P, H], F32, name="y_by_slot", tag=f"bank{e % 4}")
+            y_by_slot = psum.tile([P, H], F32, name="y_by_slot", tag=f"bank{e % EXPERT_BANKS}")
             for s in range(PASSES):
                 nc.tensor.matmul_mx(
                     out=y_by_slot[:],
@@ -156,38 +157,35 @@ def tile_moe_sub_silu_kernel(
             )
 
         def turn(e):
-            turned = psum.tile([P, PACK, C], F32, name="turned", tag=f"bank{4 + e % 4}")
+            turned = psum.tile([P, PACK, C], F32, name="turned", tag=f"bank{EXPERT_BANKS + e % EXPERT_BANKS}")
             for t in range(PACK):
                 nc.tensor.transpose(turned[:, t, :], y_dealt[e][:, t, :], identity[:])
             nc.scalar.activation(out=y_rows[:, :, e * C : (e + 1) * C], in_=turned[:], func=ACT.Copy, scale=-0.5)
 
-        def scatter_target(t, first, last):
-            return neg_dh[t][:].indirect(offsets_of(first, last))
+        def vector_scatter(t, first, last):
+            nc.vector.tensor_copy(out=neg_half_dh[t][:].indirect(offsets_of(first, last)), in_=y_rows[:, t, first:last])
 
         def scalar_scatter(t, first, last):
-            nc.scalar.activation(out=scatter_target(t, first, last), in_=y_rows[:, t, first:last], func=ACT.Copy)
+            nc.scalar.activation(
+                out=neg_half_dh[t][:].indirect(offsets_of(first, last)), in_=y_rows[:, t, first:last], func=ACT.Copy
+            )
 
         multiply(0)
-        gather_scales(4, E, "words0")
+        gather_scales(EARLY_SCALES, E, "words0")
         for e in range(E):
             if e + 1 < E:
                 multiply(e + 1)
             turn(e)
 
-        for first, last in VECTOR_GROUPS:
+        for first, last in EXPERT_GROUPS:
             if first * C < SHARED_SPLIT:
-                stop = min(last * C, SHARED_SPLIT)
-                nc.vector.tensor_copy(
-                    out=scatter_target(VECTOR_SLICES, first * C, stop), in_=y_rows[:, VECTOR_SLICES, first * C : stop]
-                )
-            for t in range(VECTOR_SLICES):
-                nc.vector.tensor_copy(
-                    out=scatter_target(t, first * C, last * C), in_=y_rows[:, t, first * C : last * C]
-                )
+                vector_scatter(SHARED_SLICE, first * C, min(last * C, SHARED_SPLIT))
+            for t in range(SHARED_SLICE):
+                vector_scatter(t, first * C, last * C)
 
-        w1_words_raw = keep.tile([P, K], I32, name="w1_words_raw", tag="words4_1", align_bytes=64)
+        w1_words_raw = keep.tile([P, K], I32, name="w1_words_raw", tag=f"words{EARLY_SCALES}_1", align_bytes=64)
         nc.sync.dma_start(out=w1_words_raw[:], in_=w1t_words[0].rearrange("p k d -> p (k d)").bitcast(I32))
-        w1_plane_raw = keep.tile([P, 1, K], U8, name="w1_plane_raw", tag="words4_0", align_bytes=64)
+        w1_plane_raw = keep.tile([P, 1, K], U8, name="w1_plane_raw", tag=f"words{EARLY_SCALES}_0", align_bytes=64)
         nc.gpsimd.memset(w1_plane_raw[:].rearrange("p g k -> p (g k)").bitcast(I32), 0)
         load_scale_planes(w1_plane_raw, w1t_scales)
         w1_plane = keep.tile([P, PACK, P], U8, name="w1_plane", align_bytes=64)
@@ -195,8 +193,8 @@ def tile_moe_sub_silu_kernel(
 
         silu_first = keep.tile([P, PACK, BLOCK], F32, name="silu_first", align_bytes=64)
         nc.scalar.activation(out=silu_first[:], in_=a_first[:], func=ACT.Silu, scale=-1.0)
-        for piece in SCALAR_SCATTERS[:2]:
-            scalar_scatter(*piece)
+        scalar_scatter(SCALAR_SLICE, 0, C)
+        scalar_scatter(SCALAR_SLICE, E * C - SCALAR_SCATTER, E * C)
         silu_rest = keep.tile([P, PACK, T - BLOCK], F32, name="silu_rest", tag=f"y_dealt{E - 1}")
         for t in range(0, PACK, 2):
             nc.scalar.activation(out=silu_rest[:, t : t + 2, :], in_=a_rest[:, t : t + 2, :], func=ACT.Silu, scale=-1.0)
@@ -206,16 +204,20 @@ def tile_moe_sub_silu_kernel(
         def take_tanh(block, pool, **place):
             rows = a_first[:] if block == 0 else a_rest[:, :, (block - 1) * BLOCK : block * BLOCK]
             values = pool.tile([P, BLOCK // RUN, PACK, RUN], F32, name=f"tanh_of_half_a{block}", **place)
-            nc.scalar.activation(out=values[:], in_=rows.rearrange("p t (c j) -> p c t j", j=RUN), func=ACT.Tanh, scale=0.5)
+            nc.scalar.activation(
+                out=values[:], in_=rows.rearrange("p t (c j) -> p c t j", j=RUN), func=ACT.Tanh, scale=0.5
+            )
             tanh_of_half_a[block * BLOCK] = values
 
         take_tanh(0, keep)
-        w1_words = keep.tile([P, PACK, P], U32, name="w1_words", align_bytes=64)
-        nc.scalar.copy(out=w1_words[:], in_=w1_words_raw[:].bitcast(U32).rearrange("p (m d) -> p d m", d=PACK))
-        for piece in SCALAR_SCATTERS[2:]:
-            scalar_scatter(*piece)
+        w1_words = keep.tile([P, PACK, P], I32, name="w1_words", align_bytes=64)
+        nc.vector.tensor_copy(
+            out=w1_words[:].rearrange("p d m -> p m d"), in_=w1_words_raw[:].rearrange("p (m d) -> p m d", d=PACK)
+        )
+        scalar_scatter(SHARED_SLICE, SHARED_SPLIT, E * C)
+        scalar_scatter(SCALAR_SLICE, C, E * C - SCALAR_SCATTER)
         for block in range(1, T // BLOCK):
-            take_tanh(block, shared, offset=block * BLOCK * PACK * 4)
+            take_tanh(block, shared, offset=block * BLOCK * PACK * F32_BYTES)
 
         out_codes = keep.tile([P, T], U32, name="out_codes", align_bytes=64)
         out_plane = keep.tile([P, T], U8, name="out_plane", align_bytes=64)
@@ -231,14 +233,13 @@ def tile_moe_sub_silu_kernel(
                     out=half_da[:, tokens.start // RUN : tokens.stop // RUN, t, :],
                     in0=silu_of_neg_a[:, t, :].rearrange("p (c j) -> p c j", j=RUN),
                     scalar=1.0,
-                    in1=neg_dh[t][:, tokens].rearrange("p (c j) -> p c j", j=RUN),
+                    in1=neg_half_dh[t][:, tokens].rearrange("p (c j) -> p c j", j=RUN),
                     op0=ALU.subtract,
                     op1=ALU.mult,
                 )
 
         def quantised_da(tokens):
-            width = tokens.stop - tokens.start
-            da_grouped = keep.tile([P, width, PACK], BF16, name=f"da_grouped{tokens.start}", align_bytes=64)
+            da_grouped = keep.tile([P, BLOCK, PACK], BF16, name=f"da_grouped{tokens.start}", align_bytes=64)
             nc.vector.scalar_tensor_tensor(
                 out=da_grouped[:].rearrange("p (j c) t -> p (c t) j", j=RUN),
                 in0=tanh_of_half_a[tokens.start][:].rearrange("p c t j -> p (c t) j"),
@@ -247,8 +248,8 @@ def tile_moe_sub_silu_kernel(
                 op0=ALU.add,
                 op1=ALU.mult,
             )
-            da_codes = keep.tile([P, width], U32, name=f"da_codes{tokens.start}", align_bytes=64)
-            da_plane = keep.tile([P, width], U8, name=f"da_plane{tokens.start}", align_bytes=64)
+            da_codes = keep.tile([P, BLOCK], U32, name=f"da_codes{tokens.start}", align_bytes=64)
+            da_plane = keep.tile([P, BLOCK], U8, name=f"da_plane{tokens.start}", align_bytes=64)
             nc.vector.quantize_mx(
                 out=da_codes[:].bitcast(FP8X4), scales=da_plane[:], in_=da_grouped[:].rearrange("p c t -> p (c t)")
             )
@@ -258,22 +259,22 @@ def tile_moe_sub_silu_kernel(
             return [slice(start, start + BLOCK) for start in range(lo, hi, BLOCK)]
 
         da_quantised = {}
-        first_products(slice(0, BLOCK), range(PACK - 1))
-        first_products(slice(BLOCK, T), range(PACK - 1))
+        first_products(slice(0, BLOCK), range(SCALAR_SLICE))
+        first_products(slice(BLOCK, T), range(SCALAR_SLICE))
         for lo, hi in zip(PRODUCT_EDGES, PRODUCT_EDGES[1:]):
-            first_products(slice(lo, hi), [PACK - 1])
+            first_products(slice(lo, hi), [SCALAR_SLICE])
             for tokens in blocks_in(lo, hi):
                 da_quantised[tokens.start] = quantised_da(tokens)
 
-        def shared_layer(da_codes, da_plane, bank, rows=slice(0, PACK)):
-            acc = psum.tile([P, rows.stop - rows.start, BLOCK], F32, name="acc", tag=f"bank{bank}")
-            for d in range(rows.start, rows.stop):
+        def shared_layer(da_codes, da_plane, bank):
+            acc = psum.tile([P, PACK, BLOCK], F32, name="acc", tag=f"bank{bank}")
+            for d in range(PACK):
                 nc.tensor.matmul_mx(
-                    out=acc[:, d - rows.start, :],
+                    out=acc[:, d, :],
                     lhsT=w1_words[:, d, :].bitcast(FP8X4),
                     lhsT_scale=w1_plane[:, d, :],
-                    rhs=da_codes.bitcast(FP8X4),
-                    rhs_scale=da_plane,
+                    rhs=da_codes[:].bitcast(FP8X4),
+                    rhs_scale=da_plane[:],
                     start=True,
                     stop=True,
                 )
@@ -284,38 +285,37 @@ def tile_moe_sub_silu_kernel(
         out_rows = keep.tile([P, PACK, T], F32, name="out_rows")
         out_grouped = keep.tile([P, T, PACK], BF16, name="out_grouped", align_bytes=64)
 
+        def copy_sums(acc, tokens):
+            nc.scalar.copy(
+                out=out_rows[:, :, tokens].rearrange("p d (c j) -> p d c j", j=RUN),
+                in_=acc[:].rearrange("p d (j c) -> p d c j", j=RUN),
+            )
+
+        def round_sums(acc, tokens):
+            nc.scalar.copy(
+                out=out_grouped[:, tokens, :].rearrange("p (c j) d -> p c j d", j=RUN),
+                in_=acc[:].rearrange("p d (j c) -> p c j d", j=RUN),
+            )
+
+        def round_rows(tokens):
+            nc.vector.tensor_copy(
+                out=out_grouped[:, tokens, :].rearrange("p (c j) d -> p c d j", j=RUN),
+                in_=out_rows[:, :, tokens].rearrange("p d (c j) -> p c d j", j=RUN),
+            )
+
         def since_last(edges, stop):
             return slice(edges[edges.index(stop) - 1], stop)
 
         for bank, tokens in enumerate(blocks_in(0, T)):
-            da_codes, da_plane = da_quantised[tokens.start]
-            acc = shared_layer(da_codes[:], da_plane[:], bank)
-            if tokens.stop < T:
-                nc.scalar.copy(
-                    out=out_rows[:, :, tokens].rearrange("p d (c j) -> p d c j", j=RUN),
-                    in_=acc[:].rearrange("p d (j c) -> p d c j", j=RUN),
-                )
-                if tokens.start < VECTOR_ROUNDS_FROM:
-                    nc.scalar.copy(
-                        out=out_grouped[:, tokens, :].rearrange("p (c j) d -> p c j d", j=RUN),
-                        in_=acc[:].rearrange("p d (j c) -> p c j d", j=RUN),
-                    )
-                else:
-                    nc.vector.tensor_copy(
-                        out=out_grouped[:, tokens, :].rearrange("p (c j) d -> p c d j", j=RUN),
-                        in_=out_rows[:, :, tokens].rearrange("p d (c j) -> p c d j", j=RUN),
-                    )
-                nc.sync.dma_start(out=out_rows_hbm[:, :, tokens], in_=out_rows[:, :, tokens])
-            else:
-                nc.scalar.copy(
-                    out=out_grouped[:, tokens, :].rearrange("p (c j) d -> p c j d", j=RUN),
-                    in_=acc[:].rearrange("p d (j c) -> p c j d", j=RUN),
-                )
-                nc.scalar.copy(
-                    out=out_rows[:, :, tokens].rearrange("p d (c j) -> p d c j", j=RUN),
-                    in_=acc[:].rearrange("p d (j c) -> p d c j", j=RUN),
-                )
-                nc.sync.dma_start(out=out_rows_hbm[:, :, tokens], in_=out_rows[:, :, tokens])
+            acc = shared_layer(*da_quantised[tokens.start], bank)
+            if tokens.stop == T:
+                round_sums(acc, tokens)
+            copy_sums(acc, tokens)
+            if tokens.start == 0:
+                round_sums(acc, tokens)
+            elif tokens.stop < T:
+                round_rows(tokens)
+            nc.sync.dma_start(out=out_rows_hbm[:, :, tokens], in_=out_rows[:, :, tokens])
             if tokens.stop in PLANE_EDGES:
                 group = since_last(PLANE_EDGES, tokens.stop)
                 nc.vector.quantize_mx(

@@ -31,7 +31,7 @@ EXPERT_GROUPS = ((0, 1), (1, 2), (2, 4), (4, E))
 EXPERT_BANKS = 4
 SHARED_SLICE = 2
 SCALAR_SLICE = 3
-SHARED_SPLIT = 416
+SHARED_SPLIT = 384
 SCALAR_SCATTER = 384
 RUN = 4
 BLOCK = 128
@@ -185,10 +185,10 @@ def tile_moe_sub_silu_kernel(
 
         w1_words_raw = keep.tile([P, K], I32, name="w1_words_raw", tag=f"words{EARLY_SCALES}_1", align_bytes=64)
         nc.sync.dma_start(out=w1_words_raw[:], in_=w1t_words[0].rearrange("p k d -> p (k d)").bitcast(I32))
-        w1_plane_raw = keep.tile([P, 1, K], U8, name="w1_plane_raw", tag=f"words{EARLY_SCALES}_0", align_bytes=64)
+        w1_plane_raw = keep.tile([P, 1, K], U8, name="w1_plane_raw", align_bytes=64)
         nc.gpsimd.memset(w1_plane_raw[:].rearrange("p g k -> p (g k)").bitcast(I32), 0)
         load_scale_planes(w1_plane_raw, w1t_scales)
-        w1_plane = keep.tile([P, PACK, P], U8, name="w1_plane", align_bytes=64)
+        w1_plane = keep.tile([P, PACK, P], U8, name="w1_plane", tag=f"words{EARLY_SCALES}_0", align_bytes=64)
         nc.vector.tensor_copy(out=w1_plane[:], in_=w1_plane_raw[:, 0, :].rearrange("p (m d) -> p d m", d=PACK))
 
         silu_first = keep.tile([P, PACK, BLOCK], F32, name="silu_first", align_bytes=64)

@@ -280,6 +280,18 @@ def tile_moe_sub_silu_kernel(
                 )
             return acc
 
+        def keep_clock(da_codes, da_plane):
+            unread = psum.tile([P, BLOCK], F32, name="unread", tag=f"bank{T // BLOCK}")
+            nc.tensor.matmul_mx(
+                out=unread[:],
+                lhsT=w1_words[:, 0, :].bitcast(FP8X4),
+                lhsT_scale=w1_plane[:, 0, :],
+                rhs=da_codes[:].bitcast(FP8X4),
+                rhs_scale=da_plane[:],
+                start=True,
+                stop=True,
+            )
+
         out_rows_hbm = out_0.rearrange("(p d) t -> p d t", d=PACK)
         codes_hbm = out_1[0].rearrange("p t d -> p (t d)").bitcast(I32)
         out_rows = keep.tile([P, PACK, T], F32, name="out_rows")
@@ -308,6 +320,8 @@ def tile_moe_sub_silu_kernel(
 
         for bank, tokens in enumerate(blocks_in(0, T)):
             acc = shared_layer(*da_quantised[tokens.start], bank)
+            if tokens.stop < T:
+                keep_clock(*da_quantised[tokens.start])
             if tokens.stop == T:
                 round_sums(acc, tokens)
             copy_sums(acc, tokens)

@@ -70,9 +70,10 @@ def tile_moe_sub_silu_kernel(
         load_scale_planes(token_scales, dy_scales)
 
         w2_scale_rows = w2t_scales.rearrange("e s b i -> (e s) b i")
-        early_planes = keep.tile([P, EARLY_PLANES * PASSES, H], U8, name="early_planes", align_bytes=64)
+        first_planes = keep.tile([P, PASSES, H], U8, name="first_planes", align_bytes=64)
+        second_planes = keep.tile([P, PASSES, H], U8, name="second_planes", align_bytes=64)
         late_planes = keep.tile([P, (E - EARLY_PLANES) * PASSES, H], U8, name="late_planes", align_bytes=64)
-        w2_plane = [early_planes[:, g, :] for g in range(EARLY_PLANES * PASSES)]
+        w2_plane = [planes[:, s, :] for planes in (first_planes, second_planes) for s in range(PASSES)]
         w2_plane.extend(late_planes[:, g, :] for g in range((E - EARLY_PLANES) * PASSES))
         w2_words = {}
 
@@ -89,12 +90,13 @@ def tile_moe_sub_silu_kernel(
         a_first = keep.tile([P, PACK, BLOCK], F32, name="a_first", align_bytes=64)
         a_rest = keep.tile([P, PACK, T - BLOCK], F32, name="a_rest", align_bytes=64)
         a_hbm = a.rearrange("(p t) c -> p t c", t=PACK)
-        load_scale_planes(early_planes, w2_scale_rows[0 : EARLY_PLANES * PASSES], range(1))
+        load_scale_planes(first_planes, w2_scale_rows[0:PASSES], range(1))
         token_words = keep.tile([P, PASSES, T], I32, name="token_words", align_bytes=64)
         nc.sync.dma_start(out=token_words[:], in_=dy_words.rearrange("s p t d -> p s (t d)").bitcast(I32))
-        load_scale_planes(early_planes, w2_scale_rows[0 : EARLY_PLANES * PASSES], range(1, QUADRANT_ROWS))
+        load_scale_planes(first_planes, w2_scale_rows[0:PASSES], range(1, QUADRANT_ROWS))
         load_experts(*EXPERT_GROUPS[0])
         nc.sync.dma_start(out=a_first[:], in_=a_hbm[:, :, 0:BLOCK])
+        load_scale_planes(second_planes, w2_scale_rows[PASSES : EARLY_PLANES * PASSES])
         load_experts(*EXPERT_GROUPS[1])
         load_scale_planes(late_planes, w2_scale_rows[EARLY_PLANES * PASSES : E * PASSES])
         for first, last in EXPERT_GROUPS[2:]:

from contextlib import ExitStack

import concourse.mybir as mybir
from concourse.masks import make_identity

K, T, E, C, H, N = 512, 768, 6, 128, 512, 1024
FLOPS = 2 * N * H * E * C + 2 * H * K * T

F32 = mybir.dt.float32
BF16 = mybir.dt.bfloat16
I32 = mybir.dt.int32
U32 = mybir.dt.uint32
U16 = mybir.dt.uint16
U8 = mybir.dt.uint8
FP8X4 = mybir.dt.float8_e4m3fn_x4
FP4X4 = mybir.dt.float4_e2m1fn_x4
ACT = mybir.ActivationFunctionType
ALU = mybir.AluOpType

P = 128
PACK = 4
PASSES = N // (P * PACK)
QUADRANT = 32
SCALE_ROWS = 16
QUADRANT_ROWS = 4
LIST_ROWS = 16
F32_BYTES = 4
EARLY_PLANES = 2
EARLY_SCALES = 4
EXPERT_GROUPS = ((0, 1), (1, 2), (2, 4), (4, E))
EXPERT_BANKS = 4
SHARED_SLICE = 2
SCALAR_SLICE = 3
SHARED_SPLIT = 384
SCALAR_SCATTER = 384
RUN = 4
BLOCK = 128
PRODUCT_EDGES = [0, 128, 384, 640, 768]
PLANE_EDGES = [0, 256, 512, 640, 768]
CODE_STORE_EDGES = [0, 256, 640, 768]


def tile_moe_sub_silu_kernel(
    tc, dy_words, dy_scales, w2t_words, w2t_scales, w1t_words, w1t_scales, a, gate, offs, out_0, out_1, out_2
):
    nc = tc.nc
    with ExitStack() as ctx:
        keep = ctx.enter_context(tc.tile_pool(name="keep", bufs=1))
        shared = ctx.enter_context(tc.tile_pool(name="shared", bufs=1))
        psum = ctx.enter_context(tc.psum_pool(name="psum", bufs=1))

        def offsets_of(first, last):
            return offsets[:, first // LIST_ROWS : last // LIST_ROWS]

        def load_scale_planes(planes, rows, which=range(QUADRANT_ROWS)):
            for r in which:
                nc.sync.dma_start(
                    out=planes[r:P:QUADRANT, :, :].bitcast(I32),
                    in_=rows[:, r:SCALE_ROWS:QUADRANT_ROWS, :].rearrange("g q n -> q g n").bitcast(I32),
                )

        offsets = keep.tile([P, E * C // LIST_ROWS], U16, name="offsets")
        nc.sync.dma_start(offsets[:], offs)

        token_scales = keep.tile([P, PASSES, T], U8, name="token_scales", align_bytes=64)
        nc.gpsimd.memset(token_scales[:].rearrange("p s t -> p (s t)").bitcast(I32), 0)
        gate_columns = keep.tile([P, E], F32, name="gate_columns")
        with nc.allow_non_contiguous_dma(reason="one gate a partition"):
            nc.sync.dma_start(out=gate_columns[:], in_=gate[0, :].rearrange("(e u) -> u e", u=C))
        load_scale_planes(token_scales, dy_scales)

        w2_scale_rows = w2t_scales.rearrange("e s b i -> (e s) b i")
        first_planes = keep.tile([P, PASSES, H], U8, name="first_planes", align_bytes=64)
        second_planes = keep.tile([P, PASSES, H], U8, name="second_planes", align_bytes=64)
        late_planes = keep.tile([P, (E - EARLY_PLANES) * PASSES, H], U8, name="late_planes", align_bytes=64)
        w2_plane = [planes[:, s, :] for planes in (first_planes, second_planes) for s in range(PASSES)]
        w2_plane.extend(late_planes[:, g, :] for g in range((E - EARLY_PLANES) * PASSES))
        w2_words = {}

        def load_experts(first, last):
            count = (last - first) * PASSES
            words = keep.tile([P, count, 2 * H], U8, name=f"w2_words{first}", align_bytes=64)
            nc.sync.dma_start(
                out=words[:].bitcast(I32),
                in_=w2t_words[first:last].rearrange("e s p b -> p (e s) b").bitcast(I32),
            )
            for g in range(count):
                w2_words[first * PASSES + g] = words[:, g, :]

        a_first = keep.tile([P, PACK, BLOCK], F32, name="a_first", align_bytes=64)
        a_rest = keep.tile([P, PACK, T - BLOCK], F32, name="a_rest", align_bytes=64)
        a_hbm = a.rearrange("(p t) c -> p t c", t=PACK)
        load_scale_planes(first_planes, w2_scale_rows[0:PASSES], range(1))
        token_words = keep.tile([P, PASSES, T], I32, name="token_words", align_bytes=64)
        nc.sync.dma_start(out=token_words[:], in_=dy_words.rearrange("s p t d -> p s (t d)").bitcast(I32))
        load_scale_planes(first_planes, w2_scale_rows[0:PASSES], range(1, QUADRANT_ROWS))
        load_experts(*EXPERT_GROUPS[0])
        nc.sync.dma_start(out=a_first[:], in_=a_hbm[:, :, 0:BLOCK])
        load_scale_planes(second_planes, w2_scale_rows[PASSES : EARLY_PLANES * PASSES])
        load_experts(*EXPERT_GROUPS[1])
        load_scale_planes(late_planes, w2_scale_rows[EARLY_PLANES * PASSES : E * PASSES])
        for first, last in EXPERT_GROUPS[2:]:
            load_experts(first, last)
        nc.sync.dma_start(out=a_rest[:], in_=a_hbm[:, :, BLOCK:T])

        identity = keep.tile([P, P], F32, name="identity")
        make_identity(nc, identity[:])

        slot_plane = {}
        slot_words = {}

        def gather_scales(first, last, tag):
            for s in range(PASSES):
                gathered = keep.tile(
                    [P, (last - first) * C], U8, name=f"scales{first}_{s}", tag=f"{tag}_{s}", align_bytes=64
                )
                nc.vector.tensor_copy(
                    out=gathered[:], in_=token_scales[:, s, :].indirect(offsets_of(first * C, last * C))
                )
                for e in range(first, last):
                    slot_plane[e, s] = gathered[:, (e - first) * C : (e - first + 1) * C]

        def gather_words(first, last):
            for s in range(PASSES):
                name = f"words{first}_{s}"
                gathered = keep.tile([P, (last - first) * C], U32, name=name, tag=name, align_bytes=64)
                nc.vector.tensor_copy(
                    out=gathered[:], in_=token_words[:, s, :].bitcast(U32).indirect(offsets_of(first * C, last * C))
                )
                for e in range(first, last):
                    slot_words[e, s] = gathered[:, (e - first) * C : (e - first + 1) * C]

        gather_scales(0, EARLY_SCALES, "scales0")
        for first, last in EXPERT_GROUPS:
            gather_words(first, last)

        neg_half_dh = [keep.tile([P, T], F32, name=f"neg_half_dh{t}") for t in range(PACK)]
        y_rows = shared.tile([P, PACK, E * C], F32, name="y_rows", offset=0)
        y_dealt = {}

        def multiply(e):
            y_by_slot = psum.tile([P, H], F32, name="y_by_slot", tag=f"bank{e % EXPERT_BANKS}")
            for s in range(PASSES):
                nc.tensor.matmul_mx(
                    out=y_by_slot[:],
                    lhsT=slot_words[e, s].bitcast(FP8X4),
                    lhsT_scale=slot_plane[e, s],
                    rhs=w2_words[e * PASSES + s].bitcast(FP4X4),
                    rhs_scale=w2_plane[e * PASSES + s],
                    start=(s == 0),
                    stop=(s == PASSES - 1),
                )
            y_dealt[e] = keep.tile([P, PACK, P], F32, name=f"y_dealt{e}", tag=f"y_dealt{e}")
            nc.scalar.activation(
                out=y_dealt[e][:],
                in_=y_by_slot[:].rearrange("u (m t) -> u t m", t=PACK),
                func=ACT.Copy,
                scale=gate_columns[:, e : e + 1],
            )

        def turn(e):
            turned = psum.tile([P, PACK, C], F32, name="turned", tag=f"bank{EXPERT_BANKS + e % EXPERT_BANKS}")
            for t in range(PACK):
                nc.tensor.transpose(turned[:, t, :], y_dealt[e][:, t, :], identity[:])
            nc.scalar.activation(out=y_rows[:, :, e * C : (e + 1) * C], in_=turned[:], func=ACT.Copy, scale=-0.5)

        def vector_scatter(t, first, last):
            nc.vector.tensor_copy(out=neg_half_dh[t][:].indirect(offsets_of(first, last)), in_=y_rows[:, t, first:last])

        def scalar_scatter(t, first, last):
            nc.scalar.activation(
                out=neg_half_dh[t][:].indirect(offsets_of(first, last)), in_=y_rows[:, t, first:last], func=ACT.Copy
            )

        multiply(0)
        gather_scales(EARLY_SCALES, E, "words0")
        for e in range(E):
            if e + 1 < E:
                multiply(e + 1)
            turn(e)

        for first, last in EXPERT_GROUPS:
            if first * C < SHARED_SPLIT:
                vector_scatter(SHARED_SLICE, first * C, min(last * C, SHARED_SPLIT))
            for t in range(SHARED_SLICE):
                vector_scatter(t, first * C, last * C)

        w1_words_raw = keep.tile([P, K], I32, name="w1_words_raw", tag=f"words{EARLY_SCALES}_1", align_bytes=64)
        nc.sync.dma_start(out=w1_words_raw[:], in_=w1t_words[0].rearrange("p k d -> p (k d)").bitcast(I32))
        w1_plane_raw = keep.tile([P, 1, K], U8, name="w1_plane_raw", align_bytes=64)
        nc.gpsimd.memset(w1_plane_raw[:].rearrange("p g k -> p (g k)").bitcast(I32), 0)
        load_scale_planes(w1_plane_raw, w1t_scales)
        w1_plane = keep.tile([P, PACK, P], U8, name="w1_plane", tag=f"words{EARLY_SCALES}_0", align_bytes=64)
        nc.vector.tensor_copy(out=w1_plane[:], in_=w1_plane_raw[:, 0, :].rearrange("p (m d) -> p d m", d=PACK))

        silu_first = keep.tile([P, PACK, BLOCK], F32, name="silu_first", align_bytes=64)
        nc.scalar.activation(out=silu_first[:], in_=a_first[:], func=ACT.Silu, scale=-1.0)
        scalar_scatter(SCALAR_SLICE, 0, C)
        scalar_scatter(SCALAR_SLICE, E * C - SCALAR_SCATTER, E * C)
        silu_rest = keep.tile([P, PACK, T - BLOCK], F32, name="silu_rest", tag=f"y_dealt{E - 1}")
        for t in range(0, PACK, 2):
            nc.scalar.activation(out=silu_rest[:, t : t + 2, :], in_=a_rest[:, t : t + 2, :], func=ACT.Silu, scale=-1.0)

        tanh_of_half_a = {}

        def take_tanh(block, pool, **place):
            rows = a_first[:] if block == 0 else a_rest[:, :, (block - 1) * BLOCK : block * BLOCK]
            values = pool.tile([P, BLOCK // RUN, PACK, RUN], F32, name=f"tanh_of_half_a{block}", **place)
            nc.scalar.activation(
                out=values[:], in_=rows.rearrange("p t (c j) -> p c t j", j=RUN), func=ACT.Tanh, scale=0.5
            )
            tanh_of_half_a[block * BLOCK] = values

        take_tanh(0, keep)
        w1_words = keep.tile([P, PACK, P], I32, name="w1_words", align_bytes=64)
        nc.vector.tensor_copy(
            out=w1_words[:].rearrange("p d m -> p m d"), in_=w1_words_raw[:].rearrange("p (m d) -> p m d", d=PACK)
        )
        scalar_scatter(SHARED_SLICE, SHARED_SPLIT, E * C)
        scalar_scatter(SCALAR_SLICE, C, E * C - SCALAR_SCATTER)
        for block in range(1, T // BLOCK):
            take_tanh(block, shared, offset=block * BLOCK * PACK * F32_BYTES)

        out_codes = keep.tile([P, T], U32, name="out_codes", align_bytes=64)
        out_plane = keep.tile([P, T], U8, name="out_plane", align_bytes=64)
        half_da = keep.tile([P, T // RUN, PACK, RUN], F32, name="half_da", align_bytes=64)

        def first_products(tokens, slices):
            if tokens.start == 0:
                silu_of_neg_a = silu_first[:]
            else:
                silu_of_neg_a = silu_rest[:, :, tokens.start - BLOCK : tokens.stop - BLOCK]
            for t in slices:
                nc.vector.scalar_tensor_tensor(
                    out=half_da[:, tokens.start // RUN : tokens.stop // RUN, t, :],
                    in0=silu_of_neg_a[:, t, :].rearrange("p (c j) -> p c j", j=RUN),
                    scalar=1.0,
                    in1=neg_half_dh[t][:, tokens].rearrange("p (c j) -> p c j", j=RUN),
                    op0=ALU.subtract,
                    op1=ALU.mult,
                )

        def quantised_da(tokens):
            da_grouped = keep.tile([P, BLOCK, PACK], BF16, name=f"da_grouped{tokens.start}", align_bytes=64)
            nc.vector.scalar_tensor_tensor(
                out=da_grouped[:].rearrange("p (j c) t -> p (c t) j", j=RUN),
                in0=tanh_of_half_a[tokens.start][:].rearrange("p c t j -> p (c t) j"),
                scalar=1.0,
                in1=half_da[:, tokens.start // RUN : tokens.stop // RUN, :, :].rearrange("p c t j -> p (c t) j"),
                op0=ALU.add,
                op1=ALU.mult,
            )
            da_codes = keep.tile([P, BLOCK], U32, name=f"da_codes{tokens.start}", align_bytes=64)
            da_plane = keep.tile([P, BLOCK], U8, name=f"da_plane{tokens.start}", align_bytes=64)
            nc.vector.quantize_mx(
                out=da_codes[:].bitcast(FP8X4), scales=da_plane[:], in_=da_grouped[:].rearrange("p c t -> p (c t)")
            )
            return da_codes, da_plane

        def blocks_in(lo, hi):
            return [slice(start, start + BLOCK) for start in range(lo, hi, BLOCK)]

        da_quantised = {}
        first_products(slice(0, BLOCK), range(SCALAR_SLICE))
        first_products(slice(BLOCK, T), range(SCALAR_SLICE))
        for lo, hi in zip(PRODUCT_EDGES, PRODUCT_EDGES[1:]):
            first_products(slice(lo, hi), [SCALAR_SLICE])
            for tokens in blocks_in(lo, hi):
                da_quantised[tokens.start] = quantised_da(tokens)

        def shared_layer(da_codes, da_plane, bank):
            acc = psum.tile([P, PACK, BLOCK], F32, name="acc", tag=f"bank{bank}")
            for d in range(PACK):
                nc.tensor.matmul_mx(
                    out=acc[:, d, :],
                    lhsT=w1_words[:, d, :].bitcast(FP8X4),
                    lhsT_scale=w1_plane[:, d, :],
                    rhs=da_codes[:].bitcast(FP8X4),
                    rhs_scale=da_plane[:],
                    start=True,
                    stop=True,
                )
            return acc

        def keep_clock(da_codes, da_plane):
            unread = psum.tile([P, BLOCK], F32, name="unread", tag=f"bank{T // BLOCK}")
            nc.tensor.matmul_mx(
                out=unread[:],
                lhsT=w1_words[:, 0, :].bitcast(FP8X4),
                lhsT_scale=w1_plane[:, 0, :],
                rhs=da_codes[:].bitcast(FP8X4),
                rhs_scale=da_plane[:],
                start=True,
                stop=True,
            )

        out_rows_hbm = out_0.rearrange("(p d) t -> p d t", d=PACK)
        codes_hbm = out_1[0].rearrange("p t d -> p (t d)").bitcast(I32)
        out_rows = keep.tile([P, PACK, T], F32, name="out_rows")
        out_grouped = keep.tile([P, T, PACK], BF16, name="out_grouped", align_bytes=64)

        def copy_sums(acc, tokens):
            nc.scalar.copy(
                out=out_rows[:, :, tokens].rearrange("p d (c j) -> p d c j", j=RUN),
                in_=acc[:].rearrange("p d (j c) -> p d c j", j=RUN),
            )

        def round_sums(acc, tokens):
            nc.scalar.copy(
                out=out_grouped[:, tokens, :].rearrange("p (c j) d -> p c j d", j=RUN),
                in_=acc[:].rearrange("p d (j c) -> p c j d", j=RUN),
            )

        def round_rows(tokens):
            nc.vector.tensor_copy(
                out=out_grouped[:, tokens, :].rearrange("p (c j) d -> p c d j", j=RUN),
                in_=out_rows[:, :, tokens].rearrange("p d (c j) -> p c d j", j=RUN),
            )

        def since_last(edges, stop):
            return slice(edges[edges.index(stop) - 1], stop)

        for bank, tokens in enumerate(blocks_in(0, T)):
            acc = shared_layer(*da_quantised[tokens.start], bank)
            if tokens.stop < T:
                keep_clock(*da_quantised[tokens.start])
            if tokens.stop == T:
                round_sums(acc, tokens)
            copy_sums(acc, tokens)
            if tokens.start == 0:
                round_sums(acc, tokens)
            elif tokens.stop < T:
                round_rows(tokens)
            nc.sync.dma_start(out=out_rows_hbm[:, :, tokens], in_=out_rows[:, :, tokens])
            if tokens.stop in PLANE_EDGES:
                group = since_last(PLANE_EDGES, tokens.stop)
                nc.vector.quantize_mx(
                    out=out_codes[:, group].bitcast(FP8X4),
                    scales=out_plane[:, group],
                    in_=out_grouped[:, group, :].rearrange("p c d -> p (c d)"),
                )
            if tokens.stop in CODE_STORE_EDGES:
                group = since_last(CODE_STORE_EDGES, tokens.stop)
                nc.sync.dma_start(out=codes_hbm[:, group], in_=out_codes[:, group].bitcast(I32))

        for q in range(P // QUADRANT):
            (nc.sync if q % 2 == 0 else nc.scalar).dma_start(
                out=out_2[0, QUADRANT_ROWS * q : QUADRANT_ROWS * (q + 1), :].bitcast(I32),
                in_=out_plane[QUADRANT * q : QUADRANT * q + QUADRANT_ROWS, :].bitcast(I32),
            )
